import numpy as np, ml_dtypes
CORES = [16,18,20,22]
N = 4
BF = ml_dtypes.bfloat16
W, L, OR, ST, NEED = 4096, 256, 8, 3, 9
def forest(rng):
    o = np.argsort(rng.random((N, 8, 16, L, OR)), axis=2); k = np.arange(16).reshape(1, 1, 16, 1, 1)
    q = (rng.random(o.shape) * k).astype(np.int64); p = np.zeros_like(o)
    np.put_along_axis(p, o, np.take_along_axis(o, q, 2), 2)
    return np.where(rng.random(p.shape) < 0.1, k, p)
def limits(rng, lo, n):
    base = np.argsort(rng.random((N, 8, 1, L)), axis=-1) % n + lo
    return np.clip(base + rng.integers(-2, 3, (N, 8, 16, L)), 0, 15)
def parts(rng):
    x = rng.integers(0, 16, (N, 8, 16, W)); c = rng.integers(0, W, (N, 8, 16, L, OR)); p = forest(rng); a = limits(rng, 3, 8)
    v = rng.integers(0, 33, (N, 8, OR, L))
    o = np.arange(OR).reshape(1, 1, OR, 1); fav = rng.integers(0, OR, (1, 8, 1, L)); stick = rng.random((1, 8, 1, L)) < 0.5
    v = np.where(stick, np.where(o == fav, rng.integers(20, 33, v.shape), rng.integers(0, 7, v.shape)), v)
    return x, c, p, a, v
def bf(a): return np.ascontiguousarray(a).astype(np.float32).astype(BF)
def pack(x, c, p, a, v):
    return {"xt": bf(x.reshape(N, 128, W)), "pg": np.ascontiguousarray(c.reshape(N, 128, L * OR)).astype(np.int32), "pre": bf(p.reshape(N, 128, L * OR)),
            "lim": bf(a.reshape(N, 128, L)), "vv": np.ascontiguousarray(v.reshape(N, 8 * OR, L)).astype(np.int32)}
def setup_inputs(rng):
    return pack(*parts(rng))
def setup_inputs_ties(rng):
    x, c, p, a, v = parts(rng)
    dl = rng.integers(1, 8, (1, 8, 1, 1)); x = rng.integers(0, 9, (N, 8, 16, 1)) + dl * rng.integers(0, 2, x.shape)
    k = np.argsort(rng.random((N, 8, 1, L)), axis=-1) % 5; n = np.array([0, 2 * NEED - 16, 2 * NEED - 15, NEED - 1, 16])[k]
    a = np.where(np.argsort(rng.random(a.shape), axis=2) < n, dl, dl - 1)
    t = rng.choice(np.array([0, 1, 16, 31, 32]), (N, 8, 1, L))
    v = np.where(np.argsort(rng.random(v.shape), axis=2) < 2, t, np.minimum(rng.integers(0, 33, v.shape), t))
    return pack(x, c, p, a, v)
def setup_inputs_ends(rng):
    x, c, p, a, v = parts(rng)
    x = 15 * rng.integers(0, 2, x.shape); x[..., 0] = 0; x[..., W - 1] = 15
    e = rng.choice(np.array([0, 1, W // 2, W - 2, W - 1]), c.shape); c = np.where(rng.random((N, 8, 1, L, 1)) < 0.5, e, c)
    T = np.arange(16).reshape(1, 1, 16, 1, 1); k = rng.integers(0, 6, (N, 8, 1, L, 1))
    q = np.where(k == 0, T, np.where(k == 1, np.maximum(T - 1, 0), np.where(k == 2, 0, np.where(k == 3, 15, (T + 1) % 16))))
    p = np.where(k == 5, rng.integers(0, 16, p.shape), q)
    k = np.argsort(rng.random((N, 8, 1, L)), axis=-1) % 5; pos = np.argsort(rng.random(a.shape), axis=2)
    a = np.where(k == 0, 0, np.where(k == 1, 15, np.where(k == 2, 14, np.where(pos < np.where(k == 3, NEED, NEED - 1), 15, 0))))
    o = np.arange(OR).reshape(1, 1, OR, 1); k = rng.integers(0, 5, (N, 8, 1, L))
    v = np.where(k == 0, 0, np.where(k == 1, 32, np.where(k == 2, 32 * (o == 0), np.where(k == 3, 32 * (o == OR - 1), v))))
    z = int(rng.integers(0, 8)); w = np.argsort(rng.random(L)) % 4; x[:, z] = 15 * (np.arange(W) & 1)
    tt = T[0]; ring = (w == 0).reshape(1, 1, L, 1); climb = (w == 1).reshape(1, 1, L, 1)
    par = rng.integers(0, 2, (N, 1, L, OR)); even = c[:, z] - (c[:, z] & 1)
    c[:, z] = np.where(ring, even + ((par + tt) & 1), np.where(climb, even + ((par + (tt == 15)) & 1), c[:, z]))
    p[:, z] = np.where(ring, (tt + 1) % 16, np.where(climb, 0, p[:, z]))
    a = np.where(w == 1, 15, a); a[:, z] = np.where(w <= 1, 14 * rng.integers(0, 2, (N, 16, L)), a[:, z])
    v[:, z] = np.where(w == 1, 32 * (o[0] < 5) - 1 * (o[0] == 3), v[:, z])
    return pack(x, c, p, a, v)
def setup_inputs_alike(rng):
    x, c, p, a, v = parts(rng)
    x[:, ::2] = x[:, ::2][..., rng.integers(0, 8, W)]
    few = rng.integers(0, W, 5); few[0] = 0; few[1] = W - 1; c = few[rng.integers(0, 5, c.shape)]
    m = (rng.random((N, 8, 1, L, 1)) < 0.3) | (rng.random((N, 1, 1, L, 1)) < 0.3)
    c = np.where(m, c[:, :, :1], c); a[:, rng.integers(0, 8)] = 0
    return pack(x, c, p, a, v)
def setup_inputs_same(rng):
    x, c, p, a, v = parts(rng)
    o = np.arange(OR).reshape(1, 1, OR, 1); fav = rng.integers(0, OR, (1, 8, 1, L))
    v = np.where(o == fav, 32, rng.integers(0, 3, v.shape)); a = limits(rng, 5, 6)
    a[:, rng.integers(0, 8)] = rng.integers(0, 5, (N, 16, L))
    return pack(x, c, p, a, v)
def setup_inputs_spread(rng):
    x, c, p, a, v = parts(rng); E = np.array([0.25, 0.5, 1.0, 2.0, 4.0])
    def un(n, shape, by): return np.minimum((n * rng.random(shape) ** rng.choice(E, by)).astype(np.int64), n - 1)
    x = un(16, x.shape, (N, 8, 16, 1)); c = un(W, c.shape, (N, 8, 1, L, OR)); a = un(16, a.shape, (N, 8, 1, L)); v = un(33, v.shape, (N, 8, OR, 1))
    return pack(x, c, p, a, v)
def check_inputs(d):
    bad = []
    for k, hi in (("xt", 15), ("pg", W - 1), ("pre", 15), ("lim", 15), ("vv", 32)):
        b = np.asarray(d[k]).astype(np.float64)
        if not (np.min(b) >= 0 and np.max(b) <= hi and np.all(b == np.floor(b))): bad.append("range of " + k)
    return bad
def reference(xt, pg, pre, lim, vv):
    xs = np.ascontiguousarray(xt.astype(np.int32).reshape(N, 8, 16, W).transpose(0, 1, 3, 2))
    cur = np.ascontiguousarray(pg.astype(np.int64).reshape(N, 8, 16, L, OR).transpose(0, 1, 3, 4, 2))
    prd = np.ascontiguousarray(pre.astype(np.int64).reshape(N, 8, 16, L, OR).transpose(0, 1, 3, 4, 2))
    a = np.ascontiguousarray(lim.astype(np.int32).reshape(N, 8, 16, L).transpose(0, 1, 3, 2))
    v = np.ascontiguousarray(vv.astype(np.int64).reshape(N, 8, OR, L).transpose(0, 1, 3, 2))
    m = np.zeros((N, 8, L), np.int64)
    g0 = np.arange(8).reshape(1, 8, 1); l0 = np.arange(L).reshape(1, 1, L)
    for s in range(N):
        h = ((np.arange(N) + s) % N).reshape(N, 1, 1)
        o = np.argmax(v, axis=3)
        c = cur[h, g0, l0, o]; p = prd[h, g0, l0, o]
        got = np.zeros((N, 8, L), np.int64)
        for t in range(ST):
            F = xs[h[..., None], g0[..., None], c]
            G = np.take_along_axis(F, p[..., None], 3)
            D = np.abs(F - G)
            ok = np.add.reduce((D <= a[:, :, :, None, :]).astype(np.int64), axis=4) >= NEED
            full = np.all(ok, axis=3)
            got = got + full
            c = np.where(full[..., None], (5 * c + 1) & (W - 1), np.where(ok, c, (5 * c + np.add.reduce(D, axis=4) + 1) & (W - 1)))
        cur[h, g0, l0, o] = c
        m = m + got
        odd = np.add.reduce(got, axis=1, keepdims=True) & 1
        v = v + 1 + odd[..., None]
        np.put_along_axis(v, o[..., None], np.add.reduce(ok.astype(np.int64), axis=3)[..., None], 3)
    return {"yg": np.ascontiguousarray(cur.transpose(0, 1, 4, 2, 3)).reshape(N, 128, L * OR).astype(np.float32),
            "yv": np.ascontiguousarray(v.transpose(0, 1, 3, 2)).reshape(N, 8 * OR, L).astype(np.float32), "ym": m.astype(np.float32)}

@@ -1,0 +1,468 @@
+from concourse.mybir import AluOpType, ActivationFunctionType
+
+ACT = ActivationFunctionType
+NS, ST = 4, 3
+H, J = 2, 2
+LH, LB = 128, 64
+NK = LH // 16
+KW = 8 * NK
+KG = KW + NK
+FW = ST * NK
+BIG = 65536
+OFF = 491520
+
+SCRATCH = {
+    "X": ("sbuf", [128, 4096], "bfloat16"),
+    "vvi": ("sbuf", [64, 256], "int32"), "vvb": ("sbuf", [64, 256], "bfloat16"), "R": ("sbuf", [64, 2048], "bfloat16"),
+    "limb": ("sbuf", [128, 256], "bfloat16"),
+    "ones": ("sbuf", [128, 2048], "bfloat16"), "E": ("sbuf", [128, 2048], "bfloat16"),
+    "gA": ("sbuf", [128, 128], "bfloat16"), "gm": ("sbuf", [128, 128], "bfloat16"), "okw": ("sbuf", [128, 128], "bfloat16"),
+    "g8A": ("sbuf", [64, 128], "bfloat16"), "g8m": ("sbuf", [64, 128], "bfloat16"), "g8s": ("sbuf", [64, 128], "bfloat16"),
+    "vsel": ("sbuf", [64, 2048], "bfloat16"),
+    "identb": ("sbuf", [128, 128], "bfloat16"), "negi": ("sbuf", [128, 128], "bfloat16"), "identf": ("sbuf", [128, 128], "float32"),
+    "fsel1": ("sbuf", [128, 128], "bfloat16"), "fsel": ("sbuf", [128, 128], "bfloat16"),
+    "sel1": ("sbuf", [128, 2048], "bfloat16"), "sel2": ("sbuf", [128, 2048], "bfloat16"),
+    "pm": ("sbuf", [128, 128], "int32"), "pm2": ("sbuf", [128, 128], "int32"), "sameb": ("sbuf", [128, 128], "bfloat16"),
+    "om": ("sbuf", [64, 8], "int32"), "om2": ("sbuf", [64, 8], "int32"), "omask": ("sbuf", [64, 8], "float32"),
+    "pc4": ("sbuf", [128, 4], "int32"), "pc15": ("sbuf", [128, 4], "int32"), "pc8": ("sbuf", [128, 4], "float32"),
+    "pc7": ("sbuf", [128, 4], "int32"), "rep": ("sbuf", [128, 4], "uint16"),
+    "kc": ("sbuf", [128, KW], "int32"), "keyc": ("sbuf", [128, KW], "int32"),
+    "limT": ("sbuf", [128, NS * 256], "bfloat16"),
+    "keys": ("sbuf", [128, (NS + 1) * H * KG], "int32"),
+    "pay": ("sbuf", [128, NS * H * KG], "int32"),
+    "fx": ("sbuf", [128, NS * H * FW], "bfloat16"),
+    "fl": ("sbuf", [128, NS * H * FW], "bfloat16"),
+    "PA0": ("psum", [128, 1024], "float32"), "PA1": ("psum", [128, 1024], "float32"),
+    "PP0": ("psum", [128, 512], "float32"), "PP1": ("psum", [128, 512], "float32"),
+    "PN0": ("psum", [128, 512], "float32"), "PN1": ("psum", [128, 512], "float32"),
+}
+for _h in range(H):
+    for _n, _w, _d in (("pgi", 1024, "int32"), ("pgw", 1024, "float32"), ("prew", 1024, "float32"), ("mA", KW // 2, "int32"), ("mB", KW // 4, "int32"),
+                       ("km", NK, "int32"), ("li", NK, "int32"), ("lst", NK, "uint16"), ("ea", NK, "int32"), ("eb", NK, "int32"),
+                       ("eq", KW, "float32"), ("cfl", LH, "float32"), ("c16", LH, "uint16"), ("p16", LH, "uint16"), ("u5", LH, "float32"),
+                       ("ci", LH, "int32"), ("cpp", LH, "int32"), ("qq", LH, "float32"), ("sg", ST * LH, "bfloat16"), ("nk1", NK, "float32"),
+                       ("mi", NK, "int32"), ("od", NK, "int32"), ("xx", NK, "float32"), ("dl", NK, "float32"), ("em", KW, "float32"),
+                       ("hi", KW, "int32"), ("fv", KW, "bfloat16"), ("yb", NK, "bfloat16")):
+        SCRATCH["%s%d" % (_n, _h)] = ("sbuf", [128, _w], _d)
+    SCRATCH["yvs%d" % _h] = ("sbuf", [8, 1024], "float32")
+    SCRATCH["yms%d" % _h] = ("sbuf", [8, LH], "float32")
+    for _j in range(J):
+        for _n in ("F", "F2", "D", "AD", "ni"):
+            SCRATCH["%s%d%d" % (_n, _h, _j)] = ("sbuf", [128, 16 * LB], "bfloat16")
+
+SEMAPHORES = ["cV", "cS", "cP", "cG", "lvv", "llim", "lxt", "lpg0", "lpg1", "lpre0", "lpre1", "outs", "sent"]
+SEMAPHORES += ["alim%d" % s for s in range(1, NS)] + ["akey%d%d" % (s, h) for s in range(1, NS + 1) for h in range(H)]
+SEMAPHORES += ["afl%d" % x for x in range(H, H * NS)]
+
+CYC, PEC = 0.83, 0.42
+GAT = 1.5
+VFIX, SFIX, PFIX = 60, 80, 0
+
+
+def WAY(s, st, h, j):
+    return "PS"[j]
+
+
+def graph(ctx):
+    T, A = ctx["T"], AluOpType
+    NE = ctx["X"]
+    ops = []
+
+    def add(eng, cost, rd, wr, fn, pr=0.0, pool=None, free=None, sem=None, inc=None, lat=0.0, bk=(0,)):
+        ops.append(dict(eng=eng, cost=cost, rd=rd, wr=wr, fn=fn, pr=pr, pool=pool, free=free, sem=sem, inc=inc, lat=lat, bk=bk))
+
+    def V(n, cyc, rd, wr, fn, **k):
+        add("V", VFIX + max(64, n * cyc) * CYC, rd, wr, fn, **k)
+
+    def S(n, cyc, rd, wr, fn, **k):
+        add("S", SFIX + max(64, n * cyc) * CYC, rd, wr, fn, **k)
+
+    def P(k, n, rd, wr, fn, **kw):
+        add("P", k * (PFIX + max(64, n) * PEC), rd, wr, fn, **kw)
+
+    def G(n, rd, wr, fn, **k):
+        add("G", 150 + 2 * n * CYC, rd, wr, fn, **k)
+
+    def load(eng, out, inp, tile, sem, lat, pr):
+        add(eng, 80, [], [tile], lambda e, p: e.dma_start(out, inp), pr=pr, sem=sem, inc=16, lat=lat)
+
+    def kv(s, h, a, b):
+        return T.keys[:, (H * s + h) * KG + a:(H * s + h) * KG + b]
+
+    load("Q", T.vvi[:], T.vv[:], "vvi", "lvv", 2200, -9.0)
+    load("Q", T.pgi0[:], T.pg[:, 0:1024], "pgi0", "lpg0", 4000, -8.9)
+    load("S", T.X[:], T.xt[:], "X", "lxt", 7500, -9.0)
+    load("Q", T.limb[:], T.lim[:], "limb", "llim", 3000, -8.8)
+    load("Q", T.pgi1[:], T.pg[:, 1024:2048], "pgi1", "lpg1", 9500, -8.7)
+
+    def pre_fill(h):
+        G(1024, [], ["prew%d" % h], lambda e, p: e.iota(T["prew%d" % h][:], [[0, 2], [16, 64], [0, 8]], 0, 0, allow_small_or_imprecise_dtypes=True), pr=-9.0 + 3 * h)
+        add("G", 1100, ["prew%d" % h], ["prew%d" % h], lambda e, p: e.dma_start(T["prew%d" % h][:], T.pre[:, 1024 * h:1024 * h + 1024], accum_op=A.add),
+            pr=-8.9 + 3 * h, sem="lpre%d" % h, inc=16, lat=4000)
+
+    V(128, 0.5, [], ["ones"], lambda e, p: e.memset(T.ones[:, 0:128], 1.0), pr=-9.5)
+    V(1920, 0.5, [], ["onesE"], lambda e, p: e.memset(T.ones[:, 128:2048], 1.0), pr=-8.0)
+    G(8, [], ["om"], lambda e, p: e.iota(T.om[:], [[-1, 8]], 8, 1), pr=-9.9)
+    G(4, [], ["pc4"], lambda e, p: e.iota(T.pc4[:], [[0, 4]], 0, 1), pr=-9.8)
+    G(KW, [], ["kc"], lambda e, p: e.iota(T.kc[:], [[1, 8], [128, NK]], 0, 0), pr=-9.7)
+    V(8, 1, ["om"], ["om2"], lambda e, p: e.tensor_scalar(T.om2[:], T.om[:], 7, None, A.bitwise_and), pr=-9.0)
+    V(8, 1, ["om2"], ["omask"], lambda e, p: e.tensor_scalar(T.omask[:], T.om2[:], 0.0, None, A.is_equal), pr=-9.0)
+    V(4, 1, ["pc4"], ["pc15"], lambda e, p: e.tensor_scalar(T.pc15[:], T.pc4[:], 15, None, A.bitwise_and), pr=-9.0)
+    V(4, 1, ["pc15"], ["pc8"], lambda e, p: e.tensor_scalar(T.pc8[:], T.pc15[:], 8.0, None, A.mult), pr=-9.0)
+    V(4, 1, ["pc4"], ["pc7"], lambda e, p: e.tensor_scalar(T.pc7[:], T.pc4[:], 7, None, A.bitwise_and), pr=-7.0)
+    V(4, 1, ["pc7"], ["rep"], lambda e, p: e.tensor_copy(T.rep[:], T.pc7[:]), pr=-7.0)
+    V(KW, 1, ["kc", "pc8"], ["keyc"], lambda e, p: e.tensor_scalar(T.keyc[:], T.kc[:], T.pc8[:, 0:1], None, A.add), pr=-9.0)
+    G(128, ["ones"], ["g8A"], lambda e, p: e.affine_select(T.g8A[:], T.ones[0:64, 0:128], [[-8, 8], [0, 16]], A.is_ge, 0.0, 0, 1), pr=-9.6)
+    G(128, ["g8A"], ["g8m"], lambda e, p: e.affine_select(T.g8m[:], T.g8A[:], [[8, 8], [0, 16]], A.is_ge, 0.0, 7, -1), pr=-9.5)
+    S(128, 1, ["g8m"], ["g8s"], lambda e, p: e.activation(T.g8s[:], T.g8m[:], ACT.Copy, scale=-1024.0), pr=-9.0)
+    V(2048, 0.5, [], ["vsel"], lambda e, p: e.memset(T.vsel[:], 0.0), pr=-9.2)
+    for k in range(8):
+        V(16, 1, ["g8s"], ["vsel"], lambda e, p, k=k: e.tensor_copy(T.vsel[:, 16 * k:2048:129], T.g8s[:, 16 * k:16 * k + 16]), pr=-9.0)
+    pre_fill(0)
+    V(256, 1, ["vvi"], ["vvb"], lambda e, p: e.tensor_copy(T.vvb[:], T.vvi[:]), pr=-9.0)
+    for h in range(H):
+        for o in range(8):
+            V(128, 0.5, ["vvb", "omask"], ["R%d" % h],
+              lambda e, p, h=h, o=o: e.tensor_scalar(T.R[:, 1024 * h + 128 * o:1024 * h + 128 * o + 128], T.vvb[:, 128 * h:128 * h + 128], T.omask[:, o:o + 1], None, A.mult),
+              pr=-9.0 + 2 * h)
+
+        def vmm(e, p, h=h):
+            for b in range(16):
+                i = e.matmul(p[:, 0:KW], T.vsel[:, 128 * b:128 * b + 128], T.R[:, 1024 * h + b:1024 * h + 1024:16], b == 0, b == 15)
+            return i
+        P(16, KW, ["vsel", "R%d" % h], ["vP%d" % h], vmm, pr=-9.0 + 2 * h, pool=("N", "vP%d" % h))
+        V(KW, 1, ["vP%d" % h, "keyc"], ["key0%d" % h], lambda e, p, h=h: e.tensor_tensor(kv(0, h, 0, KW), p[:, 0:KW], T.keyc[:], A.add),
+          pr=-9.0 + 2 * h, pool=("N", "vP%d" % h), free=1)
+        V(NK, 1, [], ["gro0%d" % h], lambda e, p, h=h: e.memset(kv(0, h, KW, KG), 0), pr=-8.0 + 2 * h)
+        V(1024, 1, ["pgi%d" % h], ["pgw%d" % h], lambda e, p, h=h: e.tensor_copy(T["pgw%d" % h][:], T["pgi%d" % h][:]), pr=-8.0 + 3 * h)
+    G(128, ["ones"], ["identb"], lambda e, p: e.affine_select(T.identb[:], T.ones[:, 0:128], [[-1, 128]], A.is_equal, 0.0, 0, 1), pr=-8.5)
+    S(128, 1, ["identb"], ["negi"], lambda e, p: e.activation(T.negi[:], T.identb[:], ACT.Copy, scale=-1.0), pr=-7.0)
+    S(128, 1, ["identb"], ["identf"], lambda e, p: e.activation(T.identf[:], T.identb[:], ACT.Copy), pr=-7.0)
+    G(128, ["ones"], ["gA"], lambda e, p: e.affine_select(T.gA[:], T.ones[:, 0:128], [[-16, 8], [0, 16]], A.is_ge, 0.0, 0, 1), pr=-8.4)
+    G(128, ["gA"], ["gm"], lambda e, p: e.affine_select(T.gm[:], T.gA[:], [[16, 8], [0, 16]], A.is_ge, 0.0, 15, -1), pr=-8.3)
+    S(128, 1, ["gm"], ["okw"], lambda e, p: e.activation(T.okw[:], T.gm[:], ACT.Copy, scale=float(OFF // 16)), pr=-7.0)
+    V(2048, 0.5, [], ["sel1"], lambda e, p: e.memset(T.sel1[:], 0.0), pr=-8.0)
+    for k in range(8):
+        V(16, 1, ["gm"], ["sel1"], lambda e, p, k=k: e.tensor_copy(T.sel1[:, 16 * k:2048:129], T.gm[:, 16 * k:16 * k + 16]), pr=-7.5)
+    S(2048, 1, ["sel1"], ["sel2"], lambda e, p: e.activation(T.sel2[:], T.sel1[:], ACT.Copy, scale=float(BIG)), pr=-7.5)
+
+    def lmm(e, p):
+        e.matmul(p[:, 0:128], T.limb[:, 0:128], T.identb[:], True, True)
+        return e.matmul(p[:, 128:256], T.limb[:, 128:256], T.identb[:], True, True)
+    P(2, 128, ["limb", "identb"], ["lP"], lmm, pr=-7.5, pool=("N", "lP"))
+    S(256, 1, ["lP"], ["limT0"], lambda e, p: e.activation(T.limT[:, 0:256], p[:, 0:256], ACT.Copy), pr=-7.4, pool=("N", "lP"), free=1)
+    G(2048, ["ones", "onesE"], ["E"], lambda e, p: e.affine_select(T.E[:], T.ones[:], [[-1, 128], [0, 16]], A.is_equal, 0.0, 0, 1), pr=-7.5)
+    pre_fill(1)
+    G(128, [], ["pm"], lambda e, p: e.iota(T.pm[:], [[-1, 128]], 2048, 1), pr=-5.5)
+    V(128, 1, ["pm"], ["pm2"], lambda e, p: e.tensor_scalar(T.pm2[:], T.pm[:], 15, None, A.bitwise_and), pr=0.5)
+    V(128, 1, ["pm2"], ["sameb"], lambda e, p: e.tensor_scalar(T.sameb[:], T.pm2[:], 0.0, 1024.0, A.is_equal, A.mult), pr=0.5)
+    for s in range(1, NS):
+        add("G", 500, ["limT0"], [], lambda e, p, s=s: ctx["send"](s, T.limT[:, 256 * s:256 * s + 256], T.limT[:, 0:256], "alim%d" % s), pr=-5.0, sem="sent", inc=NE, lat=2500)
+        add("W", 0, [], ["limT%d" % s], None, sem="alim%d" % s, inc=NE, lat=15000)
+    G(128, ["ones"], ["fsel1"], lambda e, p: e.affine_select(T.fsel1[:], T.ones[:, 0:128], [[-1, 16], [-16, 8]], A.is_equal, 0.0, 0, 1), pr=-4.0)
+    S(128, 1, ["fsel1"], ["fsel"], lambda e, p: e.activation(T.fsel[:], T.fsel1[:], ACT.Copy, scale=1.0 / 1024.0), pr=1.5)
+
+    def begin(s, h):
+        pr = ST * s - 0.6 + 0.5 * h
+        kt, gt = "key%d%d" % (s, h), ("gro0%d" % h if s == 0 else "key%d%d" % (s, h))
+        n = lambda x: "%s%d" % (x, h)
+        t = lambda x: T["%s%d" % (x, h)]
+        V(KW // 2, 2, [kt], [n("mA")], lambda e, p: e.tensor_tensor(t("mA")[:], kv(s, h, 0, KW // 2), kv(s, h, KW // 2, KW), A.min), pr=pr)
+        V(KW // 4, 2, [n("mA")], [n("mB")], lambda e, p: e.tensor_tensor(t("mB")[:], t("mA")[:, 0:KW // 4], t("mA")[:, KW // 4:KW // 2], A.min), pr=pr)
+        V(NK, 2, [n("mB")], [n("km")], lambda e, p: e.tensor_tensor(t("km")[:], t("mB")[:, 0:NK], t("mB")[:, NK:2 * NK], A.min), pr=pr)
+        V(NK, 1, [n("km")], [n("li")], lambda e, p: e.tensor_scalar(t("li")[:], t("km")[:], 1023, None, A.bitwise_and), pr=pr)
+        V(NK, 1, [n("li")], [n("lst")], lambda e, p: e.tensor_copy(t("lst")[:], t("li")[:]), pr=pr)
+        V(LH, GAT, [n("pgw"), n("lst")], ["c16%d%d" % (h, j) for j in range(J)], lambda e, p: e.tensor_copy(t("c16")[:], t("pgw")[:].indirect(t("lst")[:])), pr=pr)
+        S(LH, GAT, [n("pgw"), n("lst")], [n("cfl")], lambda e, p: e.activation(t("cfl")[:], t("pgw")[:].indirect(t("lst")[:]), ACT.Copy), pr=pr + .02)
+        V(LH, GAT, [n("prew"), n("lst")], [n("p16")], lambda e, p: e.tensor_copy(t("p16")[:], t("prew")[:].indirect(t("lst")[:])), pr=pr + .01)
+        S(LH, 1, [n("cfl")], ["u5%d%d" % (h, j) for j in range(J)], lambda e, p: e.activation(t("u5")[:], t("cfl")[:], ACT.Identity, scale=5.0, bias=float(1 - OFF)), pr=pr + .3)
+        V(NK, 2, [gt, n("km")], [n("ea")], lambda e, p: e.tensor_tensor(t("ea")[:], kv(s, h, KW, KG), t("km")[:], A.subtract), pr=pr + .9)
+        V(NK, 2, [n("ea"), n("li")], [n("eb")], lambda e, p: e.tensor_tensor(t("eb")[:], t("ea")[:], t("li")[:], A.add), pr=pr + .9)
+        V(KW, GAT, [n("km"), kt, "rep"], [n("eq")], lambda e, p: e.tensor_tensor(t("eq")[:], t("km")[:].indirect(T.rep[:]), kv(s, h, 0, KW), A.is_equal), pr=pr + .9)
+
+    def step(s, st, h, j):
+        pr = ST * s + st + 0.5 * h + 0.25 * j
+        x = "%d%d" % (h, j)
+        a, b = LB * j, LB * j + LB
+        F, F2, D, AD, ni = T["F" + x], T["F2" + x], T["D" + x], T["AD" + x], T["ni" + x]
+        t = lambda n: T["%s%d" % (n, h)][:, a:b]
+        sg = T["sg%d" % h][:, LH * st + a:LH * st + b]
+        sgt = "sg%s%d" % (x, st)
+        kA, kD, kP, kN = "A%s" % x, "D%s" % x, "P%s" % x, "N%s" % x
+        cin, cint = (t("cfl"), "cfl%d" % h) if st == 0 else (t("ci"), "ci" + x)
+        last = st == ST - 1
+        n16 = 16 * LB
+        S(n16, GAT, ["X", "c16" + x], ["F" + x], lambda e, p: e.activation(F[:], T.X[:].indirect(t("c16")), ACT.Copy), pr=pr)
+
+        def dfm(e, p, c):
+            e.matmul(p[:, 512 * c:512 * c + 512], T.identb[:], F[:, 512 * c:512 * c + 512], True, False)
+            return e.matmul(p[:, 512 * c:512 * c + 512], T.negi[:], D[:, 512 * c:512 * c + 512], False, True)
+        if WAY(s, st, h, j) == "P":
+            V(n16, GAT, ["F" + x, "p16%d" % h], ["D" + x], lambda e, p: e.tensor_copy(D[:], F[:].indirect(t("p16"))), pr=pr)
+            for c in range(2):
+                P(2, 512, ["F" + x, "D" + x, "identb", "negi"], ["%s_%d" % (kD, c)], lambda e, p, c=c: dfm(e, p, c), pr=pr - .2, pool=("A", kD), bk=(c,))
+            S(n16, 1, ["%s_0" % kD, "%s_1" % kD], ["AD" + x], lambda e, p: e.activation(AD[:], p[:], ACT.Abs), pr=pr, pool=("A", kD), free=1, bk=(0, 1))
+        else:
+            S(n16, 1, ["F" + x], ["F2" + x], lambda e, p: e.activation(F2[:], F[:], ACT.Copy), pr=pr)
+            V(n16, GAT, ["F" + x, "F2" + x, "p16%d" % h], ["D" + x], lambda e, p: e.tensor_tensor(D[:], F2[:].indirect(t("p16")), F[:], A.subtract), pr=pr)
+            S(n16, 1, ["D" + x], ["AD" + x], lambda e, p: e.activation(AD[:], D[:], ACT.Abs), pr=pr)
+        for c in range(2):
+            P(1, 512, ["limT%d" % s, "E", "D" + x], ["%s_%d" % (kA, c)],
+              lambda e, p, c=c: e.matmul(p[:, 512 * c:512 * c + 512], T.limT[:, 256 * s + LH * h:256 * s + LH * h + LH],
+                                         T.E[:, n16 * j + 512 * c:n16 * j + 512 * c + 512], True, True),
+              pr=pr + 0.3, pool=("A", kA), bk=(c,))
+        V(n16, 1, ["AD" + x, kA + "_0", kA + "_1"], ["ni" + x], lambda e, p: e.tensor_tensor(ni[:], AD[:], p[:], A.is_gt), pr=pr, pool=("A", kA), free=1, bk=(0, 1))
+
+        def adm(e, p):
+            e.matmul(p[:, 0:LB], T.identf[:], t("u5"), True, False)
+            for k in range(16):
+                i = e.matmul(p[:, 0:LB], T.sel1[:, 128 * k:128 * k + 128], AD[:, k:n16:16], False, False)
+            return i
+
+        def nim(e, p):
+            for k in range(16):
+                i = e.matmul(p[:, 0:LB], T.sel2[:, 128 * k:128 * k + 128], ni[:, k:n16:16], False, k == 15)
+            return i
+        P(20, LB, ["AD" + x, "u5" + x, "identf", "sel1"], [kP], adm, pr=pr + 0.2, pool=("P", kP))
+        P(16, LB, ["ni" + x, "sel2"], [kP], nim, pr=pr, pool=("P", kP))
+        S(LB, 1, [kP], [sgt], lambda e, p: e.activation(sg, p[:, 0:LB], ACT.Sign, scale=-1.0), pr=pr - .5, pool=("P", kP), free=2)
+        V(LB, 1, [kP, cint], ["qq" + x], lambda e, p: e.tensor_tensor(t("qq"), p[:, 0:LB], cin, A.max), pr=pr - .5, pool=("P", kP), free=2)
+
+        def okm(e, p):
+            e.matmul(p[:, 0:LB], T.identf[:], t("u5"), True, False)
+            return e.matmul(p[:, 0:LB], T.okw[:], sg, False, True)
+        P(5, LB, [sgt, "u5" + x, "okw", "identf"], [kN], okm, pr=pr - .5, pool=("N", kN))
+        V(LB, 1, [kN, "qq" + x], ["cpp" + x], lambda e, p: e.tensor_tensor(t("cpp"), p[:, 0:LB], t("qq"), A.max), pr=pr - .5, pool=("N", kN), free=1)
+        V(LB, 1, ["cpp" + x], ["ci" + x], lambda e, p: e.tensor_scalar(t("ci"), t("cpp"), 4095, None, A.bitwise_and), pr=pr - .5)
+        if not last:
+            V(LB, 1, ["ci" + x], ["c16" + x], lambda e, p: e.tensor_copy(t("c16"), t("ci")), pr=pr - .5)
+            V(LB, 1, ["ci" + x], ["u5" + x], lambda e, p: e.tensor_scalar(t("u5"), t("ci"), 5.0, float(1 - OFF), A.mult, A.add), pr=pr - .4)
+
+    def end(s, h):
+        pr = ST * (s + 1) - 1.0 + 0.5 * h
+        q = H * s + h
+        n = lambda x: "%s%d" % (x, h)
+        t = lambda x: T["%s%d" % (x, h)]
+        kt, gt = "key%d%d" % (s, h), ("gro0%d" % h if s == 0 else "key%d%d" % (s, h))
+        pay = lambda a, b: T.pay[:, KG * q + a:KG * q + b]
+        fx = lambda a, b: T.fx[:, FW * q + a:FW * q + b]
+        kL = "L%d" % h
+
+        def lpm(e, p):
+            for b in range(16):
+                i = e.matmul(p[:, 0:FW], T.sel1[:, 128 * b:128 * b + 128], t("sg")[:, b:ST * LH:16], b == 0, b == 15)
+            return i
+
+        def mpm(e, p):
+            for k in range(ST):
+                i = e.matmul(p[:, 64:64 + NK], T.sameb[:], fx(NK * k, NK * k + NK), k == 0, k == ST - 1)
+            return i
+        P(16, FW, ["sg%d%d%d" % (h, j, k) for j in range(J) for k in range(ST)] + ["sel1"], [kL], lpm, pr=pr, pool=("N", kL))
+        S(FW, 1, [kL], ["fx%d" % q], lambda e, p: e.activation(fx(0, FW), p[:, 0:FW], ACT.Relu, bias=-15.0), pr=pr, pool=("N", kL))
+        S(NK, 1, [kL], [n("nk1")], lambda e, p: e.activation(t("nk1")[:], p[:, FW - NK:FW], ACT.Identity, scale=-512.0, bias=float(1024 * (s + 1) - 8192)), pr=pr, pool=("N", kL))
+        P(3, NK, ["fx%d" % q, "sameb"], [kL], mpm, pr=pr, pool=("N", kL))
+        V(NK, 1, [kL], [n("mi")], lambda e, p: e.tensor_copy(t("mi")[:], p[:, 64:64 + NK]), pr=pr, pool=("N", kL), free=1)
+        V(NK, 1, [n("mi")], [n("od")], lambda e, p: e.tensor_scalar(t("od")[:], t("mi")[:], 1024, None, A.bitwise_and), pr=pr)
+        V(NK, 2, [n("nk1"), n("od")], [n("xx")], lambda e, p: e.tensor_tensor(t("xx")[:], t("nk1")[:], t("od")[:], A.add), pr=pr)
+        V(NK, 2, [n("xx"), n("eb")], [n("dl")], lambda e, p: e.tensor_tensor(t("dl")[:], t("xx")[:], t("eb")[:], A.add), pr=pr)
+        V(NK, 2, [gt, n("od")], ["payg%d" % q], lambda e, p: e.tensor_tensor(pay(KW, KG), kv(s, h, KW, KG), t("od")[:], A.add), pr=pr)
+        V(KW, GAT, [n("dl"), n("eq"), "rep"], [n("em")], lambda e, p: e.tensor_tensor(t("em")[:], t("dl")[:].indirect(T.rep[:]), t("eq")[:], A.mult), pr=pr)
+        V(KW, 2, [kt, n("em")], ["pay%d" % q], lambda e, p: e.tensor_tensor(pay(0, KW), kv(s, h, 0, KW), t("em")[:], A.add), pr=pr)
+        add("G", 500, ["pay%d" % q, "payg%d" % q], ["snd%d" % q], lambda e, p: ctx["send"](1, kv(s + 1, h, 0, KG), pay(0, KG), "akey%d%d" % (s + 1, h)), pr=pr - 2, sem="sent", inc=NE, lat=2000)
+        add("W", 0, ["snd%d" % q], ["key%d%d" % (s + 1, h)], None, sem="akey%d%d" % (s + 1, h), inc=NE, lat=600)
+        if s:
+            add("G", 500, ["fx%d" % q], ["sndf%d" % q], lambda e, p: ctx["send"](-s, T.fl[:, FW * q:FW * q + FW], fx(0, FW), "afl%d" % q), pr=pr, sem="sent", inc=NE, lat=2000)
+            add("W", 0, ["sndf%d" % q], ["fl%d" % q], None, sem="afl%d" % q, inc=NE, lat=600)
+        V(LH, 3.5, [n("lst")] + ["ci%d%d" % (h, j) for j in range(J)], [n("pgw")], lambda e, p: e.tensor_copy(t("pgw")[:].indirect(t("lst")[:]), t("ci")[:]), pr=pr + .05)
+
+    def final(h):
+        pr = ST * NS + 0.5 * h
+        n = lambda x: "%s%d" % (x, h)
+        t = lambda x: T["%s%d" % (x, h)]
+        kt = "key%d%d" % (NS, h)
+        add("Q", 80, [n("pgw")], [], lambda e, p: e.dma_start(T.yg[:, 1024 * h:1024 * h + 1024], t("pgw")[:]), pr=pr, sem="outs", inc=16, lat=4000)
+        V(KW, 2, [kt, "keyc"], [n("hi")], lambda e, p: e.tensor_tensor(t("hi")[:], kv(NS, h, 0, KW), T.keyc[:], A.subtract), pr=pr - 3)
+        V(KW, GAT, [kt, n("hi"), "rep"], [n("fv")], lambda e, p: e.tensor_tensor(t("fv")[:], kv(NS, h, KW, KG).indirect(T.rep[:]), t("hi")[:], A.subtract), pr=pr - 3)
+        for c in range(2):
+            def fvm(e, p, c=c):
+                for b in range(16):
+                    i = e.matmul(p[0:8, 512 * c + b:512 * c + 512:16], T.fsel[:, 8 * b:8 * b + 8], t("fv")[:, 32 * c:32 * c + 32], True, True)
+                return i
+            P(16, 32, [n("fv"), "fsel"], ["Y%d_%d" % (h, c)], fvm, pr=pr - 3, pool=("A", "Y%d" % h), bk=(c,))
+        V(512, 1, ["Y%d_0" % h], ["yvsA%d" % h], lambda e, p: e.tensor_scalar(t("yvs")[:, 0:512], p[0:8, 0:512], float(NS), None, A.add), pr=pr - 3, pool=("A", "Y%d" % h), free=2)
+        S(512, 1, ["Y%d_1" % h], ["yvsB%d" % h], lambda e, p: e.activation(t("yvs")[:, 512:1024], p[0:8, 512:1024], ACT.Identity, bias=float(NS)), pr=pr - 3, pool=("A", "Y%d" % h), free=2, bk=(1,))
+        add("Q", 80, ["yvsA%d" % h, "yvsB%d" % h], [], lambda e, p: e.dma_start(T.yv[:, LH * h:LH * h + LH], t("yvs")[:]), pr=pr - 3, sem="outs", inc=16, lat=2200)
+        kM = "M%d" % h
+
+        def ysum(e, p):
+            for i in range(NS):
+                for k in range(ST):
+                    c = FW * (H * i + h) + NK * k
+                    r = e.matmul(p[:, 0:NK], T.identb[:], (T.fl if i else T.fx)[:, c:c + NK], i + k == 0, i == NS - 1 and k == ST - 1)
+            return r
+
+        def ymm(e, p):
+            for b in range(16):
+                r = e.matmul(p[0:8, 128 + b:256:16], T.fsel1[:, 8 * b:8 * b + 8], t("yb")[:], True, True)
+            return r
+        P(12, NK, ["fx%d" % h, "identb"] + ["fl%d" % (H * s + h) for s in range(1, NS)], [kM], ysum, pr=pr - 2, pool=("N", kM))
+        S(NK, 1, [kM], [n("yb")], lambda e, p: e.activation(t("yb")[:], p[:, 0:NK], ACT.Copy), pr=pr - 2, pool=("N", kM))
+        P(16, NK, [n("yb"), "fsel1"], [kM], ymm, pr=pr - 2, pool=("N", kM))
+        S(LH, 1, [kM], [n("yms")], lambda e, p: e.activation(t("yms")[:], p[0:8, 128:256], ACT.Copy), pr=pr - 2, pool=("N", kM), free=1)
+        add("Q", 80, [n("yms")], [], lambda e, p: e.dma_start(T.ym[:, LH * h:LH * h + LH], t("yms")[:]), pr=pr - 2, sem="outs", inc=16, lat=2200)
+
+    for s in range(NS):
+        for h in range(H):
+            begin(s, h)
+            for st in range(ST):
+                for j in range(J):
+                    step(s, st, h, j)
+            end(s, h)
+    for h in range(H):
+        final(h)
+    return ops
+
+
+POOLS = {"A": ("PA0", "PA1"), "P": ("PP0", "PP1"), "N": ("PN0", "PN1")}
+WAKE = 100.0
+LS, LB0 = 0.0, 0.0
+
+
+def deps_of(ops, order):
+    last, readers, out = {}, {}, {}
+    for i in order:
+        o, d = ops[i], set()
+        for r in o["rd"]:
+            if r in last:
+                d.add(last[r])
+        for w in o["wr"]:
+            if w in last:
+                d.add(last[w])
+            d.update(readers.get(w, ()))
+        d.discard(i)
+        out[i] = d
+        for r in o["rd"]:
+            readers.setdefault(r, []).append(i)
+        for w in o["wr"]:
+            last[w] = i
+            readers[w] = []
+    return out
+
+
+def plan(ops):
+    n = len(ops)
+    dep = deps_of(ops, range(n))
+    succ = [[] for _ in range(n)]
+    need = [len(dep[i]) for i in range(n)]
+    for i in range(n):
+        for d in dep[i]:
+            succ[d].append(i)
+    done, start, buf = [0.0] * n, [0.0] * n, {}
+    free = {e: 0.0 for e in "VSPGQW"}
+    slot = {k: [0.0] * len(v) for k, v in POOLS.items()}
+    held, fin = {}, {}
+    ready = [i for i in range(n) if not need[i]]
+    order = []
+    while ready:
+        best = {}
+        for i in ready:
+            o = ops[i]
+            t = free[o["eng"]] if o["eng"] != "W" else 0.0
+            for d in dep[i]:
+                t = max(t, done[d] + (0.0 if o["eng"] == "W" or ops[d]["eng"] == "P" and o["eng"] == "P" else WAKE))
+            if o["pool"] and o["pool"] not in held:
+                fr = [x for x in slot[o["pool"][0]] if x is not None]
+                if not fr:
+                    continue
+                t = max(t, min(fr))
+            best.setdefault(o["eng"], []).append((t, i))
+        cand = None
+        for e, lst in best.items():
+            t0 = min(lst)[0] + LB0
+            pick = min((ops[i]["pr"], t, i) for t, i in lst if t <= t0 + (LS if ops[i]["cost"] < 260 else 0))
+            if cand is None or pick[1] < cand[0]:
+                cand = (pick[1], pick[2])
+        t, i = cand
+        o = ops[i]
+        ready.remove(i)
+        if o["pool"]:
+            k = o["pool"]
+            if k not in held:
+                fr = [(x, y) for y, x in enumerate(slot[k[0]]) if x is not None]
+                held[k] = min(fr)[1]
+                slot[k[0]][held[k]] = None
+            buf[i] = POOLS[k[0]][held[k]]
+        start[i] = t
+        done[i] = t + o["cost"] + o["lat"]
+        free[o["eng"]] = t + o["cost"]
+        if o["pool"] and o["free"]:
+            ends = fin.setdefault(o["pool"], []) + [done[i] + WAKE]
+            fin[o["pool"]] = ends
+            if len(ends) == o["free"]:
+                slot[o["pool"][0]][held.pop(o["pool"])] = max(fin.pop(o["pool"]))
+        order.append(i)
+        for x in succ[i]:
+            need[x] -= 1
+            if not need[x]:
+                ready.append(x)
+    assert len(order) == n
+    order.sort(key=lambda i: start[i])
+    return order, buf, start, done
+
+
+def emit(g, T, ops, order, buf):
+    eng = {"V": g.vector, "S": g.scalar, "P": g.tensor, "Q": g.sync, "G": g}
+    cnt = {"V": "cV", "S": "cS", "P": "cP", "G": "cG"}
+    dep = deps_of(ops, order)
+    total, at, after, bank = {}, {}, {}, {}
+    clock = {e: {} for e in eng}
+    for i in order:
+        o = ops[i]
+        d = set(dep[i])
+        b = buf.get(i)
+        if b:
+            for k in o["bk"]:
+                use = bank.setdefault((b, k), {})
+                d.update(v for x, v in use.items() if x != o["eng"])
+                use[o["eng"]] = i
+        if o["eng"] == "W":
+            at[i] = (o["sem"], o["inc"])
+            after[i] = {o["sem"]: o["inc"]}
+            continue
+        e, c = eng[o["eng"]], clock[o["eng"]]
+        for k in sorted(d, reverse=True, key=lambda k: (at[k][1], k)):
+            if o["eng"] == "P" and ops[k]["eng"] == "P":
+                continue
+            s, v = at[k]
+            if c.get(s, 0) >= v:
+                continue
+            e.wait_ge(T.sem[s], v)
+            for s2, v2 in after[k].items():
+                c[s2] = max(c.get(s2, 0), v2)
+        r = o["fn"](e, T[b] if b else None)
+        s = o["sem"] or cnt[o["eng"]]
+        if s != "sent":
+            r.then_inc(T.sem[s], o["inc"] or 1)
+        total[s] = total.get(s, 0) + (o["inc"] or 1)
+        at[i] = (s, total[s])
+        after[i] = dict(c)
+        after[i][s] = total[s]
+    for s in ("cV", "cS", "cP", "cG", "outs", "sent"):
+        g.wait_ge(T.sem[s], total[s])
+
+
+def rank_program(g, core, T, topo):
+    rank = T.rank_of(core)
+    if rank is None:
+        return
+    cores = T.cores
+
+    def send(d, out, inp, sem):
+        dst = cores[(rank + d) % len(cores)]
+        rid, pid = topo.addr(dst)[:2]
+        return g.remote_dma(out, inp, T.sem[sem], T.sem["sent"], pid, rid, topo.mask(core, dst))
+
+    ne = len(topo.engines(core, cores[(rank + 1) % len(cores)]))
+    ops = graph({"T": T, "send": send, "X": ne})
+    order, buf, start, done = plan(ops)
+    emit(g, T, ops, order, buf)

@@ -1,75 +1,64 @@
 from concourse.mybir import AluOpType, ActivationFunctionType
 
 ACT = ActivationFunctionType
-NS, ST = 4, 3
-H, J = 2, 2
-LH, LB = 128, 64
-NK = LH // 16
-KW = 8 * NK
-KG = KW + NK
-FW = ST * NK
+NS, ST, NL = 4, 3, 256
+LU, NU = 64, 4
 BIG = 65536
 OFF = 491520
+MAG = 129
 
-SCRATCH = {
-    "X": ("sbuf", [128, 4096], "bfloat16"),
-    "vvi": ("sbuf", [64, 256], "int32"), "vvb": ("sbuf", [64, 256], "bfloat16"), "R": ("sbuf", [64, 2048], "bfloat16"),
-    "limb": ("sbuf", [128, 256], "bfloat16"),
-    "ones": ("sbuf", [128, 2048], "bfloat16"), "E": ("sbuf", [128, 2048], "bfloat16"),
-    "gA": ("sbuf", [128, 128], "bfloat16"), "gm": ("sbuf", [128, 128], "bfloat16"), "okw": ("sbuf", [128, 128], "bfloat16"),
-    "g8A": ("sbuf", [64, 128], "bfloat16"), "g8m": ("sbuf", [64, 128], "bfloat16"), "g8s": ("sbuf", [64, 128], "bfloat16"),
-    "vsel": ("sbuf", [64, 2048], "bfloat16"),
-    "identb": ("sbuf", [128, 128], "bfloat16"), "negi": ("sbuf", [128, 128], "bfloat16"), "identf": ("sbuf", [128, 128], "float32"),
-    "fsel1": ("sbuf", [128, 128], "bfloat16"), "fsel": ("sbuf", [128, 128], "bfloat16"),
-    "sel1": ("sbuf", [128, 2048], "bfloat16"), "sel2": ("sbuf", [128, 2048], "bfloat16"),
-    "pm": ("sbuf", [128, 128], "int32"), "pm2": ("sbuf", [128, 128], "int32"), "sameb": ("sbuf", [128, 128], "bfloat16"),
-    "om": ("sbuf", [64, 8], "int32"), "om2": ("sbuf", [64, 8], "int32"), "omask": ("sbuf", [64, 8], "float32"),
-    "pc4": ("sbuf", [128, 4], "int32"), "pc15": ("sbuf", [128, 4], "int32"), "pc8": ("sbuf", [128, 4], "float32"),
-    "pc7": ("sbuf", [128, 4], "int32"), "rep": ("sbuf", [128, 4], "uint16"),
-    "kc": ("sbuf", [128, KW], "int32"), "keyc": ("sbuf", [128, KW], "int32"),
-    "limT": ("sbuf", [128, NS * 256], "bfloat16"),
-    "keys": ("sbuf", [128, (NS + 1) * H * KG], "int32"),
-    "pay": ("sbuf", [128, NS * H * KG], "int32"),
-    "fx": ("sbuf", [128, NS * H * FW], "bfloat16"),
-    "fl": ("sbuf", [128, NS * H * FW], "bfloat16"),
-    "PA0": ("psum", [128, 1024], "float32"), "PA1": ("psum", [128, 1024], "float32"),
-    "PP0": ("psum", [128, 512], "float32"), "PP1": ("psum", [128, 512], "float32"),
-    "PN0": ("psum", [128, 512], "float32"), "PN1": ("psum", [128, 512], "float32"),
-}
-for _h in range(H):
-    for _n, _w, _d in (("pgi", 1024, "int32"), ("pgw", 1024, "float32"), ("prew", 1024, "float32"), ("mA", KW // 2, "int32"), ("mB", KW // 4, "int32"),
-                       ("km", NK, "int32"), ("li", NK, "int32"), ("lst", NK, "uint16"), ("ea", NK, "int32"), ("eb", NK, "int32"),
-                       ("eq", KW, "float32"), ("cfl", LH, "float32"), ("c16", LH, "uint16"), ("p16", LH, "uint16"), ("u5", LH, "float32"),
-                       ("ci", LH, "int32"), ("cpp", LH, "int32"), ("qq", LH, "float32"), ("sg", ST * LH, "bfloat16"), ("nk1", NK, "float32"),
-                       ("mi", NK, "int32"), ("od", NK, "int32"), ("xx", NK, "float32"), ("dl", NK, "float32"), ("em", KW, "float32"),
-                       ("hi", KW, "int32"), ("fv", KW, "bfloat16"), ("yb", NK, "bfloat16")):
-        SCRATCH["%s%d" % (_n, _h)] = ("sbuf", [128, _w], _d)
-    SCRATCH["yvs%d" % _h] = ("sbuf", [8, 1024], "float32")
-    SCRATCH["yms%d" % _h] = ("sbuf", [8, LH], "float32")
-    for _j in range(J):
-        for _n in ("F", "F2", "D", "AD", "ni"):
-            SCRATCH["%s%d%d" % (_n, _h, _j)] = ("sbuf", [128, 16 * LB], "bfloat16")
+CFG = dict(LT=64, CH=512, way="BBBBBT", copy="G", look=0.0, banks=(3, 2, 3), t0=7500.0, slot=3200.0, hold=1e9, mix=1.0, cap=5000.0,
+           turn=((0, 3, 7), (2, 5, 9), (4, 8, 11), (6, 10, 13)), end=181400.0,
+           gat=1.5, wake=100.0, dma=2300.0, send=2600.0)
+LT, CH = CFG["LT"], CFG["CH"]
+NT, NK, NC = NL // LT, LT // 16, 16 * LU // CH
+KW = 8 * NK
+HD = 16 * (-(-3 * NK // 16))
+PW = HD + KW
+LG = NK.bit_length() - 1
 
-SEMAPHORES = ["cV", "cS", "cP", "cG", "lvv", "llim", "lxt", "lpg0", "lpg1", "lpre0", "lpre1", "outs", "sent"]
-SEMAPHORES += ["alim%d" % s for s in range(1, NS)] + ["akey%d%d" % (s, h) for s in range(1, NS + 1) for h in range(H)]
-SEMAPHORES += ["afl%d" % x for x in range(H, H * NS)]
+B16, F32, I32, U16 = "bfloat16", "float32", "int32", "uint16"
+SCRATCH = {}
+for _n, _p, _w, _d in (
+        ("X", 128, 4096, B16), ("pgi", 128, 2048, I32), ("pgw", 128, 2048, F32), ("prew", 128, 2048, F32), ("E", 128, 2048, B16),
+        ("vvi", 128, 256, I32), ("vvb", 128, 256, B16), ("R", 64, 2048, B16), ("limb", 128, 256, B16), ("limT", 128, NS * 256, B16),
+        ("ones", 128, 128, B16), ("ident", 128, 128, B16), ("mI", 128, 128 * 10, B16), ("i5", 128, 128, F32),
+        ("gA", 128, 128, B16), ("gm", 128, 128, B16), ("okw", 128, 128, B16), ("W", 128, 3 * 144, B16),
+        ("g8A", 64, 8, B16), ("g8m", 64, 8, B16), ("W8", 64, 144, B16), ("cst", 64, 128, B16), ("crow", 64, 160, B16), ("cz", 64, 8 * NK, B16),
+        ("pm", 128, 128, I32), ("pm2", 128, 128, I32), ("same", 128, 256, B16),
+        ("om", 64, 8, I32), ("om2", 64, 8, I32), ("omask", 64, 8, F32),
+        ("vp", 128, 16, I32), ("vp2", 128, 16, I32), ("vperm", 128, 16, U16),
+        ("p1", 128, 2, I32), ("p8", 128, 2, I32), ("bi", 128, 8, I32), ("bf", 128, 8, F32), ("cc", 128, 8, I32),
+        ("rep7", 128, 8, U16), ("repk", 128, 8, U16), ("turn8", 128, 8, U16), ("repg", 128, 8, U16), ("pa", 128, 8, F32),
+        ("lane8", 128, NK, B16), ("rst", 128, KW, B16), ("oko", 128, KW, B16), ("ook", 128, KW, B16),
+        ("keys", 128, (NS + 1) * NT * PW, B16), ("pay", 128, NS * NT * PW, B16),
+        ("ks", 128, NT * KW, B16), ("eq", 128, NT * KW, B16), ("tt", 128, NT * KW, B16), ("lst", 128, NT * NK, U16),
+        ("fx", 128, NT * ST * NK, B16), ("hn", 128, NT * 2 * NK, B16), ("sg", 128, ST * NL, B16),
+        ("fa", 128, NT * KW, B16), ("fv", 128, NT * KW, B16), ("yvs", 8, 8 * NL, F32), ("yms", 8, NL, F32),
+        ("c16", 128, NL, U16), ("p16", 128, NL, U16), ("cf", 128, NL, F32), ("ci", 128, NL, I32), ("cpp", 128, NL, I32), ("qq", 128, NL, F32),
+        ("F", 128, 16 * NL, B16), ("F2", 128, 16 * NL, B16), ("D", 128, 16 * NL, B16), ("AD", 128, 16 * NL, B16), ("ni", 128, 16 * NL, B16)):
+    SCRATCH[_n] = ("sbuf", [_p, _w], _d)
+POOLS = {}
+for _k, _n, _w in zip("APN", CFG["banks"], (CH, 512, 512)):
+    POOLS[_k] = ["P%s%d" % (_k, _i) for _i in range(_n)]
+    for _b in POOLS[_k]:
+        SCRATCH[_b] = ("psum", [128, _w], F32)
+
+SEMAPHORES = ["cV", "cS", "cP", "cG", "lvv", "llim", "lxt", "outs", "sent"]
+SEMAPHORES += ["lpg%d" % t for t in range(NT)] + ["lpre%d" % t for t in range(NT)] + ["cp%d" % x for x in range(NU * NC)]
+SEMAPHORES += ["alim%d" % s for s in range(1, NS)] + ["akey%d%d" % (s, t) for s in range(1, NS + 1) for t in range(NT)]
 
 CYC, PEC = 0.83, 0.42
-GAT = 1.5
-VFIX, SFIX, PFIX = 60, 80, 0
-
-
-def WAY(s, st, h, j):
-    return "PS"[j]
+VFIX, SFIX = 55, 70
 
 
 def graph(ctx):
-    T, A = ctx["T"], AluOpType
-    NE = ctx["X"]
-    ops = []
+    T, A, NE = ctx["T"], AluOpType, ctx["NE"]
+    GAT = CFG["gat"]
+    ops, at = [], [0.0]
 
-    def add(eng, cost, rd, wr, fn, pr=0.0, pool=None, free=None, sem=None, inc=None, lat=0.0, bk=(0,)):
-        ops.append(dict(eng=eng, cost=cost, rd=rd, wr=wr, fn=fn, pr=pr, pool=pool, free=free, sem=sem, inc=inc, lat=lat, bk=bk))
+    def add(eng, cost, rd, wr, fn, pool=None, free=None, sem=None, inc=None, lat=0.0, bk=(0,), due=1e9):
+        ops.append(dict(eng=eng, cost=cost, rd=rd, wr=wr, fn=fn, due=due, pool=pool, free=free, sem=sem, inc=inc, lat=lat, bk=bk))
 
     def V(n, cyc, rd, wr, fn, **k):
         add("V", VFIX + max(64, n * cyc) * CYC, rd, wr, fn, **k)
@@ -78,254 +67,289 @@ def graph(ctx):
         add("S", SFIX + max(64, n * cyc) * CYC, rd, wr, fn, **k)
 
     def P(k, n, rd, wr, fn, **kw):
-        add("P", k * (PFIX + max(64, n) * PEC), rd, wr, fn, **kw)
+        add("P", k * max(64, n) * PEC, rd, wr, fn, **kw)
 
     def G(n, rd, wr, fn, **k):
         add("G", 150 + 2 * n * CYC, rd, wr, fn, **k)
 
-    def load(eng, out, inp, tile, sem, lat, pr):
-        add(eng, 80, [], [tile], lambda e, p: e.dma_start(out, inp), pr=pr, sem=sem, inc=16, lat=lat)
+    def load(eng, out, inp, tile, sem, lat, rd=()):
+        add(eng, 60, list(rd), [tile], lambda e, p: e.dma_start(out, inp), sem=sem, inc=16, lat=lat, due=len(ops) - 1e9)
 
-    def kv(s, h, a, b):
-        return T.keys[:, (H * s + h) * KG + a:(H * s + h) * KG + b]
+    def mms(lst, start=True, stop=True):
+        def fn(e, p):
+            for i, (o, l, r) in enumerate(lst):
+                x = e.matmul(p[o], l, r, start and i == 0, stop and i == len(lst) - 1)
+            return x
+        return fn
 
-    load("Q", T.vvi[:], T.vv[:], "vvi", "lvv", 2200, -9.0)
-    load("Q", T.pgi0[:], T.pg[:, 0:1024], "pgi0", "lpg0", 4000, -8.9)
-    load("S", T.X[:], T.xt[:], "X", "lxt", 7500, -9.0)
-    load("Q", T.limb[:], T.lim[:], "limb", "llim", 3000, -8.8)
-    load("Q", T.pgi1[:], T.pg[:, 1024:2048], "pgi1", "lpg1", 9500, -8.7)
+    def cols(a, b, c=None):
+        return (slice(None), slice(a, b, c))
 
-    def pre_fill(h):
-        G(1024, [], ["prew%d" % h], lambda e, p: e.iota(T["prew%d" % h][:], [[0, 2], [16, 64], [0, 8]], 0, 0, allow_small_or_imprecise_dtypes=True), pr=-9.0 + 3 * h)
-        add("G", 1100, ["prew%d" % h], ["prew%d" % h], lambda e, p: e.dma_start(T["prew%d" % h][:], T.pre[:, 1024 * h:1024 * h + 1024], accum_op=A.add),
-            pr=-8.9 + 3 * h, sem="lpre%d" % h, inc=16, lat=4000)
+    def kv(s, t, a, b, c=None):
+        return T.keys[:, (NT * s + t) * PW + a:(NT * s + t) * PW + b:c]
 
-    V(128, 0.5, [], ["ones"], lambda e, p: e.memset(T.ones[:, 0:128], 1.0), pr=-9.5)
-    V(1920, 0.5, [], ["onesE"], lambda e, p: e.memset(T.ones[:, 128:2048], 1.0), pr=-8.0)
-    G(8, [], ["om"], lambda e, p: e.iota(T.om[:], [[-1, 8]], 8, 1), pr=-9.9)
-    G(4, [], ["pc4"], lambda e, p: e.iota(T.pc4[:], [[0, 4]], 0, 1), pr=-9.8)
-    G(KW, [], ["kc"], lambda e, p: e.iota(T.kc[:], [[1, 8], [128, NK]], 0, 0), pr=-9.7)
-    V(8, 1, ["om"], ["om2"], lambda e, p: e.tensor_scalar(T.om2[:], T.om[:], 7, None, A.bitwise_and), pr=-9.0)
-    V(8, 1, ["om2"], ["omask"], lambda e, p: e.tensor_scalar(T.omask[:], T.om2[:], 0.0, None, A.is_equal), pr=-9.0)
-    V(4, 1, ["pc4"], ["pc15"], lambda e, p: e.tensor_scalar(T.pc15[:], T.pc4[:], 15, None, A.bitwise_and), pr=-9.0)
-    V(4, 1, ["pc15"], ["pc8"], lambda e, p: e.tensor_scalar(T.pc8[:], T.pc15[:], 8.0, None, A.mult), pr=-9.0)
-    V(4, 1, ["pc4"], ["pc7"], lambda e, p: e.tensor_scalar(T.pc7[:], T.pc4[:], 7, None, A.bitwise_and), pr=-7.0)
-    V(4, 1, ["pc7"], ["rep"], lambda e, p: e.tensor_copy(T.rep[:], T.pc7[:]), pr=-7.0)
-    V(KW, 1, ["kc", "pc8"], ["keyc"], lambda e, p: e.tensor_scalar(T.keyc[:], T.kc[:], T.pc8[:, 0:1], None, A.add), pr=-9.0)
-    G(128, ["ones"], ["g8A"], lambda e, p: e.affine_select(T.g8A[:], T.ones[0:64, 0:128], [[-8, 8], [0, 16]], A.is_ge, 0.0, 0, 1), pr=-9.6)
-    G(128, ["g8A"], ["g8m"], lambda e, p: e.affine_select(T.g8m[:], T.g8A[:], [[8, 8], [0, 16]], A.is_ge, 0.0, 7, -1), pr=-9.5)
-    S(128, 1, ["g8m"], ["g8s"], lambda e, p: e.activation(T.g8s[:], T.g8m[:], ACT.Copy, scale=-1024.0), pr=-9.0)
-    V(2048, 0.5, [], ["vsel"], lambda e, p: e.memset(T.vsel[:], 0.0), pr=-9.2)
-    for k in range(8):
-        V(16, 1, ["g8s"], ["vsel"], lambda e, p, k=k: e.tensor_copy(T.vsel[:, 16 * k:2048:129], T.g8s[:, 16 * k:16 * k + 16]), pr=-9.0)
-    pre_fill(0)
-    V(256, 1, ["vvi"], ["vvb"], lambda e, p: e.tensor_copy(T.vvb[:], T.vvi[:]), pr=-9.0)
-    for h in range(H):
-        for o in range(8):
-            V(128, 0.5, ["vvb", "omask"], ["R%d" % h],
-              lambda e, p, h=h, o=o: e.tensor_scalar(T.R[:, 1024 * h + 128 * o:1024 * h + 128 * o + 128], T.vvb[:, 128 * h:128 * h + 128], T.omask[:, o:o + 1], None, A.mult),
-              pr=-9.0 + 2 * h)
+    MUL = (2, 3, 4, 5, 6, 7, -1, -8, -16)
+    WMUL = (1, BIG, -1) if set(CFG["way"]) & set("AC") else (1, BIG)
 
-        def vmm(e, p, h=h):
-            for b in range(16):
-                i = e.matmul(p[:, 0:KW], T.vsel[:, 128 * b:128 * b + 128], T.R[:, 1024 * h + b:1024 * h + 1024:16], b == 0, b == 15)
-            return i
-        P(16, KW, ["vsel", "R%d" % h], ["vP%d" % h], vmm, pr=-9.0 + 2 * h, pool=("N", "vP%d" % h))
-        V(KW, 1, ["vP%d" % h, "keyc"], ["key0%d" % h], lambda e, p, h=h: e.tensor_tensor(kv(0, h, 0, KW), p[:, 0:KW], T.keyc[:], A.add),
-          pr=-9.0 + 2 * h, pool=("N", "vP%d" % h), free=1)
-        V(NK, 1, [], ["gro0%d" % h], lambda e, p, h=h: e.memset(kv(0, h, KW, KG), 0), pr=-8.0 + 2 * h)
-        V(1024, 1, ["pgi%d" % h], ["pgw%d" % h], lambda e, p, h=h: e.tensor_copy(T["pgw%d" % h][:], T["pgi%d" % h][:]), pr=-8.0 + 3 * h)
-    G(128, ["ones"], ["identb"], lambda e, p: e.affine_select(T.identb[:], T.ones[:, 0:128], [[-1, 128]], A.is_equal, 0.0, 0, 1), pr=-8.5)
-    S(128, 1, ["identb"], ["negi"], lambda e, p: e.activation(T.negi[:], T.identb[:], ACT.Copy, scale=-1.0), pr=-7.0)
-    S(128, 1, ["identb"], ["identf"], lambda e, p: e.activation(T.identf[:], T.identb[:], ACT.Copy), pr=-7.0)
-    G(128, ["ones"], ["gA"], lambda e, p: e.affine_select(T.gA[:], T.ones[:, 0:128], [[-16, 8], [0, 16]], A.is_ge, 0.0, 0, 1), pr=-8.4)
-    G(128, ["gA"], ["gm"], lambda e, p: e.affine_select(T.gm[:], T.gA[:], [[16, 8], [0, 16]], A.is_ge, 0.0, 15, -1), pr=-8.3)
-    S(128, 1, ["gm"], ["okw"], lambda e, p: e.activation(T.okw[:], T.gm[:], ACT.Copy, scale=float(OFF // 16)), pr=-7.0)
-    V(2048, 0.5, [], ["sel1"], lambda e, p: e.memset(T.sel1[:], 0.0), pr=-8.0)
-    for k in range(8):
-        V(16, 1, ["gm"], ["sel1"], lambda e, p, k=k: e.tensor_copy(T.sel1[:, 16 * k:2048:129], T.gm[:, 16 * k:16 * k + 16]), pr=-7.5)
-    S(2048, 1, ["sel1"], ["sel2"], lambda e, p: e.activation(T.sel2[:], T.sel1[:], ACT.Copy, scale=float(BIG)), pr=-7.5)
+    def mI(x):
+        return T.ident[:] if x == 1 else T.mI[:, 128 * MUL.index(x):128 * MUL.index(x) + 128]
 
-    def lmm(e, p):
-        e.matmul(p[:, 0:128], T.limb[:, 0:128], T.identb[:], True, True)
-        return e.matmul(p[:, 128:256], T.limb[:, 128:256], T.identb[:], True, True)
-    P(2, 128, ["limb", "identb"], ["lP"], lmm, pr=-7.5, pool=("N", "lP"))
-    S(256, 1, ["lP"], ["limT0"], lambda e, p: e.activation(T.limT[:, 0:256], p[:, 0:256], ACT.Copy), pr=-7.4, pool=("N", "lP"), free=1)
-    G(2048, ["ones", "onesE"], ["E"], lambda e, p: e.affine_select(T.E[:], T.ones[:], [[-1, 128], [0, 16]], A.is_equal, 0.0, 0, 1), pr=-7.5)
-    pre_fill(1)
-    G(128, [], ["pm"], lambda e, p: e.iota(T.pm[:], [[-1, 128]], 2048, 1), pr=-5.5)
-    V(128, 1, ["pm"], ["pm2"], lambda e, p: e.tensor_scalar(T.pm2[:], T.pm[:], 15, None, A.bitwise_and), pr=0.5)
-    V(128, 1, ["pm2"], ["sameb"], lambda e, p: e.tensor_scalar(T.sameb[:], T.pm2[:], 0.0, 1024.0, A.is_equal, A.mult), pr=0.5)
-    for s in range(1, NS):
-        add("G", 500, ["limT0"], [], lambda e, p, s=s: ctx["send"](s, T.limT[:, 256 * s:256 * s + 256], T.limT[:, 0:256], "alim%d" % s), pr=-5.0, sem="sent", inc=NE, lat=2500)
-        add("W", 0, [], ["limT%d" % s], None, sem="alim%d" % s, inc=NE, lat=15000)
-    G(128, ["ones"], ["fsel1"], lambda e, p: e.affine_select(T.fsel1[:], T.ones[:, 0:128], [[-1, 16], [-16, 8]], A.is_equal, 0.0, 0, 1), pr=-4.0)
-    S(128, 1, ["fsel1"], ["fsel"], lambda e, p: e.activation(T.fsel[:], T.fsel1[:], ACT.Copy, scale=1.0 / 1024.0), pr=1.5)
+    def mt(x):
+        return "ident" if x == 1 else "mI%d" % x
 
-    def begin(s, h):
-        pr = ST * s - 0.6 + 0.5 * h
-        kt, gt = "key%d%d" % (s, h), ("gro0%d" % h if s == 0 else "key%d%d" % (s, h))
-        n = lambda x: "%s%d" % (x, h)
-        t = lambda x: T["%s%d" % (x, h)]
-        V(KW // 2, 2, [kt], [n("mA")], lambda e, p: e.tensor_tensor(t("mA")[:], kv(s, h, 0, KW // 2), kv(s, h, KW // 2, KW), A.min), pr=pr)
-        V(KW // 4, 2, [n("mA")], [n("mB")], lambda e, p: e.tensor_tensor(t("mB")[:], t("mA")[:, 0:KW // 4], t("mA")[:, KW // 4:KW // 2], A.min), pr=pr)
-        V(NK, 2, [n("mB")], [n("km")], lambda e, p: e.tensor_tensor(t("km")[:], t("mB")[:, 0:NK], t("mB")[:, NK:2 * NK], A.min), pr=pr)
-        V(NK, 1, [n("km")], [n("li")], lambda e, p: e.tensor_scalar(t("li")[:], t("km")[:], 1023, None, A.bitwise_and), pr=pr)
-        V(NK, 1, [n("li")], [n("lst")], lambda e, p: e.tensor_copy(t("lst")[:], t("li")[:]), pr=pr)
-        V(LH, GAT, [n("pgw"), n("lst")], ["c16%d%d" % (h, j) for j in range(J)], lambda e, p: e.tensor_copy(t("c16")[:], t("pgw")[:].indirect(t("lst")[:])), pr=pr)
-        S(LH, GAT, [n("pgw"), n("lst")], [n("cfl")], lambda e, p: e.activation(t("cfl")[:], t("pgw")[:].indirect(t("lst")[:]), ACT.Copy), pr=pr + .02)
-        V(LH, GAT, [n("prew"), n("lst")], [n("p16")], lambda e, p: e.tensor_copy(t("p16")[:], t("prew")[:].indirect(t("lst")[:])), pr=pr + .01)
-        S(LH, 1, [n("cfl")], ["u5%d%d" % (h, j) for j in range(J)], lambda e, p: e.activation(t("u5")[:], t("cfl")[:], ACT.Identity, scale=5.0, bias=float(1 - OFF)), pr=pr + .3)
-        V(NK, 2, [gt, n("km")], [n("ea")], lambda e, p: e.tensor_tensor(t("ea")[:], kv(s, h, KW, KG), t("km")[:], A.subtract), pr=pr + .9)
-        V(NK, 2, [n("ea"), n("li")], [n("eb")], lambda e, p: e.tensor_tensor(t("eb")[:], t("ea")[:], t("li")[:], A.add), pr=pr + .9)
-        V(KW, GAT, [n("km"), kt, "rep"], [n("eq")], lambda e, p: e.tensor_tensor(t("eq")[:], t("km")[:].indirect(T.rep[:]), kv(s, h, 0, KW), A.is_equal), pr=pr + .9)
+    def sel(x, b):
+        return T.W[:, 144 * WMUL.index(x) + 15 - b:144 * WMUL.index(x) + 143 - b]
 
-    def step(s, st, h, j):
-        pr = ST * s + st + 0.5 * h + 0.25 * j
-        x = "%d%d" % (h, j)
-        a, b = LB * j, LB * j + LB
-        F, F2, D, AD, ni = T["F" + x], T["F2" + x], T["D" + x], T["AD" + x], T["ni" + x]
-        t = lambda n: T["%s%d" % (n, h)][:, a:b]
-        sg = T["sg%d" % h][:, LH * st + a:LH * st + b]
-        sgt = "sg%s%d" % (x, st)
-        kA, kD, kP, kN = "A%s" % x, "D%s" % x, "P%s" % x, "N%s" % x
-        cin, cint = (t("cfl"), "cfl%d" % h) if st == 0 else (t("ci"), "ci" + x)
-        last = st == ST - 1
-        n16 = 16 * LB
-        S(n16, GAT, ["X", "c16" + x], ["F" + x], lambda e, p: e.activation(F[:], T.X[:].indirect(t("c16")), ACT.Copy), pr=pr)
+    load("Q", T.vvi[0:64, :], T.vv[:], "vvi", "lvv", 2000)
+    load("Q", T.limb[:], T.lim[:], "limb", "llim", 2600)
+    load("Q", T.pgi[:, 0:8 * LT], T.pg[:, 0:8 * LT], "pgi0", "lpg0", 2600 + 20 * LT)
+    load("Q", T.X[:], T.xt[:], "X", "lxt", 6300 + 20 * LT)
+    for t in range(1, NT):
+        load("Q", T.pgi[:, 8 * LT * t:8 * LT * t + 8 * LT], T.pg[:, 8 * LT * t:8 * LT * t + 8 * LT], "pgi%d" % t, "lpg%d" % t, 8000 + 40 * LT * t)
 
-        def dfm(e, p, c):
-            e.matmul(p[:, 512 * c:512 * c + 512], T.identb[:], F[:, 512 * c:512 * c + 512], True, False)
-            return e.matmul(p[:, 512 * c:512 * c + 512], T.negi[:], D[:, 512 * c:512 * c + 512], False, True)
-        if WAY(s, st, h, j) == "P":
-            V(n16, GAT, ["F" + x, "p16%d" % h], ["D" + x], lambda e, p: e.tensor_copy(D[:], F[:].indirect(t("p16"))), pr=pr)
-            for c in range(2):
-                P(2, 512, ["F" + x, "D" + x, "identb", "negi"], ["%s_%d" % (kD, c)], lambda e, p, c=c: dfm(e, p, c), pr=pr - .2, pool=("A", kD), bk=(c,))
-            S(n16, 1, ["%s_0" % kD, "%s_1" % kD], ["AD" + x], lambda e, p: e.activation(AD[:], p[:], ACT.Abs), pr=pr, pool=("A", kD), free=1, bk=(0, 1))
+    bits = (("p1", A.bitwise_and, 8, None, None), ("p1", A.logical_shift_right, 3, A.bitwise_and, 1), ("p8", A.bitwise_and, 127, None, None),
+            ("p8", A.bitwise_and, 8 * NK - 8, None, None), ("p1", A.bitwise_and, 15, A.logical_shift_right, LG), ("p1", A.bitwise_and, NK - 1, None, None))
+    V(128, 0.5, [], ["ones"], lambda e, p: e.memset(T.ones[:], 1.0))
+    V(256, 1, [], ["vvu"], lambda e, p: e.memset(T.vvi[64:128, :], 0))
+    G(16, [], ["vp"], lambda e, p: e.iota(T.vp[:], [[1, 16]], 0, 16))
+    V(16, 1, ["vp"], ["vp2"], lambda e, p: e.tensor_scalar(T.vp2[:], T.vp[:], 255, None, A.bitwise_and))
+    V(16, 1, ["vp2"], ["vperm"], lambda e, p: e.tensor_copy(T.vperm[:], T.vp2[:]))
+    G(8, [], ["om"], lambda e, p: e.iota(T.om[:], [[-1, 8]], 8, 1))
+    V(8, 1, ["om"], ["om2"], lambda e, p: e.tensor_scalar(T.om2[:], T.om[:], 7, None, A.bitwise_and))
+    V(8, 1, ["om2"], ["omask"], lambda e, p: e.tensor_scalar(T.omask[:], T.om2[:], 0.0, None, A.is_equal))
+    G(2, [], ["p1"], lambda e, p: e.iota(T.p1[:], [[0, 2]], 0, 1))
+    G(2, [], ["p8"], lambda e, p: e.iota(T.p8[:], [[0, 2]], 0, 8))
+    G(8, [], ["cc"], lambda e, p: e.iota(T.cc[:], [[1, 8]], 0, 0))
+    for i, (src, o0, a0, o1, a1) in enumerate(bits):
+        V(1, 1, [src], ["bi%d" % i], lambda e, p, i=i, src=src, o0=o0, a0=a0, o1=o1, a1=a1:
+          e.tensor_scalar(T.bi[:, i:i + 1], T[src][:, 0:1], a0, a1, o0, o1) if o1 else e.tensor_scalar(T.bi[:, i:i + 1], T[src][:, 0:1], a0, None, o0))
+    V(3, 1, ["bi0", "bi1", "bi2"], ["bfa"], lambda e, p: e.tensor_copy(T.bf[:, 0:3], T.bi[:, 0:3]))
+    V(3, 1, ["bi3", "bi4", "bi5"], ["bfb"], lambda e, p: e.tensor_copy(T.bf[:, 3:6], T.bi[:, 3:6]))
+    S(1, 1, ["bfa"], ["bf7"], lambda e, p: e.activation(T.bf[:, 6:7], T.bf[:, 0:1], ACT.Identity, bias=7.0))
+    S(1, 1, ["bfb"], ["bfg"], lambda e, p: e.activation(T.bf[:, 7:8], T.bf[:, 5:6], ACT.Identity, bias=float(NK)))
+    V(8, 1, ["cc", "bf7"], ["rep7"], lambda e, p: e.tensor_scalar(T.rep7[:], T.cc[:], 16.0, T.bf[:, 6:7], A.mult, A.add))
+    V(8, 1, ["cc", "bfa"], ["repk"], lambda e, p: e.tensor_scalar(T.repk[:], T.cc[:], 2.0, T.bf[:, 1:2], A.mult, A.add))
+    V(8, 1, ["cc", "bfa"], ["lane8"], lambda e, p: e.tensor_scalar(T.lane8[:], T.cc[:, 0:NK], 128.0, T.bf[:, 2:3], A.mult, A.add))
+    V(8, 1, ["cc", "bfb"], ["pa"], lambda e, p: e.tensor_scalar(T.pa[:], T.cc[:], float(16 // NK), T.bf[:, 3:4], A.mult, A.add))
+    V(8, 1, ["pa", "bfb"], ["perm"], lambda e, p: e.tensor_scalar(T.turn8[:], T.pa[:], T.bf[:, 4:5], None, A.add))
+    V(8, 1, ["cc", "bfg"], ["repg"], lambda e, p: e.tensor_scalar(T.repg[:], T.cc[:], 0.0, T.bf[:, 7:8], A.mult, A.add))
+    V(KW, 0.5, [], ["rst"], lambda e, p: e.memset(T.rst[:], 0.0))
+    V(NK, 0.5, [], ["rst"], lambda e, p: e.memset(T.rst[:, 0:KW:8], 1024.0))
+    G(KW, [], ["oko"], lambda e, p: e.iota(T.oko[:], [[0, NK], [1, 8]], 0, 0, allow_small_or_imprecise_dtypes=True))
+    G(KW, [], ["ook"], lambda e, p: e.iota(T.ook[:], [[1, 8], [0, NK]], 0, 0, allow_small_or_imprecise_dtypes=True))
+    V(NT * PW, 0.5, [], ["key0%d" % t for t in range(NT)], lambda e, p: e.memset(T.keys[:, 0:NT * PW], 0.0))
+    V(NS * NT * PW, 0.5, [], ["payh%d%d" % (s, t) for s in range(NS) for t in range(NT)], lambda e, p: e.memset(T.pay[:], 0.0))
+    G(8, ["ones"], ["g8A"], lambda e, p: e.affine_select(T.g8A[:], T.ones[0:64, 0:8], [[-8, 8]], A.is_ge, 0.0, 0, 1))
+    G(8, ["g8A"], ["g8m"], lambda e, p: e.affine_select(T.g8m[:], T.g8A[:], [[8, 8]], A.is_ge, 0.0, 7, -1))
+    V(144, 0.5, [], ["W8"], lambda e, p: e.memset(T.W8[:], 0.0))
+    V(8, 1, ["g8m"], ["W8"], lambda e, p: e.tensor_scalar(T.W8[:, 15:143:16], T.g8m[:], -8.0, None, A.mult))
+    G(128, ["ones"], ["ident"], lambda e, p: e.affine_select(T.ident[:], T.ones[:], [[-1, 128]], A.is_equal, 0.0, 0, 1))
+    for x in MUL:
+        if x in (3, 5, 7, -8, -16):
+            S(128, 1, ["ident"], [mt(x)], lambda e, p, x=x: e.activation(mI(x), T.ident[:], ACT.Copy, scale=float(x)))
         else:
-            S(n16, 1, ["F" + x], ["F2" + x], lambda e, p: e.activation(F2[:], F[:], ACT.Copy), pr=pr)
-            V(n16, GAT, ["F" + x, "F2" + x, "p16%d" % h], ["D" + x], lambda e, p: e.tensor_tensor(D[:], F2[:].indirect(t("p16")), F[:], A.subtract), pr=pr)
-            S(n16, 1, ["D" + x], ["AD" + x], lambda e, p: e.activation(AD[:], D[:], ACT.Abs), pr=pr)
-        for c in range(2):
-            P(1, 512, ["limT%d" % s, "E", "D" + x], ["%s_%d" % (kA, c)],
-              lambda e, p, c=c: e.matmul(p[:, 512 * c:512 * c + 512], T.limT[:, 256 * s + LH * h:256 * s + LH * h + LH],
-                                         T.E[:, n16 * j + 512 * c:n16 * j + 512 * c + 512], True, True),
-              pr=pr + 0.3, pool=("A", kA), bk=(c,))
-        V(n16, 1, ["AD" + x, kA + "_0", kA + "_1"], ["ni" + x], lambda e, p: e.tensor_tensor(ni[:], AD[:], p[:], A.is_gt), pr=pr, pool=("A", kA), free=1, bk=(0, 1))
+            V(128, 0.5, ["ident"], [mt(x)], lambda e, p, x=x: e.tensor_scalar(mI(x), T.ident[:], float(x), None, A.mult))
+    S(128, 1, ["ident"], ["i5"], lambda e, p: e.activation(T.i5[:], T.ident[:], ACT.Copy, scale=5.0))
+    G(128, ["ones"], ["gA"], lambda e, p: e.affine_select(T.gA[:], T.ones[:], [[-16, 8], [0, 16]], A.is_ge, 0.0, 0, 1))
+    G(128, ["gA"], ["gm"], lambda e, p: e.affine_select(T.gm[:], T.gA[:], [[16, 8], [0, 16]], A.is_ge, 0.0, 15, -1))
+    S(128, 1, ["gm"], ["okw"], lambda e, p: e.activation(T.okw[:], T.gm[:], ACT.Copy, scale=float(OFF // 16)))
+    V(432, 0.5, [], ["W%d" % x for x in WMUL], lambda e, p: e.memset(T.W[:], 0.0))
+    for i, x in enumerate(WMUL):
+        S(8, 1, ["gm"], ["W%d" % x], lambda e, p, i=i, x=x: e.activation(T.W[:, 144 * i + 15:144 * i + 143:16], T.gm[:, 0:128:16], ACT.Copy, scale=float(x)))
+    for buf, (a, b, c, d), val in (("cst", (0, 32, 0, 128), 1 / 32), ("cst", (32, 64, 0, 128), BIG / 64), ("crow", (0, 32, 0, 160), 1.0), ("crow", (32, 64, 0, 160), -15.0),
+                                   ("crow", (32, 64, 64, 128), 2.0)):
+        V(d - c, 0.5, [], ["cst"], lambda e, p, buf=buf, a=a, b=b, c=c, d=d, val=val: e.memset(T[buf][a:b, c:d], val))
+    for (a, b, c, d), val in (((0, 64, 0, 8 * NK), 0.0), ((0, 32, 0, NK), (24 * MAG + 8) / 32), ((0, 32, NK, 2 * NK), 16 * MAG / 32), ((32, 64, NK, 2 * NK), 8 / 32),
+                              ((0, 32, 4 * NK, 7 * NK), 16 / 32)):
+        V(d - c, 0.5, [], ["cz"], lambda e, p, a=a, b=b, c=c, d=d, val=val: e.memset(T.cz[a:b, c:d], val))
+    for h in range(2):
+        V(1024, 0.5, [], ["E%d" % h], lambda e, p, h=h: e.memset(T.E[:, 1024 * h:1024 * h + 1024], 1.0))
+        G(1024, ["E%d" % h], ["E%d" % h], lambda e, p, h=h: e.affine_select(T.E[:, 1024 * h:1024 * h + 1024], T.E[:, 1024 * h:1024 * h + 1024],
+                                                                           [[-1, 64], [0, 16]], A.is_equal, 0.0, -64 * h, 1))
+    G(128, [], ["pm"], lambda e, p: e.iota(T.pm[:], [[-1, 128]], 2048, 1))
+    V(128, 1, ["pm"], ["pm2"], lambda e, p: e.tensor_scalar(T.pm2[:], T.pm[:], 15, None, A.bitwise_and))
+    V(128, 1, ["pm2"], ["same1"], lambda e, p: e.tensor_scalar(T.same[:, 0:128], T.pm2[:], 0.0, None, A.is_equal))
+    V(128, 0.5, ["same1"], ["same8"], lambda e, p: e.tensor_scalar(T.same[:, 128:256], T.same[:, 0:128], 8.0, None, A.mult))
 
-        def adm(e, p):
-            e.matmul(p[:, 0:LB], T.identf[:], t("u5"), True, False)
-            for k in range(16):
-                i = e.matmul(p[:, 0:LB], T.sel1[:, 128 * k:128 * k + 128], AD[:, k:n16:16], False, False)
-            return i
+    V(256, GAT, ["vvi", "vvu", "vperm"], ["vvb"], lambda e, p: e.tensor_copy(T.vvb[:], T.vvi[:].indirect(T.vperm[:])))
+    for o in range(8):
+        if o % 3 == 2:
+            S(256, 1, ["vvb", "omask"], ["R%d" % o], lambda e, p, o=o: e.activation(T.R[:, o:2048:8], T.vvb[0:64, :], ACT.Copy, scale=T.omask[:, o:o + 1]))
+        else:
+            V(256, 0.5, ["vvb", "omask"], ["R%d" % o], lambda e, p, o=o: e.tensor_scalar(T.R[:, o:2048:8], T.vvb[0:64, :], T.omask[:, o:o + 1], None, A.mult))
+    P(16, 128, ["W8"] + ["R%d" % o for o in range(8)], ["vP"],
+      mms([(cols(0, 128), T.W8[:, 15 - b:143 - b], T.R[:, 128 * b:128 * b + 128]) for b in range(16)]), pool=("N", "vP"))
+    for t in range(NT):
+        V(KW, 1, ["vP", "oko"], ["key0%d" % t], lambda e, p, t=t: e.tensor_tensor(kv(0, t, HD, PW), p[:, KW * t:KW * t + KW], T.oko[:], A.add), pool=("N", "vP"), free=NT)
+        w = slice(8 * LT * t, 8 * LT * t + 8 * LT)
+        V(8 * LT, 1, ["pgi%d" % t], ["pgw%d" % t], lambda e, p, w=w: e.tensor_copy(T.pgw[:, w], T.pgi[:, w]))
+        G(8 * LT, [], ["prew%d" % t], lambda e, p, w=w: e.iota(T.prew[:, w], [[0, 16 * LT // CH], [16, CH // 16], [0, 8]], 0, 0, allow_small_or_imprecise_dtypes=True))
+        add("G", 1100, ["prew%d" % t], ["prew%d" % t], lambda e, p, w=w: e.dma_start(T.prew[:, w], T.pre[:, w], accum_op=A.add), sem="lpre%d" % t, inc=16, lat=3500)
 
-        def nim(e, p):
-            for k in range(16):
-                i = e.matmul(p[:, 0:LB], T.sel2[:, 128 * k:128 * k + 128], ni[:, k:n16:16], False, k == 15)
-            return i
-        P(20, LB, ["AD" + x, "u5" + x, "identf", "sel1"], [kP], adm, pr=pr + 0.2, pool=("P", kP))
-        P(16, LB, ["ni" + x, "sel2"], [kP], nim, pr=pr, pool=("P", kP))
-        S(LB, 1, [kP], [sgt], lambda e, p: e.activation(sg, p[:, 0:LB], ACT.Sign, scale=-1.0), pr=pr - .5, pool=("P", kP), free=2)
-        V(LB, 1, [kP, cint], ["qq" + x], lambda e, p: e.tensor_tensor(t("qq"), p[:, 0:LB], cin, A.max), pr=pr - .5, pool=("P", kP), free=2)
+    P(2, 128, ["limb", "ident"], ["lP"], lambda e, p: [e.matmul(p[:, 128 * h:128 * h + 128], T.limb[:, 128 * h:128 * h + 128], T.ident[:], True, True) for h in range(2)][-1],
+      pool=("N", "lP"))
+    S(256, 1, ["lP"], ["limT0"], lambda e, p: e.activation(T.limT[:, 0:256], p[:, 0:256], ACT.Copy), pool=("N", "lP"), free=1)
+    for s in range(1, NS):
+        add("G", 500 + 2000 * (s == 1), ["limT0"], ["sl%d" % s], lambda e, p, s=s: ctx["send"](s, T.limT[:, 256 * s:256 * s + 256], T.limT[:, 0:256], "alim%d" % s), sem="sent", inc=NE, lat=2500)
+        add("W", 0, ["sl%d" % s], ["limT%d" % s], None, sem="alim%d" % s, inc=NE, lat=8000)
 
-        def okm(e, p):
-            e.matmul(p[:, 0:LB], T.identf[:], t("u5"), True, False)
-            return e.matmul(p[:, 0:LB], T.okw[:], sg, False, True)
-        P(5, LB, [sgt, "u5" + x, "okw", "identf"], [kN], okm, pr=pr - .5, pool=("N", kN))
-        V(LB, 1, [kN, "qq" + x], ["cpp" + x], lambda e, p: e.tensor_tensor(t("cpp"), p[:, 0:LB], t("qq"), A.max), pr=pr - .5, pool=("N", kN), free=1)
-        V(LB, 1, ["cpp" + x], ["ci" + x], lambda e, p: e.tensor_scalar(t("ci"), t("cpp"), 4095, None, A.bitwise_and), pr=pr - .5)
-        if not last:
-            V(LB, 1, ["ci" + x], ["c16" + x], lambda e, p: e.tensor_copy(t("c16"), t("ci")), pr=pr - .5)
-            V(LB, 1, ["ci" + x], ["u5" + x], lambda e, p: e.tensor_scalar(t("u5"), t("ci"), 5.0, float(1 - OFF), A.mult, A.add), pr=pr - .4)
+    def begin(s, t):
+        kt, n = "key%d%d" % (s, t), lambda x: "%s%d" % (x, t)
+        ks, eq, lst = T.ks[:, KW * t:KW * t + KW], T.eq[:, KW * t:KW * t + KW], T.lst[:, NK * t:NK * t + NK]
+        w, ln = slice(8 * LT * t, 8 * LT * t + 8 * LT), slice(LT * t, LT * t + LT)
+        us = range(LT * t // LU, (LT * t + LT) // LU)
+        V(KW, 0.5, [kt, "rst"], [n("ks")], lambda e, p: e.tensor_tensor_scan(ks, T.rst[:], kv(s, t, HD, PW), 0.0, A.add, A.min))
+        V(KW, GAT, [kt, n("ks"), "rep7"], [n("eq")], lambda e, p: e.tensor_tensor(eq, ks.indirect(T.rep7[:, 0:KW // 16]), kv(s, t, HD, PW), A.is_equal))
+        P(8, NK, [n("eq"), "lane8"] + [mt(o) for o in range(1, 8)], [n("O")],
+          mms([(cols(0, NK), mI(1), T.lane8[:])] + [(cols(0, NK), mI(o), T.eq[:, KW * t + o:KW * t + KW:8]) for o in range(1, 8)]), pool=("N", n("O")))
+        V(NK, 1, [n("O")], [n("lst")], lambda e, p: e.tensor_copy(lst, p[:, 0:NK]), pool=("N", n("O")), free=1)
+        V(LT, GAT, [n("pgw"), n("lst")], ["c16%d" % u for u in us], lambda e, p: e.tensor_copy(T.c16[:, ln], T.pgw[:, w].indirect(lst)))
+        V(LT, GAT, [n("prew"), n("lst")], [n("p16")], lambda e, p: e.tensor_copy(T.p16[:, ln], T.prew[:, w].indirect(lst)))
+        S(LT, GAT, [n("pgw"), n("lst")], ["cf%d" % u for u in us], lambda e, p: e.activation(T.cf[:, ln], T.pgw[:, w].indirect(lst), ACT.Copy))
 
-    def end(s, h):
-        pr = ST * (s + 1) - 1.0 + 0.5 * h
-        q = H * s + h
-        n = lambda x: "%s%d" % (x, h)
-        t = lambda x: T["%s%d" % (x, h)]
-        kt, gt = "key%d%d" % (s, h), ("gro0%d" % h if s == 0 else "key%d%d" % (s, h))
-        pay = lambda a, b: T.pay[:, KG * q + a:KG * q + b]
-        fx = lambda a, b: T.fx[:, FW * q + a:FW * q + b]
-        kL = "L%d" % h
+    def step(s, st, u):
+        t = u * LU // LT
+        way = [CFG["way"][(NC * (ST * NU * s + CFG["turn"][u][st]) + c) % len(CFG["way"])] for c in range(NC)]
+        ln = slice(LU * u, LU * u + LU)
+        sgc = ST * LT * t + LT * st + LU * u - LT * t
+        sg, sgt = T.sg[:, sgc:sgc + LU], "sg%d%d" % (u, st)
+        kP, kN = "P%d" % u, "N%d" % u
+        n = lambda x: "%s%d" % (x, u)
+        for c in range(NC):
+            chunk(s, st, u, c, way[c])
+        al = lambda x: ["%s%d%d" % (x, u, c) for c in range(NC)]
+        red = lambda x, buf, a=0, z=LU: [(cols(a, z), sel(x, b), buf[:, 16 * (LU * u + a) + b:16 * (LU * u + z):16]) for b in range(16)]
+        base = lambda k: [(cols(0, LU), T.i5[:], T.cf[:, ln]), (cols(0, LU), T.cst[:], T.crow[:, k:k + LU])]
+        k = {(0, 0): 0, (0, 1): 32, (1, 1): 64, (1, 0): 96}[(way[0] in "AT") + 0, (way[-1] in "AT") + 0]
+        rel = [c for c in range(NC) if way[c] in "AC"]
+        if rel:
+            P(21, LU, al("D") + [n("cf"), "i5", "cst", "W-1"], [kP], mms(base(k) + red(-1, T.D, LU // NC * rel[0], LU // NC * (rel[-1] + 1)), True, False), pool=("P", kP))
+            P(16, LU, al("AD") + ["W1"], [kP], mms(red(1, T.AD), False, False), pool=("P", kP))
+        else:
+            P(21, LU, al("AD") + [n("cf"), "i5", "cst", "W1"], [kP], mms(base(k) + red(1, T.AD), True, False), pool=("P", kP))
+        P(16, LU, al("ni") + ["W%d" % BIG], [kP], mms(red(BIG, T.ni), False, True), pool=("P", kP))
+        S(LU, 1, [kP], [sgt], lambda e, p: e.activation(sg, p[:, 0:LU], ACT.Sign, scale=-1.0), pool=("P", kP), free=2)
+        V(LU, 1, [kP, n("cf"), sgt], [n("qq")], lambda e, p: e.tensor_tensor(T.qq[:, ln], p[:, 0:LU], T.cf[:, ln], A.max), pool=("P", kP), free=2)
+        P(5, LU, [n("cf"), "i5", "cst", kP], [kN], mms(base(0), True, False), pool=("N", kN))
+        P(1, LU, [sgt, "okw"], [kN], mms([(cols(0, LU), T.okw[:], sg)], False, True), pool=("N", kN))
+        V(LU, 1, [kN, n("qq")], [n("cpp")], lambda e, p: e.tensor_tensor(T.cpp[:, ln], p[:, 0:LU], T.qq[:, ln], A.max), pool=("N", kN), free=1)
+        V(LU, 1, [n("cpp")], [n("ci")], lambda e, p: e.tensor_scalar(T.ci[:, ln], T.cpp[:, ln], 4095, None, A.bitwise_and))
+        if st < ST - 1:
+            V(LU, 1, [n("ci")], [n("c16")], lambda e, p: e.tensor_copy(T.c16[:, ln], T.ci[:, ln]))
+            V(LU, 1, [n("ci")], [n("cf")], lambda e, p: e.tensor_copy(T.cf[:, ln], T.ci[:, ln]))
 
-        def lpm(e, p):
-            for b in range(16):
-                i = e.matmul(p[:, 0:FW], T.sel1[:, 128 * b:128 * b + 128], t("sg")[:, b:ST * LH:16], b == 0, b == 15)
-            return i
+    def chunk(s, st, u, c, way):
+        t, x = u * LU // LT, NC * u + c
+        a = CH * x
+        n = lambda y: "%s%d%d" % (y, u, c)
+        F, F2, D, AD, ni = (T[y][:, a:a + CH] for y in ("F", "F2", "D", "AD", "ni"))
+        ln = slice(a // 16, (a + CH) // 16)
+        bk, kA, kD = tuple(range(CH // 512)), n("A"), n("B")
+        halves = [(cols(512 * i, 512 * i + 512), slice(a + 512 * i, a + 512 * i + 512)) for i in bk]
 
-        def mpm(e, p):
-            for k in range(ST):
-                i = e.matmul(p[:, 64:64 + NK], T.sameb[:], fx(NK * k, NK * k + NK), k == 0, k == ST - 1)
-            return i
-        P(16, FW, ["sg%d%d%d" % (h, j, k) for j in range(J) for k in range(ST)] + ["sel1"], [kL], lpm, pr=pr, pool=("N", kL))
-        S(FW, 1, [kL], ["fx%d" % q], lambda e, p: e.activation(fx(0, FW), p[:, 0:FW], ACT.Relu, bias=-15.0), pr=pr, pool=("N", kL))
-        S(NK, 1, [kL], [n("nk1")], lambda e, p: e.activation(t("nk1")[:], p[:, FW - NK:FW], ACT.Identity, scale=-512.0, bias=float(1024 * (s + 1) - 8192)), pr=pr, pool=("N", kL))
-        P(3, NK, ["fx%d" % q, "sameb"], [kL], mpm, pr=pr, pool=("N", kL))
-        V(NK, 1, [kL], [n("mi")], lambda e, p: e.tensor_copy(t("mi")[:], p[:, 64:64 + NK]), pr=pr, pool=("N", kL), free=1)
-        V(NK, 1, [n("mi")], [n("od")], lambda e, p: e.tensor_scalar(t("od")[:], t("mi")[:], 1024, None, A.bitwise_and), pr=pr)
-        V(NK, 2, [n("nk1"), n("od")], [n("xx")], lambda e, p: e.tensor_tensor(t("xx")[:], t("nk1")[:], t("od")[:], A.add), pr=pr)
-        V(NK, 2, [n("xx"), n("eb")], [n("dl")], lambda e, p: e.tensor_tensor(t("dl")[:], t("xx")[:], t("eb")[:], A.add), pr=pr)
-        V(NK, 2, [gt, n("od")], ["payg%d" % q], lambda e, p: e.tensor_tensor(pay(KW, KG), kv(s, h, KW, KG), t("od")[:], A.add), pr=pr)
-        V(KW, GAT, [n("dl"), n("eq"), "rep"], [n("em")], lambda e, p: e.tensor_tensor(t("em")[:], t("dl")[:].indirect(T.rep[:]), t("eq")[:], A.mult), pr=pr)
-        V(KW, 2, [kt, n("em")], ["pay%d" % q], lambda e, p: e.tensor_tensor(pay(0, KW), kv(s, h, 0, KW), t("em")[:], A.add), pr=pr)
-        add("G", 500, ["pay%d" % q, "payg%d" % q], ["snd%d" % q], lambda e, p: ctx["send"](1, kv(s + 1, h, 0, KG), pay(0, KG), "akey%d%d" % (s + 1, h)), pr=pr - 2, sem="sent", inc=NE, lat=2000)
-        add("W", 0, ["snd%d" % q], ["key%d%d" % (s + 1, h)], None, sem="akey%d%d" % (s + 1, h), inc=NE, lat=600)
-        if s:
-            add("G", 500, ["fx%d" % q], ["sndf%d" % q], lambda e, p: ctx["send"](-s, T.fl[:, FW * q:FW * q + FW], fx(0, FW), "afl%d" % q), pr=pr, sem="sent", inc=NE, lat=2000)
-            add("W", 0, ["sndf%d" % q], ["fl%d" % q], None, sem="afl%d" % q, inc=NE, lat=600)
-        V(LH, 3.5, [n("lst")] + ["ci%d%d" % (h, j) for j in range(J)], [n("pgw")], lambda e, p: e.tensor_copy(t("pgw")[:].indirect(t("lst")[:]), t("ci")[:]), pr=pr + .05)
+        def stream(x, buf, start, stop):
+            return lambda e, p: [e.matmul(p[o], x, buf(w), start, stop) for o, w in halves][-1]
+        S(CH, GAT, ["X", "c16%d" % u], [n("F")], lambda e, p: e.activation(F, T.X[:].indirect(T.c16[:, ln]), ACT.Copy), due=at[0] + c * CH * GAT * CYC)
+        if way == "P":
+            V(CH, GAT, [n("F"), "p16%d" % t], [n("D")], lambda e, p: e.tensor_copy(D, F.indirect(T.p16[:, ln])))
+            P(len(bk), 512, [n("F"), "ident"], [kD], stream(mI(1), lambda w: T.F[:, w], True, False), pool=("A", kD), bk=bk)
+            P(len(bk), 512, [n("D"), mt(-1)], [kD], stream(mI(-1), lambda w: T.D[:, w], False, True), pool=("A", kD), bk=bk)
+            S(CH, 1, [kD], [n("AD")], lambda e, p: e.activation(AD, p[:], ACT.Abs), pool=("A", kD), free=1, bk=bk)
+        else:
+            how = CFG["copy"][(x + (ST * s + st) * NU * NC) % len(CFG["copy"])]
+            if how == "Q":
+                add("Q", 60, [n("F")], [n("F2")], lambda e, p: e.dma_start(F2, F), sem="cp%d" % x, inc=16, lat=CFG["dma"] * (0.7 + 0.3 * CH / 512))
+            elif how == "G":
+                G(CH, [n("F")], [n("F2")], lambda e, p: e.affine_select(F2, F, [[0, CH]], A.is_ge, 0.0, 0, 0))
+            elif how == "V":
+                V(CH, 0.5, [n("F")], [n("F2")], lambda e, p: e.tensor_copy(F2, F))
+            else:
+                S(CH, 1, [n("F")], [n("F2")], lambda e, p: e.activation(F2, F, ACT.Copy))
+            V(CH, GAT, [n("F"), n("F2"), "p16%d" % t], [n("D")], lambda e, p: e.tensor_tensor(D, F2.indirect(T.p16[:, ln]), F, A.subtract))
+            if way in "AC":
+                V(CH, 0.5, [n("D")], [n("AD")], lambda e, p: e.tensor_scalar(AD, D, 0.0, 2.0, A.max, A.mult))
+            else:
+                S(CH, 1, [n("D")], [n("AD")], lambda e, p: e.activation(AD, D, ACT.Abs))
+        lim = T.limT[:, 256 * s + 128 * (u // 2):256 * s + 128 * (u // 2) + 128]
+        P(len(bk), 512, ["limT%d" % s, "E%d" % (u % 2), n("D")], [kA], stream(lim, lambda w: T.E[:, w.start % 2048:w.start % 2048 + 512], True, way in "BP"), pool=("A", kA), bk=bk)
+        if way in "AC":
+            P(len(bk), 512, [n("D"), "ident"], [kA], stream(mI(1), lambda w: T.D[:, w], False, False), pool=("A", kA), bk=bk)
+        if way in "ACT":
+            P(len(bk), 512, [n("AD"), mt(-1)], [kA], stream(mI(-1), lambda w: T.AD[:, w], False, True), pool=("A", kA), bk=bk)
+        if way in "BP":
+            V(CH, 1, [n("AD"), kA], [n("ni")], lambda e, p: e.tensor_tensor(ni, AD, p[:], A.is_gt), pool=("A", kA), free=1, bk=bk)
+        elif way == "C":
+            V(CH, 1, [kA], [n("ni")], lambda e, p: e.tensor_scalar(ni, p[:], 0.0, None, A.is_lt), pool=("A", kA), free=1, bk=bk)
+        else:
+            S(CH, 1, [kA], [n("ni")], lambda e, p: e.activation(ni, p[:], ACT.Sign, scale=-1.0, bias=-0.5), pool=("A", kA), free=1, bk=bk)
 
-    def final(h):
-        pr = ST * NS + 0.5 * h
-        n = lambda x: "%s%d" % (x, h)
-        t = lambda x: T["%s%d" % (x, h)]
-        kt = "key%d%d" % (NS, h)
-        add("Q", 80, [n("pgw")], [], lambda e, p: e.dma_start(T.yg[:, 1024 * h:1024 * h + 1024], t("pgw")[:]), pr=pr, sem="outs", inc=16, lat=4000)
-        V(KW, 2, [kt, "keyc"], [n("hi")], lambda e, p: e.tensor_tensor(t("hi")[:], kv(NS, h, 0, KW), T.keyc[:], A.subtract), pr=pr - 3)
-        V(KW, GAT, [kt, n("hi"), "rep"], [n("fv")], lambda e, p: e.tensor_tensor(t("fv")[:], kv(NS, h, KW, KG).indirect(T.rep[:]), t("hi")[:], A.subtract), pr=pr - 3)
-        for c in range(2):
-            def fvm(e, p, c=c):
-                for b in range(16):
-                    i = e.matmul(p[0:8, 512 * c + b:512 * c + 512:16], T.fsel[:, 8 * b:8 * b + 8], t("fv")[:, 32 * c:32 * c + 32], True, True)
-                return i
-            P(16, 32, [n("fv"), "fsel"], ["Y%d_%d" % (h, c)], fvm, pr=pr - 3, pool=("A", "Y%d" % h), bk=(c,))
-        V(512, 1, ["Y%d_0" % h], ["yvsA%d" % h], lambda e, p: e.tensor_scalar(t("yvs")[:, 0:512], p[0:8, 0:512], float(NS), None, A.add), pr=pr - 3, pool=("A", "Y%d" % h), free=2)
-        S(512, 1, ["Y%d_1" % h], ["yvsB%d" % h], lambda e, p: e.activation(t("yvs")[:, 512:1024], p[0:8, 512:1024], ACT.Identity, bias=float(NS)), pr=pr - 3, pool=("A", "Y%d" % h), free=2, bk=(1,))
-        add("Q", 80, ["yvsA%d" % h, "yvsB%d" % h], [], lambda e, p: e.dma_start(T.yv[:, LH * h:LH * h + LH], t("yvs")[:]), pr=pr - 3, sem="outs", inc=16, lat=2200)
-        kM = "M%d" % h
+    def end(s, t):
+        n, q = lambda x: "%s%d" % (x, t), "%d%d" % (s, t)
+        kt = "key" + q
+        us = range(LT * t // LU, (LT * t + LT) // LU)
+        pay = lambda a, b: T.pay[:, PW * (NT * s + t) + a:PW * (NT * s + t) + b]
+        fx = lambda k: T.fx[:, NK * (ST * t + k):NK * (ST * t + k + 1)]
+        hn = lambda k: T.hn[:, NK * (2 * t + k):NK * (2 * t + k + 1)]
+        eq, tt, lst = T.eq[:, KW * t:KW * t + KW], T.tt[:, KW * t:KW * t + KW], T.lst[:, NK * t:NK * t + NK]
+        kL, kZ = n("L"), n("Z")
+        d, g8, mc = cols(0, NK), cols(NK, 2 * NK), cols(2 * NK, 3 * NK)
+        P(17, ST * NK, ["sg%d%d" % (u, k) for u in us for k in range(ST)] + ["W1", "cz", "ones"], [kL],
+          mms([(cols(0, ST * NK), T.ones[0:64, :], T.cz[:, 4 * NK:7 * NK])] +
+              [(cols(0, ST * NK), sel(1, b), T.sg[:, ST * LT * t + b:ST * LT * (t + 1):16]) for b in range(16)]), pool=("N", kL))
+        P(11, NK, [kL, kt, n("ks"), n("eq"), "cz", "ones"] + [mt(o) for o in (1, 2, 3, 4, 5, 6, 7, -1)], [kZ],
+          mms([(cols(0, 3 * NK), T.ones[0:64, :], T.cz[:, 0:3 * NK]), (d, mI(1), kv(s, t, NK, 2 * NK)), (cols(NK, 3 * NK), mI(1), kv(s, t, NK, 3 * NK)),
+               (d, mI(-1), T.ks[:, KW * t + 7:KW * t + KW:8])] + [(d, mI(o), T.eq[:, KW * t + o:KW * t + KW:8]) for o in range(1, 8)], True, False), pool=("N", kZ))
+        S(ST * NK, 1, [kL], [n("fx")], lambda e, p: e.activation(T.fx[:, ST * NK * t:ST * NK * (t + 1)], p[:, 0:ST * NK], ACT.Relu, bias=-31.0), pool=("N", kL))
+        P(3, NK, [n("fx"), "same1"], [kL], mms([(cols(ST * NK, (ST + 1) * NK), T.same[:, 0:128], fx(k)) for k in range(ST)]), pool=("N", kL))
+        P(9, NK, [n("fx"), "same8", "ident", kL], [kZ], mms([(o, l, fx(k)) for k in range(ST) for o, l in ((d, T.same[:, 128:256]), (g8, T.same[:, 128:256]), (mc, mI(1)))], False, False),
+          pool=("N", kZ))
+        S(2 * NK, 1, [kL], [n("hn")], lambda e, p: e.activation(T.hn[:, 2 * NK * t:2 * NK * (t + 1)], p[:, (ST - 1) * NK:(ST + 1) * NK], ACT.Identity, scale=0.5, bias=MAG - 0.25),
+          pool=("N", kL), free=1)
+        P(3, NK, [n("hn"), mt(-8), mt(-16)], [kZ], mms([(d, mI(-8), hn(0)), (d, mI(-16), hn(1)), (g8, mI(-16), hn(1))], False, True), pool=("N", kZ))
+        V(3 * NK, 1, [kZ], ["payh" + q], lambda e, p: e.tensor_copy(pay(0, 3 * NK), p[:, 0:3 * NK]), pool=("N", kZ), free=1)
+        V(KW, GAT, ["payh" + q, n("eq"), "repk"], [n("tt")], lambda e, p: e.tensor_tensor(tt, pay(0, HD).indirect(T.repk[:, 0:KW // 16]), eq, A.mult))
+        V(KW, 2, [kt, n("tt")], ["pay" + q], lambda e, p: e.tensor_tensor(pay(HD, PW), kv(s, t, HD, PW), tt, A.add))
+        add("G", 500, ["pay" + q, "payh" + q], ["snd" + q], lambda e, p: ctx["send"](1, kv(s + 1, t, 0, PW), pay(0, PW), "akey%d%d" % (s + 1, t)), sem="sent", inc=NE, lat=CFG["send"] - 500)
+        add("W", 0, ["snd" + q], ["key%d%d" % (s + 1, t)], None, sem="akey%d%d" % (s + 1, t), inc=NE)
+        V(LT, 3.5, [n("lst")] + ["ci%d" % u for u in us], [n("pgw")],
+          lambda e, p: e.tensor_copy(T.pgw[:, 8 * LT * t:8 * LT * (t + 1)].indirect(lst), T.ci[:, LT * t:LT * t + LT]))
 
-        def ysum(e, p):
-            for i in range(NS):
-                for k in range(ST):
-                    c = FW * (H * i + h) + NK * k
-                    r = e.matmul(p[:, 0:NK], T.identb[:], (T.fl if i else T.fx)[:, c:c + NK], i + k == 0, i == NS - 1 and k == ST - 1)
-            return r
+    def final(t):
+        n, kt = lambda x: "%s%d" % (x, t), "key%d%d" % (NS, t)
+        fa, fv = T.fa[:, KW * t:KW * t + KW], T.fv[:, KW * t:KW * t + KW]
+        w = slice(8 * LT * t, 8 * LT * (t + 1))
+        add("Q", 60, [n("pgw")], [], lambda e, p: e.dma_start(T.yg[:, w], T.pgw[:, w]), sem="outs", inc=16, lat=3000)
+        V(KW, GAT, [kt, "ook", "perm"], [n("fa")], lambda e, p: e.tensor_tensor(fa, kv(NS, t, HD, PW).indirect(T.turn8[:, 0:KW // 16]), T.ook[:], A.subtract))
+        V(KW, GAT, [kt, n("fa"), "repg"], [n("fv")], lambda e, p: e.tensor_tensor(fv, kv(NS, t, 0, HD).indirect(T.repg[:, 0:KW // 16]), fa, A.subtract))
+        for c in range(KW // 32):
+            k = "Y%d%d" % (t, c)
+            P(8, 64, [n("fv"), "ident"], [k], lambda e, p, c=c: [e.matmul(p[0:8, b:512:16], T.ident[:, b:128:16], T.fv[:, KW * t + 32 * c:KW * t + 32 * c + 32], True, True)
+                                                               for b in range(16)][-1], pool=("P", k))
+            y = T.yvs[:, 8 * LT * t + 512 * c:8 * LT * t + 512 * c + 512]
+            if (t + c) % 2:
+                V(512, 1, [k], ["yv%d%d" % (t, c)], lambda e, p, y=y: e.tensor_scalar(y, p[0:8, :], 0.125, None, A.mult), pool=("P", k), free=1)
+            else:
+                S(512, 1, [k], ["yv%d%d" % (t, c)], lambda e, p, y=y: e.activation(y, p[0:8, :], ACT.Copy, scale=0.125), pool=("P", k), free=1)
+        add("Q", 60, ["yv%d%d" % (t, c) for c in range(KW // 32)], [], lambda e, p: e.dma_start(T.yv[:, LT * t:LT * t + LT], T.yvs[:, w]), sem="outs", inc=16, lat=2200)
+        P(4, 64, [kt, "ident"], [n("M")], lambda e, p: [e.matmul(p[0:8, b:LT:16], T.ident[:, b:128:16], kv(NS, t, 2 * NK, 3 * NK), True, True) for b in range(16)][-1], pool=("N", n("M")))
+        S(LT, 1, [n("M")], [n("ym")], lambda e, p: e.activation(T.yms[:, LT * t:LT * t + LT], p[0:8, 0:LT], ACT.Copy), pool=("N", n("M")), free=1)
 
-        def ymm(e, p):
-            for b in range(16):
-                r = e.matmul(p[0:8, 128 + b:256:16], T.fsel1[:, 8 * b:8 * b + 8], t("yb")[:], True, True)
-            return r
-        P(12, NK, ["fx%d" % h, "identb"] + ["fl%d" % (H * s + h) for s in range(1, NS)], [kM], ysum, pr=pr - 2, pool=("N", kM))
-        S(NK, 1, [kM], [n("yb")], lambda e, p: e.activation(t("yb")[:], p[:, 0:NK], ACT.Copy), pr=pr - 2, pool=("N", kM))
-        P(16, NK, [n("yb"), "fsel1"], [kM], ymm, pr=pr - 2, pool=("N", kM))
-        S(LH, 1, [kM], [n("yms")], lambda e, p: e.activation(t("yms")[:], p[0:8, 128:256], ACT.Copy), pr=pr - 2, pool=("N", kM), free=1)
-        add("Q", 80, [n("yms")], [], lambda e, p: e.dma_start(T.ym[:, LH * h:LH * h + LH], t("yms")[:]), pr=pr - 2, sem="outs", inc=16, lat=2200)
+    def due(s, st, u):
+        return CFG["t0"] + CFG["slot"] * (ST * NU * s + CFG["turn"][u][st])
 
     for s in range(NS):
-        for h in range(H):
-            begin(s, h)
+        for t in range(NT):
+            u0 = LT * t // LU
+            begin(s, t)
             for st in range(ST):
-                for j in range(J):
-                    step(s, st, h, j)
-            end(s, h)
-    for h in range(H):
-        final(h)
+                for u in range(u0, u0 + LT // LU):
+                    at[0] = due(s, st, u)
+                    step(s, st, u)
+            end(s, t)
+    for t in range(NT):
+        final(t)
+    add("Q", 60, ["ym%d" % t for t in range(NT)], [], lambda e, p: e.dma_start(T.ym[:], T.yms[:]), sem="outs", inc=16, lat=2200)
     return ops
-
-
-POOLS = {"A": ("PA0", "PA1"), "P": ("PP0", "PP1"), "N": ("PN0", "PN1")}
-WAKE = 100.0
-LS, LB0 = 0.0, 0.0
 
 
 def deps_of(ops, order):
@@ -350,26 +374,31 @@ def deps_of(ops, order):
 
 
 def plan(ops):
-    n = len(ops)
+    n, wake = len(ops), CFG["wake"]
     dep = deps_of(ops, range(n))
     succ = [[] for _ in range(n)]
     need = [len(dep[i]) for i in range(n)]
     for i in range(n):
         for d in dep[i]:
             succ[d].append(i)
+    pr = [0.0] * n
+    for i in reversed(range(n)):
+        pr[i] = min(ops[i]["due"], min([pr[x] for x in succ[i]] + [CFG["end"]]) - ops[i]["cost"] - ops[i]["lat"] - wake)
+    es = [0.0] * n
+    for i in range(n):
+        es[i] = ops[i]["due"] if ops[i]["due"] < 1e8 else max([es[d] + ops[d]["cost"] + ops[d]["lat"] + wake for d in dep[i]] + [0.0])
+    pr = [pr[i] if pr[i] < CFG["t0"] else pr[i] + CFG["mix"] * min(0.0, max(es[i] - pr[i], -CFG["cap"])) for i in range(n)]
     done, start, buf = [0.0] * n, [0.0] * n, {}
     free = {e: 0.0 for e in "VSPGQW"}
     slot = {k: [0.0] * len(v) for k, v in POOLS.items()}
     held, fin = {}, {}
     ready = [i for i in range(n) if not need[i]]
-    order = []
+    can, order = [o["due"] - CFG["hold"] if o["due"] < 1e8 else 0.0 for o in ops], []
     while ready:
         best = {}
         for i in ready:
             o = ops[i]
-            t = free[o["eng"]] if o["eng"] != "W" else 0.0
-            for d in dep[i]:
-                t = max(t, done[d] + (0.0 if o["eng"] == "W" or ops[d]["eng"] == "P" and o["eng"] == "P" else WAKE))
+            t = max(can[i], free[o["eng"]] if o["eng"] != "W" else 0.0)
             if o["pool"] and o["pool"] not in held:
                 fr = [x for x in slot[o["pool"][0]] if x is not None]
                 if not fr:
@@ -378,8 +407,8 @@ def plan(ops):
             best.setdefault(o["eng"], []).append((t, i))
         cand = None
         for e, lst in best.items():
-            t0 = min(lst)[0] + LB0
-            pick = min((ops[i]["pr"], t, i) for t, i in lst if t <= t0 + (LS if ops[i]["cost"] < 260 else 0))
+            t0 = min(lst)[0]
+            pick = min((pr[i], t, i) for t, i in lst if t <= t0 + CFG["look"])
             if cand is None or pick[1] < cand[0]:
                 cand = (pick[1], pick[2])
         t, i = cand
@@ -388,21 +417,21 @@ def plan(ops):
         if o["pool"]:
             k = o["pool"]
             if k not in held:
-                fr = [(x, y) for y, x in enumerate(slot[k[0]]) if x is not None]
-                held[k] = min(fr)[1]
+                held[k] = min((x, y) for y, x in enumerate(slot[k[0]]) if x is not None)[1]
                 slot[k[0]][held[k]] = None
             buf[i] = POOLS[k[0]][held[k]]
         start[i] = t
         done[i] = t + o["cost"] + o["lat"]
         free[o["eng"]] = t + o["cost"]
         if o["pool"] and o["free"]:
-            ends = fin.setdefault(o["pool"], []) + [done[i] + WAKE]
+            ends = fin.setdefault(o["pool"], []) + [done[i] + wake]
             fin[o["pool"]] = ends
             if len(ends) == o["free"]:
                 slot[o["pool"][0]][held.pop(o["pool"])] = max(fin.pop(o["pool"]))
         order.append(i)
         for x in succ[i]:
             need[x] -= 1
+            can[x] = max(can[x], done[i] + (0.0 if ops[x]["eng"] == "W" or o["eng"] == ops[x]["eng"] == "P" else wake))
             if not need[x]:
                 ready.append(x)
     assert len(order) == n
@@ -463,6 +492,6 @@ def rank_program(g, core, T, topo):
         return g.remote_dma(out, inp, T.sem[sem], T.sem["sent"], pid, rid, topo.mask(core, dst))
 
     ne = len(topo.engines(core, cores[(rank + 1) % len(cores)]))
-    ops = graph({"T": T, "send": send, "X": ne})
+    ops = graph({"T": T, "send": send, "NE": ne})
     order, buf, start, done = plan(ops)
     emit(g, T, ops, order, buf)

@@ -7,24 +7,37 @@ BIG = 65536
 OFF = 491520
 MAG = 129
 
-CFG = dict(LT=64, CH=512, way="BBBBBT", copy="G", look=0.0, banks=(3, 2, 3), t0=7500.0, slot=3200.0, hold=1e9, mix=1.0, cap=5000.0,
-           turn=((0, 3, 7), (2, 5, 9), (4, 8, 11), (6, 10, 13)), end=181400.0,
-           gat=1.5, wake=100.0, dma=2300.0, send=2600.0)
+CFG = dict(LT=64, CH=512, way="TBBB", copy="G", look={"V": 30}, cutS=2, sg="S", shift=(0,) * 12, idle={}, gap=0.0, tol=30.0, fE="S", one=0, ld=0.72, fillS=("cst", "crow", "cz"), mV=(2, 4, 6, -1), rS=3, cf="V", pgw="VVVV", eV=4, rush=0, rush0=0, rushc="VV", banks=(3, 2, 3), t0=7500.0, slot=3300.0, hold=1e9, mix=0.85, cap=5000.0,
+           seq="ABCABDACBDCADBACBDACBDCADBACBDACBDCADBACBDACDBCD", tail=11000.0, early=1000.0, ygw=0, head="V",
+           bias={"pgw": 1200, "ks": 2500, "cpp": 600, "N": -300, "ni": -300},
+           cutF="22", cutC="22", cutD="22", cutA="22", cutN="22", Ldep="D",
+           loads="pg0 xt pre0 pg1 lim pre1 pg2 pre2 pg3 pre3",
+           gat=1.5, wake=80.0, dma=2300.0, send=2600.0)
+CFG.update({'wake': 100.0, 'gat': 1.45, 'slot': 3300, 'bias': {'Z': -300, 'A': -300}, 'look': {}, 'way': 'TBBB', 'sg': 'V', 'head': 'S', 'banks': (8, 0, 0), 'one': 1, 'eV': 4,
+            'early': 0, 'tail': 9000, 'loads': 'pg0 lim xt pre0 pg1 pre1 pg2 pre2 pg3 pre3', 'fillS': (), 'cf': 'V'})
+CFG.update({'vfix': 20, 'sfix': 30, 'wake': 160.0, 'idle': {'V': 0.3, 'S': 0.3, 'P': 0, 'G': 1.5}, 'cutC': '211', 'cutD': '211', 'cutA': '211', 'cutN': '211',
+            'bias': {'pay': -1200, 'snd': -2500, 'fx': -2500, 'cf': 2500, 'tt': 600}, 'shift': [0, 0, 0, 0, -0.25, 0, 0, 0, 0, 0, 0, 0], 'eV': 2, 'mV': (2, 4, 6), 'fillS': ('cz',), 'tail': 11000})
+CFG.update(dup=4, cutN="22", way="B", loads="lim pg0 xt pre0 pg1 pre1 pg2 pre2 pg3 pre3", cutQ=1, limw=1, limt=4000.0)
+CFG.update({'dup': 8, 'cutN': '22', 'cutC': '22', 'cutD': '22', 'cutA': '22', 'copy': 'RGGGGG', 'bias': {'ks': -600, 'cf': -300, 'Z': -900, 'p': -300, 'pgw': 2500}, 'idle': {'P': 0.8},
+            'shift': [0, 0, -0.25, 0, 0.5, 0, 0, 0, 0, 0, 0, 0], 'rS': 2, 'gat': 1.4, 'tol': 80, 'limw': 0, 'vfix': 20, 'loads': 'pg0 lim xt pre0 pg1 pre1 pg2 pre2 pg3 pre3'})
 LT, CH = CFG["LT"], CFG["CH"]
 NT, NK, NC = NL // LT, LT // 16, 16 * LU // CH
 KW = 8 * NK
 HD = 16 * (-(-3 * NK // 16))
 PW = HD + KW
 LG = NK.bit_length() - 1
+TURN = [[i for i, x in enumerate(CFG["seq"]) if x == "ABCD"[u]] for u in range(NU)]
+END = CFG["t0"] + CFG["slot"] * (len(CFG["seq"]) - 1) + CFG["tail"]
 
 B16, F32, I32, U16 = "bfloat16", "float32", "int32", "uint16"
 SCRATCH = {}
 for _n, _p, _w, _d in (
-        ("X", 128, 4096, B16), ("pgi", 128, 2048, I32), ("pgw", 128, 2048, F32), ("prew", 128, 2048, F32), ("E", 128, 2048, B16),
-        ("vvi", 128, 256, I32), ("vvb", 128, 256, B16), ("R", 64, 2048, B16), ("limb", 128, 256, B16), ("limT", 128, NS * 256, B16),
-        ("ones", 128, 128, B16), ("ident", 128, 128, B16), ("mI", 128, 128 * 10, B16), ("i5", 128, 128, F32),
+        ("X", 128, 4096, B16), ("pgi", 128, 2048, I32), ("pgw", 128, 2048, F32), ("prew", 128, 2048, F32),
+        ("preb", 128, 2048, B16), ("loff", 32, 512, B16),
+        ("vvi", 128, 256, I32), ("vvb", 128, 256, B16), ("R", 64, 2048, B16), ("limS", 128, NS * 256, B16),
+        ("ones", 128, 128, B16), ("wide", 128, 224, B16), ("ident", 128, 128, B16), ("mI", 128, 128 * 10, B16), ("i5", 128, 128, F32),
         ("gA", 128, 128, B16), ("gm", 128, 128, B16), ("okw", 128, 128, B16), ("W", 128, 3 * 144, B16),
-        ("g8A", 64, 8, B16), ("g8m", 64, 8, B16), ("W8", 64, 144, B16), ("cst", 64, 128, B16), ("crow", 64, 160, B16), ("cz", 64, 8 * NK, B16),
+        ("g8A", 64, 8, B16), ("g8m", 64, 8, B16), ("W8", 64, 144, B16), ("cst", 64, 128, B16), ("crow", 64, 224, B16), ("cz", 64, 8 * NK, B16),
         ("pm", 128, 128, I32), ("pm2", 128, 128, I32), ("same", 128, 256, B16),
         ("om", 64, 8, I32), ("om2", 64, 8, I32), ("omask", 64, 8, F32),
         ("vp", 128, 16, I32), ("vp2", 128, 16, I32), ("vperm", 128, 16, U16),
@@ -36,35 +49,43 @@ for _n, _p, _w, _d in (
         ("fx", 128, NT * ST * NK, B16), ("hn", 128, NT * 2 * NK, B16), ("sg", 128, ST * NL, B16),
         ("fa", 128, NT * KW, B16), ("fv", 128, NT * KW, B16), ("yvs", 8, 8 * NL, F32), ("yms", 8, NL, F32),
         ("c16", 128, NL, U16), ("p16", 128, NL, U16), ("cf", 128, NL, F32), ("ci", 128, NL, I32), ("cpp", 128, NL, I32), ("qq", 128, NL, F32),
-        ("F", 128, 16 * NL, B16), ("F2", 128, 16 * NL, B16), ("D", 128, 16 * NL, B16), ("AD", 128, 16 * NL, B16), ("ni", 128, 16 * NL, B16)):
+        ("F", 128, 16 * NL, B16), ("F2", 128, 16 * NL, B16), ("D", 128, 16 * NL, B16)):
     SCRATCH[_n] = ("sbuf", [_p, _w], _d)
+DUP = CFG["dup"]
+LB = 512 // DUP
+for _n in ("AD", "ni"):
+    SCRATCH[_n] = ("sbuf", [128, NL, 16], B16)
+for _i in range(NL // LB):
+    SCRATCH["LP%d" % _i] = ("psum", [128, LB, DUP], F32)
 POOLS = {}
-for _k, _n, _w in zip("APN", CFG["banks"], (CH, 512, 512)):
+for _k, _n, _w in zip("APN", (8 - NL // LB, 0, 0), (CH, 512, 512)):
     POOLS[_k] = ["P%s%d" % (_k, _i) for _i in range(_n)]
     for _b in POOLS[_k]:
         SCRATCH[_b] = ("psum", [128, _w], F32)
 
 SEMAPHORES = ["cV", "cS", "cP", "cG", "lvv", "llim", "lxt", "outs", "sent"]
-SEMAPHORES += ["lpg%d" % t for t in range(NT)] + ["lpre%d" % t for t in range(NT)] + ["cp%d" % x for x in range(NU * NC)]
+SEMAPHORES += ["lpg%d" % t for t in range(NT)] + ["lpre%d" % t for t in range(NT)] + ["cp%d" % x for x in range(NU * 4) if "Q" in CFG["copy"]]
 SEMAPHORES += ["alim%d" % s for s in range(1, NS)] + ["akey%d%d" % (s, t) for s in range(1, NS + 1) for t in range(NT)]
 
 CYC, PEC = 0.83, 0.42
-VFIX, SFIX = 55, 70
+VFIX, SFIX = CFG.get("vfix", 5), CFG.get("sfix", 10)
 
 
 def graph(ctx):
     T, A, NE = ctx["T"], AluOpType, ctx["NE"]
     GAT = CFG["gat"]
-    ops, at = [], [0.0]
+    ops, at = [], [0.0, END]
 
-    def add(eng, cost, rd, wr, fn, pool=None, free=None, sem=None, inc=None, lat=0.0, bk=(0,), due=1e9):
-        ops.append(dict(eng=eng, cost=cost, rd=rd, wr=wr, fn=fn, due=due, pool=pool, free=free, sem=sem, inc=inc, lat=lat, bk=bk))
+    def add(eng, cost, rd, wr, fn, pool=None, free=None, sem=None, inc=None, lat=0.0, bk=(0,), due=1e9, fix=None):
+        if pool:
+            pool = ("A", pool[0] + pool[1])
+        ops.append(dict(fix=fix, eng=eng, cost=cost, rd=rd, wr=wr, fn=fn, due=due, end=at[1], pool=pool, free=free, sem=sem, inc=inc, lat=lat, bk=bk))
 
     def V(n, cyc, rd, wr, fn, **k):
-        add("V", VFIX + max(64, n * cyc) * CYC, rd, wr, fn, **k)
+        add("V", 50 + n * cyc * CYC if cyc in (GAT, 3.5) and VFIX < 50 else VFIX + max(64, n * cyc) * CYC, rd, wr, fn, **k)
 
     def S(n, cyc, rd, wr, fn, **k):
-        add("S", SFIX + max(64, n * cyc) * CYC, rd, wr, fn, **k)
+        add("S", 65 + n * cyc * CYC if cyc == GAT and VFIX < 50 else SFIX + max(64, n * cyc) * CYC, rd, wr, fn, **k)
 
     def P(k, n, rd, wr, fn, **kw):
         add("P", k * max(64, n) * PEC, rd, wr, fn, **kw)
@@ -101,15 +122,25 @@ def graph(ctx):
         return T.W[:, 144 * WMUL.index(x) + 15 - b:144 * WMUL.index(x) + 143 - b]
 
     load("Q", T.vvi[0:64, :], T.vv[:], "vvi", "lvv", 2000)
-    load("Q", T.limb[:], T.lim[:], "limb", "llim", 2600)
-    load("Q", T.pgi[:, 0:8 * LT], T.pg[:, 0:8 * LT], "pgi0", "lpg0", 2600 + 20 * LT)
-    load("Q", T.X[:], T.xt[:], "X", "lxt", 6300 + 20 * LT)
-    for t in range(1, NT):
-        load("Q", T.pgi[:, 8 * LT * t:8 * LT * t + 8 * LT], T.pg[:, 8 * LT * t:8 * LT * t + 8 * LT], "pgi%d" % t, "lpg%d" % t, 8000 + 40 * LT * t)
+    lat = 1800
+    for x in CFG["loads"].split():
+        w = slice(8 * LT * int(x[-1]), 8 * LT * int(x[-1]) + 8 * LT) if x[-1].isdigit() else None
+        out, inp, dt = {"pg": (T.pgi, T.pg, 1200), "pr": (T.preb, T.pre, 800), "li": (T.limS, T.lim, 600), "xt": (T.X, T.xt, 3700)}[x[:2]]
+        lat += dt * CFG["ld"]
+        load("Q", out[:, w] if w else out[:, 0:inp.shape[1]], inp[:, w] if w else inp[:], {"pg": "pgi", "pr": "preb", "li": "lim0", "xt": "X"}[x[:2]] + (x[-1] if w else ""), "l" + x, lat)
 
     bits = (("p1", A.bitwise_and, 8, None, None), ("p1", A.logical_shift_right, 3, A.bitwise_and, 1), ("p8", A.bitwise_and, 127, None, None),
             ("p8", A.bitwise_and, 8 * NK - 8, None, None), ("p1", A.bitwise_and, 15, A.logical_shift_right, LG), ("p1", A.bitwise_and, NK - 1, None, None))
+    def fill(buf, tile, a, b, c, d, step, val):
+        m, tiles = len(range(c, d, step)), [tile] if isinstance(tile, str) else tile
+        if buf in CFG["fillS"]:
+            S(m, 1, ["wide"], tiles, lambda e, p: e.activation(T[buf][a:b, c:d:step], T.wide[a:b, 0:m], ACT.Copy, scale=val))
+        else:
+            V(m, 0.5, [], tiles, lambda e, p: e.memset(T[buf][a:b, c:d:step], val))
+
     V(128, 0.5, [], ["ones"], lambda e, p: e.memset(T.ones[:], 1.0))
+    if CFG["fillS"]:
+        V(224, 0.5, [], ["wide"], lambda e, p: e.memset(T.wide[:], 1.0))
     V(256, 1, [], ["vvu"], lambda e, p: e.memset(T.vvi[64:128, :], 0))
     G(16, [], ["vp"], lambda e, p: e.iota(T.vp[:], [[1, 16]], 0, 16))
     V(16, 1, ["vp"], ["vp2"], lambda e, p: e.tensor_scalar(T.vp2[:], T.vp[:], 255, None, A.bitwise_and))
@@ -133,19 +164,18 @@ def graph(ctx):
     V(8, 1, ["cc", "bfb"], ["pa"], lambda e, p: e.tensor_scalar(T.pa[:], T.cc[:], float(16 // NK), T.bf[:, 3:4], A.mult, A.add))
     V(8, 1, ["pa", "bfb"], ["perm"], lambda e, p: e.tensor_scalar(T.turn8[:], T.pa[:], T.bf[:, 4:5], None, A.add))
     V(8, 1, ["cc", "bfg"], ["repg"], lambda e, p: e.tensor_scalar(T.repg[:], T.cc[:], 0.0, T.bf[:, 7:8], A.mult, A.add))
-    V(KW, 0.5, [], ["rst"], lambda e, p: e.memset(T.rst[:], 0.0))
-    V(NK, 0.5, [], ["rst"], lambda e, p: e.memset(T.rst[:, 0:KW:8], 1024.0))
+    fill("rst", "rst", 0, 128, 0, KW, 1, 0.0)
+    fill("rst", "rst", 0, 128, 0, KW, 8, 1024.0)
     G(KW, [], ["oko"], lambda e, p: e.iota(T.oko[:], [[0, NK], [1, 8]], 0, 0, allow_small_or_imprecise_dtypes=True))
     G(KW, [], ["ook"], lambda e, p: e.iota(T.ook[:], [[1, 8], [0, NK]], 0, 0, allow_small_or_imprecise_dtypes=True))
-    V(NT * PW, 0.5, [], ["key0%d" % t for t in range(NT)], lambda e, p: e.memset(T.keys[:, 0:NT * PW], 0.0))
-    V(NS * NT * PW, 0.5, [], ["payh%d%d" % (s, t) for s in range(NS) for t in range(NT)], lambda e, p: e.memset(T.pay[:], 0.0))
+    fill("keys", ["key0%d" % t for t in range(NT)], 0, 128, 0, NT * PW, 1, 0.0)
     G(8, ["ones"], ["g8A"], lambda e, p: e.affine_select(T.g8A[:], T.ones[0:64, 0:8], [[-8, 8]], A.is_ge, 0.0, 0, 1))
     G(8, ["g8A"], ["g8m"], lambda e, p: e.affine_select(T.g8m[:], T.g8A[:], [[8, 8]], A.is_ge, 0.0, 7, -1))
-    V(144, 0.5, [], ["W8"], lambda e, p: e.memset(T.W8[:], 0.0))
+    fill("W8", "W8", 0, 64, 0, 144, 1, 0.0)
     V(8, 1, ["g8m"], ["W8"], lambda e, p: e.tensor_scalar(T.W8[:, 15:143:16], T.g8m[:], -8.0, None, A.mult))
     G(128, ["ones"], ["ident"], lambda e, p: e.affine_select(T.ident[:], T.ones[:], [[-1, 128]], A.is_equal, 0.0, 0, 1))
     for x in MUL:
-        if x in (3, 5, 7, -8, -16):
+        if x not in CFG["mV"]:
             S(128, 1, ["ident"], [mt(x)], lambda e, p, x=x: e.activation(mI(x), T.ident[:], ACT.Copy, scale=float(x)))
         else:
             V(128, 0.5, ["ident"], [mt(x)], lambda e, p, x=x: e.tensor_scalar(mI(x), T.ident[:], float(x), None, A.mult))
@@ -153,19 +183,16 @@ def graph(ctx):
     G(128, ["ones"], ["gA"], lambda e, p: e.affine_select(T.gA[:], T.ones[:], [[-16, 8], [0, 16]], A.is_ge, 0.0, 0, 1))
     G(128, ["gA"], ["gm"], lambda e, p: e.affine_select(T.gm[:], T.gA[:], [[16, 8], [0, 16]], A.is_ge, 0.0, 15, -1))
     S(128, 1, ["gm"], ["okw"], lambda e, p: e.activation(T.okw[:], T.gm[:], ACT.Copy, scale=float(OFF // 16)))
-    V(432, 0.5, [], ["W%d" % x for x in WMUL], lambda e, p: e.memset(T.W[:], 0.0))
+    for i, x in enumerate(WMUL):
+        fill("W", "W%d" % x, 0, 128, 144 * i, 144 * i + 144, 1, 0.0)
     for i, x in enumerate(WMUL):
         S(8, 1, ["gm"], ["W%d" % x], lambda e, p, i=i, x=x: e.activation(T.W[:, 144 * i + 15:144 * i + 143:16], T.gm[:, 0:128:16], ACT.Copy, scale=float(x)))
-    for buf, (a, b, c, d), val in (("cst", (0, 32, 0, 128), 1 / 32), ("cst", (32, 64, 0, 128), BIG / 64), ("crow", (0, 32, 0, 160), 1.0), ("crow", (32, 64, 0, 160), -15.0),
-                                   ("crow", (32, 64, 64, 128), 2.0)):
-        V(d - c, 0.5, [], ["cst"], lambda e, p, buf=buf, a=a, b=b, c=c, d=d, val=val: e.memset(T[buf][a:b, c:d], val))
+    for buf, (a, b, c, d), val in (("cst", (0, 32, 0, 128), 1 / 32), ("cst", (32, 64, 0, 128), BIG / 64), ("crow", (0, 32, 0, 224), 1.0), ("crow", (32, 64, 0, 160), -15.0),
+                                   ("crow", (32, 64, 64, 128), 2.0), ("crow", (32, 64, 160, 224), -30.0)):
+        fill(buf, "cst", a, b, c, d, 1, val)
     for (a, b, c, d), val in (((0, 64, 0, 8 * NK), 0.0), ((0, 32, 0, NK), (24 * MAG + 8) / 32), ((0, 32, NK, 2 * NK), 16 * MAG / 32), ((32, 64, NK, 2 * NK), 8 / 32),
-                              ((0, 32, 4 * NK, 7 * NK), 16 / 32)):
-        V(d - c, 0.5, [], ["cz"], lambda e, p, a=a, b=b, c=c, d=d, val=val: e.memset(T.cz[a:b, c:d], val))
-    for h in range(2):
-        V(1024, 0.5, [], ["E%d" % h], lambda e, p, h=h: e.memset(T.E[:, 1024 * h:1024 * h + 1024], 1.0))
-        G(1024, ["E%d" % h], ["E%d" % h], lambda e, p, h=h: e.affine_select(T.E[:, 1024 * h:1024 * h + 1024], T.E[:, 1024 * h:1024 * h + 1024],
-                                                                           [[-1, 64], [0, 16]], A.is_equal, 0.0, -64 * h, 1))
+                              ((0, 32, 4 * NK, 7 * NK), 16 / 32))[:4 + (CFG["sg"] == "S")]:
+        fill("cz", "cz", a, b, c, d, 1, val)
     G(128, [], ["pm"], lambda e, p: e.iota(T.pm[:], [[-1, 128]], 2048, 1))
     V(128, 1, ["pm"], ["pm2"], lambda e, p: e.tensor_scalar(T.pm2[:], T.pm[:], 15, None, A.bitwise_and))
     V(128, 1, ["pm2"], ["same1"], lambda e, p: e.tensor_scalar(T.same[:, 0:128], T.pm2[:], 0.0, None, A.is_equal))
@@ -173,25 +200,29 @@ def graph(ctx):
 
     V(256, GAT, ["vvi", "vvu", "vperm"], ["vvb"], lambda e, p: e.tensor_copy(T.vvb[:], T.vvi[:].indirect(T.vperm[:])))
     for o in range(8):
-        if o % 3 == 2:
+        if o < CFG["rS"]:
             S(256, 1, ["vvb", "omask"], ["R%d" % o], lambda e, p, o=o: e.activation(T.R[:, o:2048:8], T.vvb[0:64, :], ACT.Copy, scale=T.omask[:, o:o + 1]))
         else:
             V(256, 0.5, ["vvb", "omask"], ["R%d" % o], lambda e, p, o=o: e.tensor_scalar(T.R[:, o:2048:8], T.vvb[0:64, :], T.omask[:, o:o + 1], None, A.mult))
-    P(16, 128, ["W8"] + ["R%d" % o for o in range(8)], ["vP"],
-      mms([(cols(0, 128), T.W8[:, 15 - b:143 - b], T.R[:, 128 * b:128 * b + 128]) for b in range(16)]), pool=("N", "vP"))
+    for h in range(2):
+        P(16, 64, ["W8"] + ["R%d" % o for o in range(8)], ["vP%d" % h],
+          mms([(cols(0, 64), T.W8[:, 15 - b:143 - b], T.R[:, 128 * b + 64 * h:128 * b + 64 * h + 64]) for b in range(16)]), pool=("N", "vP%d" % h))
+    G(512, [], ["loff"], lambda e, p: e.iota(T.loff[:], [[16, LU], [0, 8]], 0, 0, allow_small_or_imprecise_dtypes=True))
     for t in range(NT):
-        V(KW, 1, ["vP", "oko"], ["key0%d" % t], lambda e, p, t=t: e.tensor_tensor(kv(0, t, HD, PW), p[:, KW * t:KW * t + KW], T.oko[:], A.add), pool=("N", "vP"), free=NT)
+        V(KW, 1, ["vP%d" % (t // 2), "oko"], ["key0%d" % t], lambda e, p, t=t: e.tensor_tensor(kv(0, t, HD, PW), p[:, KW * (t % 2):KW * (t % 2) + KW], T.oko[:], A.add),
+          pool=("N", "vP%d" % (t // 2)), free=2)
         w = slice(8 * LT * t, 8 * LT * t + 8 * LT)
-        V(8 * LT, 1, ["pgi%d" % t], ["pgw%d" % t], lambda e, p, w=w: e.tensor_copy(T.pgw[:, w], T.pgi[:, w]))
-        G(8 * LT, [], ["prew%d" % t], lambda e, p, w=w: e.iota(T.prew[:, w], [[0, 16 * LT // CH], [16, CH // 16], [0, 8]], 0, 0, allow_small_or_imprecise_dtypes=True))
-        add("G", 1100, ["prew%d" % t], ["prew%d" % t], lambda e, p, w=w: e.dma_start(T.prew[:, w], T.pre[:, w], accum_op=A.add), sem="lpre%d" % t, inc=16, lat=3500)
+        if CFG["pgw"][t] == "G":
+            G(8 * LT, ["pgi%d" % t], ["pgw%d" % t], lambda e, p, w=w: e.affine_select(T.pgw[:, w], T.pgi[:, w], [[0, 8 * LT]], A.is_ge, 0.0, 0, 0))
+        else:
+            V(8 * LT, 1, ["pgi%d" % t], ["pgw%d" % t], lambda e, p, w=w: e.tensor_copy(T.pgw[:, w], T.pgi[:, w]))
+        P(2, 512, ["preb%d" % t, "loff", "cst", "ident"], ["pP%d" % t], mms([(cols(0, 512), T.cst[0:32, :], T.loff[:]), (cols(0, 512), mI(1), T.preb[:, w])]), pool=("A", "pP%d" % t))
+        S(512, 1, ["pP%d" % t], ["prew%d" % t], lambda e, p, w=w: e.activation(T.prew[:, w], p[:, 0:512], ACT.Copy), pool=("A", "pP%d" % t), free=1)
 
-    P(2, 128, ["limb", "ident"], ["lP"], lambda e, p: [e.matmul(p[:, 128 * h:128 * h + 128], T.limb[:, 128 * h:128 * h + 128], T.ident[:], True, True) for h in range(2)][-1],
-      pool=("N", "lP"))
-    S(256, 1, ["lP"], ["limT0"], lambda e, p: e.activation(T.limT[:, 0:256], p[:, 0:256], ACT.Copy), pool=("N", "lP"), free=1)
     for s in range(1, NS):
-        add("G", 500 + 2000 * (s == 1), ["limT0"], ["sl%d" % s], lambda e, p, s=s: ctx["send"](s, T.limT[:, 256 * s:256 * s + 256], T.limT[:, 0:256], "alim%d" % s), sem="sent", inc=NE, lat=2500)
-        add("W", 0, ["sl%d" % s], ["limT%d" % s], None, sem="alim%d" % s, inc=NE, lat=8000)
+        add("G", 500 + 2000 * (s == 1), ["lim0"] + ["loff", "gm", "oko", "g8m", "ident", "cc"] * CFG["limw"], ["sl%d" % s],
+            lambda e, p, s=s: ctx["send"](s, T.limS[:, 256 * s:256 * s + 256], T.limS[:, 0:256], "alim%d" % s), sem="sent", inc=NE, lat=2500, due=CFG["limt"] + 1000 * s)
+        add("W", 0, ["sl%d" % s], ["lim%d" % s], None, sem="alim%d" % s, inc=NE, lat=8000)
 
     def begin(s, t):
         kt, n = "key%d%d" % (s, t), lambda x: "%s%d" % (x, t)
@@ -206,82 +237,97 @@ def graph(ctx):
         V(LT, GAT, [n("pgw"), n("lst")], ["c16%d" % u for u in us], lambda e, p: e.tensor_copy(T.c16[:, ln], T.pgw[:, w].indirect(lst)))
         V(LT, GAT, [n("prew"), n("lst")], [n("p16")], lambda e, p: e.tensor_copy(T.p16[:, ln], T.prew[:, w].indirect(lst)))
         S(LT, GAT, [n("pgw"), n("lst")], ["cf%d" % u for u in us], lambda e, p: e.activation(T.cf[:, ln], T.pgw[:, w].indirect(lst), ACT.Copy))
+        l0 = LT * t % LB
+        P(DUP, LT, ["lim%d" % s, "ident", n("lst")], [n("lp")], lambda e, p: [e.matmul(p[:, l0:l0 + LT, j], T.ident[:], T.limS[:, 256 * s + LT * t:256 * s + LT * t + LT], True, True)
+                                                                          for j in range(DUP)][-1], fix="LP%d" % (LT * t // LB))
 
     def step(s, st, u):
         t = u * LU // LT
-        way = [CFG["way"][(NC * (ST * NU * s + CFG["turn"][u][st]) + c) % len(CFG["way"])] for c in range(NC)]
+        way = [CFG["way"][(NC * TURN[u][ST * s + st] + c) % len(CFG["way"])] for c in range(NC)]
         ln = slice(LU * u, LU * u + LU)
         sgc = ST * LT * t + LT * st + LU * u - LT * t
         sg, sgt = T.sg[:, sgc:sgc + LU], "sg%d%d" % (u, st)
         kP, kN = "P%d" % u, "N%d" % u
         n = lambda x: "%s%d" % (x, u)
-        for c in range(NC):
-            chunk(s, st, u, c, way[c])
-        al = lambda x: ["%s%d%d" % (x, u, c) for c in range(NC)]
-        red = lambda x, buf, a=0, z=LU: [(cols(a, z), sel(x, b), buf[:, 16 * (LU * u + a) + b:16 * (LU * u + z):16]) for b in range(16)]
+        wide(s, st, u, way)
+        al = lambda x: ["%s%d%d" % (x, u, q) for q in range(4)]
+        red = lambda x, buf: [(cols(0, LU), sel(x, b), buf[:, ln, b]) for b in range(16)]
         base = lambda k: [(cols(0, LU), T.i5[:], T.cf[:, ln]), (cols(0, LU), T.cst[:], T.crow[:, k:k + LU])]
-        k = {(0, 0): 0, (0, 1): 32, (1, 1): 64, (1, 0): 96}[(way[0] in "AT") + 0, (way[-1] in "AT") + 0]
-        rel = [c for c in range(NC) if way[c] in "AC"]
-        if rel:
-            P(21, LU, al("D") + [n("cf"), "i5", "cst", "W-1"], [kP], mms(base(k) + red(-1, T.D, LU // NC * rel[0], LU // NC * (rel[-1] + 1)), True, False), pool=("P", kP))
-            P(16, LU, al("AD") + ["W1"], [kP], mms(red(1, T.AD), False, False), pool=("P", kP))
+        m = 16 // CFG["cutS"]
+        P(5 + m, LU, al("AD") + [n("cf"), "i5", "cst", "W1"], [kP], mms(base(0) + red(1, T.AD)[:m], True, False), pool=("P", kP))
+        for i in range(m, 16, m):
+            P(m, LU, al("AD") + ["W1"], [kP], mms(red(1, T.AD)[i:i + m], False, False), pool=("P", kP))
+        for j in range(0, 16, DUP):
+            P(DUP, LU, ["ni%d%d_%d" % (u, q, j) for q in range(4)] + ["W%d" % BIG], [kP], mms(red(BIG, T.ni)[j:j + DUP], False, j + DUP == 16), pool=("P", kP))
+        if CFG["sg"] == "V":
+            V(LU, 1, [kP], [sgt], lambda e, p: e.tensor_scalar(sg, p[:, 0:LU], 0.0, 2.0, A.is_lt, A.mult), pool=("P", kP), free=2)
         else:
-            P(21, LU, al("AD") + [n("cf"), "i5", "cst", "W1"], [kP], mms(base(k) + red(1, T.AD), True, False), pool=("P", kP))
-        P(16, LU, al("ni") + ["W%d" % BIG], [kP], mms(red(BIG, T.ni), False, True), pool=("P", kP))
-        S(LU, 1, [kP], [sgt], lambda e, p: e.activation(sg, p[:, 0:LU], ACT.Sign, scale=-1.0), pool=("P", kP), free=2)
-        V(LU, 1, [kP, n("cf"), sgt], [n("qq")], lambda e, p: e.tensor_tensor(T.qq[:, ln], p[:, 0:LU], T.cf[:, ln], A.max), pool=("P", kP), free=2)
-        P(5, LU, [n("cf"), "i5", "cst", kP], [kN], mms(base(0), True, False), pool=("N", kN))
+            S(LU, 1, [kP], [sgt], lambda e, p: e.activation(sg, p[:, 0:LU], ACT.Sign, scale=-1.0), pool=("P", kP), free=2)
+        V(LU, 1, [kP, n("cf")] + [sgt] * (CFG["sg"] == "S"), [n("qq")], lambda e, p: e.tensor_tensor(T.qq[:, ln], p[:, 0:LU], T.cf[:, ln], A.max), pool=("P", kP), free=2)
+        P(5, LU, [n("cf"), "i5", "cst", kP], [kN], mms(base(160 * (CFG["sg"] == "V")), True, False), pool=("N", kN))
         P(1, LU, [sgt, "okw"], [kN], mms([(cols(0, LU), T.okw[:], sg)], False, True), pool=("N", kN))
         V(LU, 1, [kN, n("qq")], [n("cpp")], lambda e, p: e.tensor_tensor(T.cpp[:, ln], p[:, 0:LU], T.qq[:, ln], A.max), pool=("N", kN), free=1)
         V(LU, 1, [n("cpp")], [n("ci")], lambda e, p: e.tensor_scalar(T.ci[:, ln], T.cpp[:, ln], 4095, None, A.bitwise_and))
         if st < ST - 1:
             V(LU, 1, [n("ci")], [n("c16")], lambda e, p: e.tensor_copy(T.c16[:, ln], T.ci[:, ln]))
-            V(LU, 1, [n("ci")], [n("cf")], lambda e, p: e.tensor_copy(T.cf[:, ln], T.ci[:, ln]))
+            if CFG["cf"] == "G":
+                G(LU, [n("ci")], [n("cf")], lambda e, p: e.affine_select(T.cf[:, ln], T.ci[:, ln], [[0, LU]], A.is_ge, 0.0, 0, 0))
+            else:
+                V(LU, 1, [n("ci")], [n("cf")], lambda e, p: e.tensor_copy(T.cf[:, ln], T.ci[:, ln]))
 
-    def chunk(s, st, u, c, way):
-        t, x = u * LU // LT, NC * u + c
-        a = CH * x
-        n = lambda y: "%s%d%d" % (y, u, c)
-        F, F2, D, AD, ni = (T[y][:, a:a + CH] for y in ("F", "F2", "D", "AD", "ni"))
-        ln = slice(a // 16, (a + CH) // 16)
-        bk, kA, kD = tuple(range(CH // 512)), n("A"), n("B")
-        halves = [(cols(512 * i, 512 * i + 512), slice(a + 512 * i, a + 512 * i + 512)) for i in bk]
+    def pieces(split):
+        out, a = [], 0
+        for x in split:
+            out.append((a, a + int(x)))
+            a += int(x)
+        return out
 
-        def stream(x, buf, start, stop):
-            return lambda e, p: [e.matmul(p[o], x, buf(w), start, stop) for o, w in halves][-1]
-        S(CH, GAT, ["X", "c16%d" % u], [n("F")], lambda e, p: e.activation(F, T.X[:].indirect(T.c16[:, ln]), ACT.Copy), due=at[0] + c * CH * GAT * CYC)
-        if way == "P":
-            V(CH, GAT, [n("F"), "p16%d" % t], [n("D")], lambda e, p: e.tensor_copy(D, F.indirect(T.p16[:, ln])))
-            P(len(bk), 512, [n("F"), "ident"], [kD], stream(mI(1), lambda w: T.F[:, w], True, False), pool=("A", kD), bk=bk)
-            P(len(bk), 512, [n("D"), mt(-1)], [kD], stream(mI(-1), lambda w: T.D[:, w], False, True), pool=("A", kD), bk=bk)
-            S(CH, 1, [kD], [n("AD")], lambda e, p: e.activation(AD, p[:], ACT.Abs), pool=("A", kD), free=1, bk=bk)
-        else:
-            how = CFG["copy"][(x + (ST * s + st) * NU * NC) % len(CFG["copy"])]
-            if how == "Q":
-                add("Q", 60, [n("F")], [n("F2")], lambda e, p: e.dma_start(F2, F), sem="cp%d" % x, inc=16, lat=CFG["dma"] * (0.7 + 0.3 * CH / 512))
+    def wide(s, st, u, way):
+        t, byP = u * LU // LT, {}
+        n = lambda y, a, b: ["%s%d%d" % (y, u, q) for q in range(a, b)]
+        v = lambda y, a, b: T[y][:, 1024 * u + 256 * a:1024 * u + 256 * b]
+        ln = lambda y, a, b: T[y][:, LU * u + 16 * a:LU * u + 16 * b]
+        for i, (a, b) in enumerate(pieces(CFG["cutF"])):
+            if CFG["fE"][(len(CFG["cutF"]) * TURN[u][ST * s + st] + i) % len(CFG["fE"])] == "V":
+                V(256 * (b - a), GAT, ["X", "c16%d" % u], n("F", a, b), lambda e, p, a=a, b=b: e.tensor_copy(v("F", a, b), T.X[:].indirect(ln("c16", a, b))),
+                  due=at[0] + 256 * a * GAT * CYC)
+                continue
+            S(256 * (b - a), GAT, ["X", "c16%d" % u], n("F", a, b), lambda e, p, a=a, b=b: e.activation(v("F", a, b), T.X[:].indirect(ln("c16", a, b)), ACT.Copy),
+              due=at[0] + 256 * a * GAT * CYC)
+        for i, (a, b) in enumerate(pieces(CFG["cutC"])):
+            how, m = CFG["copy"][(len(CFG["cutC"]) * TURN[u][ST * s + st] + i) % len(CFG["copy"])], 256 * (b - a)
+            if TURN[u][ST * s + st] >= len(CFG["seq"]) - CFG["rush"] or TURN[u][ST * s + st] < CFG["rush0"]:
+                how = CFG["rushc"][i]
+            if how in "PR":
+                byP.update(dict.fromkeys(range(a, b), how))
+            elif how == "Q":
+                add("Q", 60, n("F", a, b), n("F2", a, b), lambda e, p, a=a, b=b: e.dma_start(v("F2", a, b), v("F", a, b)), sem="cp%d" % (4 * u + i), inc=16,
+                    lat=CFG["dma"] * (0.7 + 0.3 * m / 512))
             elif how == "G":
-                G(CH, [n("F")], [n("F2")], lambda e, p: e.affine_select(F2, F, [[0, CH]], A.is_ge, 0.0, 0, 0))
-            elif how == "V":
-                V(CH, 0.5, [n("F")], [n("F2")], lambda e, p: e.tensor_copy(F2, F))
+                G(m, n("F", a, b), n("F2", a, b), lambda e, p, a=a, b=b, m=m: e.affine_select(v("F2", a, b), v("F", a, b), [[0, m]], A.is_ge, 0.0, 0, 0))
             else:
-                S(CH, 1, [n("F")], [n("F2")], lambda e, p: e.activation(F2, F, ACT.Copy))
-            V(CH, GAT, [n("F"), n("F2"), "p16%d" % t], [n("D")], lambda e, p: e.tensor_tensor(D, F2.indirect(T.p16[:, ln]), F, A.subtract))
-            if way in "AC":
-                V(CH, 0.5, [n("D")], [n("AD")], lambda e, p: e.tensor_scalar(AD, D, 0.0, 2.0, A.max, A.mult))
-            else:
-                S(CH, 1, [n("D")], [n("AD")], lambda e, p: e.activation(AD, D, ACT.Abs))
-        lim = T.limT[:, 256 * s + 128 * (u // 2):256 * s + 128 * (u // 2) + 128]
-        P(len(bk), 512, ["limT%d" % s, "E%d" % (u % 2), n("D")], [kA], stream(lim, lambda w: T.E[:, w.start % 2048:w.start % 2048 + 512], True, way in "BP"), pool=("A", kA), bk=bk)
-        if way in "AC":
-            P(len(bk), 512, [n("D"), "ident"], [kA], stream(mI(1), lambda w: T.D[:, w], False, False), pool=("A", kA), bk=bk)
-        if way in "ACT":
-            P(len(bk), 512, [n("AD"), mt(-1)], [kA], stream(mI(-1), lambda w: T.AD[:, w], False, True), pool=("A", kA), bk=bk)
-        if way in "BP":
-            V(CH, 1, [n("AD"), kA], [n("ni")], lambda e, p: e.tensor_tensor(ni, AD, p[:], A.is_gt), pool=("A", kA), free=1, bk=bk)
-        elif way == "C":
-            V(CH, 1, [kA], [n("ni")], lambda e, p: e.tensor_scalar(ni, p[:], 0.0, None, A.is_lt), pool=("A", kA), free=1, bk=bk)
-        else:
-            S(CH, 1, [kA], [n("ni")], lambda e, p: e.activation(ni, p[:], ACT.Sign, scale=-1.0, bias=-0.5), pool=("A", kA), free=1, bk=bk)
+                V(m, 0.5, n("F", a, b), n("F2", a, b), lambda e, p, a=a, b=b: e.tensor_copy(v("F2", a, b), v("F", a, b)))
+        for a, b in pieces(CFG["cutD"]):
+            if a in byP:
+                kD = "B%d%d" % (u, a)
+                if byP[a] == "P":
+                    V(512, GAT, n("F", 0, b) + ["p16%d" % t], n("D", a, b), lambda e, p, a=a, b=b: e.tensor_copy(v("D", a, b), v("F", 0, b).indirect(ln("p16", a, b))))
+                else:
+                    S(512, GAT, n("F", 0, b) + ["p16%d" % t], n("D", a, b), lambda e, p, a=a, b=b: e.activation(v("D", a, b), v("F", 0, b).indirect(ln("p16", a, b)), ACT.Copy))
+                P(1, 512, n("F", a, b) + ["ident"], [kD], mms([(cols(0, 512), mI(1), v("F", a, b))], True, False), pool=("A", kD))
+                P(1, 512, n("D", a, b) + [mt(-1)], [kD], mms([(cols(0, 512), mI(-1), v("D", a, b))], False, True), pool=("A", kD))
+                S(512, 1, [kD], n("AD", a, b), lambda e, p, a=a, b=b: e.activation(T.AD[:, LU * u + 16 * a:LU * u + 16 * b, :], p[:, 0:512], ACT.Abs), pool=("A", kD), free=1)
+                continue
+            V(256 * (b - a), GAT, n("F", 0, b) + n("F2", a, b) + ["p16%d" % t], n("D", a, b),
+              lambda e, p, a=a, b=b: e.tensor_tensor(v("D", a, b), v("F", 0, b).indirect(ln("p16", a, b)), v("F2", a, b), A.subtract))
+        for a, b in pieces(CFG["cutA"]):
+            if a not in byP:
+                S(256 * (b - a), 1, n("D", a, b), n("AD", a, b), lambda e, p, a=a, b=b: e.activation(T.AD[:, LU * u + 16 * a:LU * u + 16 * b, :], v("D", a, b), ACT.Abs))
+        for a, b in pieces(CFG["cutN"]):
+            for j in range(0, 16, DUP):
+                l, l0 = slice(LU * u + 16 * a, LU * u + 16 * b), LU * u % LB
+                V(16 * (b - a) * DUP, 1, n("AD", a, b) + ["lp%d" % u], ["ni%d%d_%d" % (u, q, j) for q in range(a, b)],
+                  lambda e, p, l=l, j=j, m=slice(l0 + 16 * a, l0 + 16 * b): e.tensor_tensor(T.ni[:, l, j:j + DUP], T.AD[:, l, j:j + DUP], p[:, m, :], A.is_gt), fix="LP%d" % (LU * u // LB))
 
     def end(s, t):
         n, q = lambda x: "%s%d" % (x, t), "%d%d" % (s, t)
@@ -294,10 +340,10 @@ def graph(ctx):
         kL, kZ = n("L"), n("Z")
         d, g8, mc = cols(0, NK), cols(NK, 2 * NK), cols(2 * NK, 3 * NK)
         P(17, ST * NK, ["sg%d%d" % (u, k) for u in us for k in range(ST)] + ["W1", "cz", "ones"], [kL],
-          mms([(cols(0, ST * NK), T.ones[0:64, :], T.cz[:, 4 * NK:7 * NK])] +
+          mms([(cols(0, ST * NK), T.ones[0:64, :], T.cz[:, 4 * NK:7 * NK])] * (CFG["sg"] == "S") +
               [(cols(0, ST * NK), sel(1, b), T.sg[:, ST * LT * t + b:ST * LT * (t + 1):16]) for b in range(16)]), pool=("N", kL))
         P(11, NK, [kL, kt, n("ks"), n("eq"), "cz", "ones"] + [mt(o) for o in (1, 2, 3, 4, 5, 6, 7, -1)], [kZ],
-          mms([(cols(0, 3 * NK), T.ones[0:64, :], T.cz[:, 0:3 * NK]), (d, mI(1), kv(s, t, NK, 2 * NK)), (cols(NK, 3 * NK), mI(1), kv(s, t, NK, 3 * NK)),
+          mms([(cols(0, HD), T.ones[0:64, :], T.cz[:, 0:HD]), (d, mI(1), kv(s, t, NK, 2 * NK)), (cols(NK, 3 * NK), mI(1), kv(s, t, NK, 3 * NK)),
                (d, mI(-1), T.ks[:, KW * t + 7:KW * t + KW:8])] + [(d, mI(o), T.eq[:, KW * t + o:KW * t + KW:8]) for o in range(1, 8)], True, False), pool=("N", kZ))
         S(ST * NK, 1, [kL], [n("fx")], lambda e, p: e.activation(T.fx[:, ST * NK * t:ST * NK * (t + 1)], p[:, 0:ST * NK], ACT.Relu, bias=-31.0), pool=("N", kL))
         P(3, NK, [n("fx"), "same1"], [kL], mms([(cols(ST * NK, (ST + 1) * NK), T.same[:, 0:128], fx(k)) for k in range(ST)]), pool=("N", kL))
@@ -306,7 +352,10 @@ def graph(ctx):
         S(2 * NK, 1, [kL], [n("hn")], lambda e, p: e.activation(T.hn[:, 2 * NK * t:2 * NK * (t + 1)], p[:, (ST - 1) * NK:(ST + 1) * NK], ACT.Identity, scale=0.5, bias=MAG - 0.25),
           pool=("N", kL), free=1)
         P(3, NK, [n("hn"), mt(-8), mt(-16)], [kZ], mms([(d, mI(-8), hn(0)), (d, mI(-16), hn(1)), (g8, mI(-16), hn(1))], False, True), pool=("N", kZ))
-        V(3 * NK, 1, [kZ], ["payh" + q], lambda e, p: e.tensor_copy(pay(0, 3 * NK), p[:, 0:3 * NK]), pool=("N", kZ), free=1)
+        if CFG["head"] == "V":
+            V(3 * NK, 1, [kZ], ["payh" + q], lambda e, p: e.tensor_copy(pay(0, HD), p[:, 0:HD]), pool=("N", kZ), free=1)
+        else:
+            S(3 * NK, 1, [kZ], ["payh" + q], lambda e, p: e.activation(pay(0, HD), p[:, 0:HD], ACT.Copy), pool=("N", kZ), free=1)
         V(KW, GAT, ["payh" + q, n("eq"), "repk"], [n("tt")], lambda e, p: e.tensor_tensor(tt, pay(0, HD).indirect(T.repk[:, 0:KW // 16]), eq, A.mult))
         V(KW, 2, [kt, n("tt")], ["pay" + q], lambda e, p: e.tensor_tensor(pay(HD, PW), kv(s, t, HD, PW), tt, A.add))
         add("G", 500, ["pay" + q, "payh" + q], ["snd" + q], lambda e, p: ctx["send"](1, kv(s + 1, t, 0, PW), pay(0, PW), "akey%d%d" % (s + 1, t)), sem="sent", inc=NE, lat=CFG["send"] - 500)
@@ -318,24 +367,24 @@ def graph(ctx):
         n, kt = lambda x: "%s%d" % (x, t), "key%d%d" % (NS, t)
         fa, fv = T.fa[:, KW * t:KW * t + KW], T.fv[:, KW * t:KW * t + KW]
         w = slice(8 * LT * t, 8 * LT * (t + 1))
-        add("Q", 60, [n("pgw")], [], lambda e, p: e.dma_start(T.yg[:, w], T.pgw[:, w]), sem="outs", inc=16, lat=3000)
+        add("Q", 60, [n("pgw")] + ["snd%d%d" % (NS - 1, t)] * CFG["ygw"], [], lambda e, p: e.dma_start(T.yg[:, w], T.pgw[:, w]), sem="outs", inc=16, lat=3000)
         V(KW, GAT, [kt, "ook", "perm"], [n("fa")], lambda e, p: e.tensor_tensor(fa, kv(NS, t, HD, PW).indirect(T.turn8[:, 0:KW // 16]), T.ook[:], A.subtract))
         V(KW, GAT, [kt, n("fa"), "repg"], [n("fv")], lambda e, p: e.tensor_tensor(fv, kv(NS, t, 0, HD).indirect(T.repg[:, 0:KW // 16]), fa, A.subtract))
-        for c in range(KW // 32):
+        for c in range(2):
             k = "Y%d%d" % (t, c)
-            P(8, 64, [n("fv"), "ident"], [k], lambda e, p, c=c: [e.matmul(p[0:8, b:512:16], T.ident[:, b:128:16], T.fv[:, KW * t + 32 * c:KW * t + 32 * c + 32], True, True)
-                                                               for b in range(16)][-1], pool=("P", k))
-            y = T.yvs[:, 8 * LT * t + 512 * c:8 * LT * t + 512 * c + 512]
-            if (t + c) % 2:
-                V(512, 1, [k], ["yv%d%d" % (t, c)], lambda e, p, y=y: e.tensor_scalar(y, p[0:8, :], 0.125, None, A.mult), pool=("P", k), free=1)
+            P(4, 64, [n("fv"), "ident"], [k], lambda e, p, c=c: [e.matmul(p[0:8, b:256:16], T.ident[:, b:128:16], T.fv[:, KW * t + 16 * c:KW * t + 16 * c + 16], True, True)
+                                                               for b in range(16)][-1], pool=("A", k))
+            y = T.yvs[:, 8 * LT * t + 256 * c:8 * LT * t + 256 * c + 256]
+            if c:
+                V(256, 1, [k], ["yv%d%d" % (t, c)], lambda e, p, y=y: e.tensor_scalar(y, p[0:8, 0:256], 0.125, None, A.mult), pool=("A", k), free=1)
             else:
-                S(512, 1, [k], ["yv%d%d" % (t, c)], lambda e, p, y=y: e.activation(y, p[0:8, :], ACT.Copy, scale=0.125), pool=("P", k), free=1)
-        add("Q", 60, ["yv%d%d" % (t, c) for c in range(KW // 32)], [], lambda e, p: e.dma_start(T.yv[:, LT * t:LT * t + LT], T.yvs[:, w]), sem="outs", inc=16, lat=2200)
+                S(256, 1, [k], ["yv%d%d" % (t, c)], lambda e, p, y=y: e.activation(y, p[0:8, 0:256], ACT.Copy, scale=0.125), pool=("A", k), free=1)
+        add("Q", 60, ["yv%d%d" % (t, c) for c in range(2)], [], lambda e, p: e.dma_start(T.yv[:, LT * t:LT * t + LT], T.yvs[:, w]), sem="outs", inc=16, lat=2200)
         P(4, 64, [kt, "ident"], [n("M")], lambda e, p: [e.matmul(p[0:8, b:LT:16], T.ident[:, b:128:16], kv(NS, t, 2 * NK, 3 * NK), True, True) for b in range(16)][-1], pool=("N", n("M")))
         S(LT, 1, [n("M")], [n("ym")], lambda e, p: e.activation(T.yms[:, LT * t:LT * t + LT], p[0:8, 0:LT], ACT.Copy), pool=("N", n("M")), free=1)
 
     def due(s, st, u):
-        return CFG["t0"] + CFG["slot"] * (ST * NU * s + CFG["turn"][u][st])
+        return CFG["t0"] + CFG["slot"] * (TURN[u][ST * s + st] + CFG["shift"][ST * u + st])
 
     for s in range(NS):
         for t in range(NT):
@@ -347,7 +396,9 @@ def graph(ctx):
                     step(s, st, u)
             end(s, t)
     for t in range(NT):
+        at[1] = END - CFG["early"] * (len(CFG["seq"]) - 1 - TURN[t][-1])
         final(t)
+    at[1] = END
     add("Q", 60, ["ym%d" % t for t in range(NT)], [], lambda e, p: e.dma_start(T.ym[:], T.yms[:]), sem="outs", inc=16, lat=2200)
     return ops
 
@@ -383,11 +434,12 @@ def plan(ops):
             succ[d].append(i)
     pr = [0.0] * n
     for i in reversed(range(n)):
-        pr[i] = min(ops[i]["due"], min([pr[x] for x in succ[i]] + [CFG["end"]]) - ops[i]["cost"] - ops[i]["lat"] - wake)
+        pr[i] = min(ops[i]["due"], min([pr[x] for x in succ[i]] + [ops[i]["end"]]) - ops[i]["cost"] - ops[i]["lat"] - wake)
     es = [0.0] * n
     for i in range(n):
         es[i] = ops[i]["due"] if ops[i]["due"] < 1e8 else max([es[d] + ops[d]["cost"] + ops[d]["lat"] + wake for d in dep[i]] + [0.0])
     pr = [pr[i] if pr[i] < CFG["t0"] else pr[i] + CFG["mix"] * min(0.0, max(es[i] - pr[i], -CFG["cap"])) for i in range(n)]
+    pr = [pr[i] + CFG["bias"].get((ops[i]["wr"] + [""])[0].rstrip("0123456789"), 0.0) for i in range(n)]
     done, start, buf = [0.0] * n, [0.0] * n, {}
     free = {e: 0.0 for e in "VSPGQW"}
     slot = {k: [0.0] * len(v) for k, v in POOLS.items()}
@@ -408,7 +460,15 @@ def plan(ops):
         cand = None
         for e, lst in best.items():
             t0 = min(lst)[0]
-            pick = min((pr[i], t, i) for t, i in lst if t <= t0 + CFG["look"])
+            pick = min((pr[i], t, i) for t, i in lst if t <= t0 + CFG["look"].get(e, 0.0))
+            d = ops[pick[2]]["cost"]
+            soon = min((pr[i], t, i) for t, i in lst if t <= pick[1] + d)
+            if soon[0] < pick[0] - CFG["gap"] and CFG["idle"].get(e):
+                fit = [(pr[i], t, i) for t, i in lst if t + ops[i]["cost"] <= soon[1] + CFG["tol"] and i != soon[2]]
+                if fit:
+                    pick = min(fit)
+                elif soon[1] - pick[1] <= CFG["idle"][e] * (pick[1] + d - soon[1]):
+                    pick = soon
             if cand is None or pick[1] < cand[0]:
                 cand = (pick[1], pick[2])
         t, i = cand
@@ -420,6 +480,8 @@ def plan(ops):
                 held[k] = min((x, y) for y, x in enumerate(slot[k[0]]) if x is not None)[1]
                 slot[k[0]][held[k]] = None
             buf[i] = POOLS[k[0]][held[k]]
+        if o["fix"]:
+            buf[i] = o["fix"]
         start[i] = t
         done[i] = t + o["cost"] + o["lat"]
         free[o["eng"]] = t + o["cost"]

@@ -3,89 +3,75 @@ from concourse.mybir import AluOpType, ActivationFunctionType
 ACT = ActivationFunctionType
 NS, ST, NL = 4, 3, 256
 LU, NU = 64, 4
+NK = LU // 16
+KW, HD = 8 * NK, 16
+PW = HD + KW
+WW = 8 * LU + KW
+XW = 4096 + 8 * NL
 BIG = 65536
 OFF = 491520
 MAG = 129
+DUP = 8
 
-CFG = dict(LT=64, CH=512, way="TBBB", copy="G", look={"V": 30}, cutS=2, sg="S", shift=(0,) * 12, idle={}, gap=0.0, tol=30.0, fE="S", one=0, ld=0.72, fillS=("cst", "crow", "cz"), mV=(2, 4, 6, -1), rS=3, cf="V", pgw="VVVV", eV=4, rush=0, rush0=0, rushc="VV", banks=(3, 2, 3), t0=7500.0, slot=3300.0, hold=1e9, mix=0.85, cap=5000.0,
-           seq="ABCABDACBDCADBACBDACBDCADBACBDACBDCADBACBDACDBCD", tail=11000.0, early=1000.0, ygw=0, head="V",
-           bias={"pgw": 1200, "ks": 2500, "cpp": 600, "N": -300, "ni": -300},
-           cutF="22", cutC="22", cutD="22", cutA="22", cutN="22", Ldep="D",
-           loads="pg0 xt pre0 pg1 lim pre1 pg2 pre2 pg3 pre3",
-           gat=1.5, wake=80.0, dma=2300.0, send=2600.0)
-CFG.update({'wake': 100.0, 'gat': 1.45, 'slot': 3300, 'bias': {'Z': -300, 'A': -300}, 'look': {}, 'way': 'TBBB', 'sg': 'V', 'head': 'S', 'banks': (8, 0, 0), 'one': 1, 'eV': 4,
-            'early': 0, 'tail': 9000, 'loads': 'pg0 lim xt pre0 pg1 pre1 pg2 pre2 pg3 pre3', 'fillS': (), 'cf': 'V'})
-CFG.update({'vfix': 20, 'sfix': 30, 'wake': 160.0, 'idle': {'V': 0.3, 'S': 0.3, 'P': 0, 'G': 1.5}, 'cutC': '211', 'cutD': '211', 'cutA': '211', 'cutN': '211',
-            'bias': {'pay': -1200, 'snd': -2500, 'fx': -2500, 'cf': 2500, 'tt': 600}, 'shift': [0, 0, 0, 0, -0.25, 0, 0, 0, 0, 0, 0, 0], 'eV': 2, 'mV': (2, 4, 6), 'fillS': ('cz',), 'tail': 11000})
-CFG.update(dup=4, cutN="22", way="B", loads="lim pg0 xt pre0 pg1 pre1 pg2 pre2 pg3 pre3", cutQ=1, limw=1, limt=4000.0)
-CFG.update({'dup': 8, 'cutN': '22', 'cutC': '22', 'cutD': '22', 'cutA': '22', 'copy': 'RGGGGG', 'bias': {'ks': -600, 'cf': -300, 'Z': -900, 'p': -300, 'pgw': 2500}, 'idle': {'P': 0.8},
-            'shift': [0, 0, -0.25, 0, 0.5, 0, 0, 0, 0, 0, 0, 0], 'rS': 2, 'gat': 1.4, 'tol': 80, 'limw': 0, 'vfix': 20, 'loads': 'pg0 lim xt pre0 pg1 pre1 pg2 pre2 pg3 pre3'})
-LT, CH = CFG["LT"], CFG["CH"]
-NT, NK, NC = NL // LT, LT // 16, 16 * LU // CH
-KW = 8 * NK
-HD = 16 * (-(-3 * NK // 16))
-PW = HD + KW
-LG = NK.bit_length() - 1
+CFG = dict(seq="ABCABDACBDCADBACBDACBDCADBACBDACBDCADBACBDACDBCD", t0=7500.0, slot=3000.0, shift=(0,) * 12, tail=9000.0, early=0.0,
+           copy="RGGGGG", cutF="22", cutC="22", cutD="22", cutA="22", cutN="22", cutS=2, cfS=1,
+           loads="pg0 xt pre0 lim pg1 pre1 pg2 pre2 pg3 pre3", ld=0.72, rS=2, big=(13000.0, 46000.0, 80000.0), parts=(0, 0, 0), first=6000.0, grp=2, one="win10",
+           gat=1.5, wake=190.0, send=2600.0, vfix=5, sfix=10, mix=0.85, cap=5000.0, idle={"P": 0.8, "V": 0.15, "S": 0.15}, gap=0.0, tol=60.0, bias={})
+CFG.update({'seq': 'ABCD' * 12, 'slot': 2900, 'grp': 4, 'big': (11000.0, 16000.0, 21000.0), 'mix': 0.75, 'tol': 30.0, 'early': 400.0, 'tail': 11000.0, 'gat': 1.55, 'first': 6000,
+            'bias': {'sg': -300, 'N': -300, 'cpp': -300, 'ci': -300, 'c': -300, 'cout': -300, 'p': -300, 'Fc': 900, 'od': -4200, 'B': -300, 'eq': 2400, 'cf': 300, 'sndwin': -1200},
+            'idle': {'P': 0.15, 'V': 0.15, 'S': 0.15, 'G': 0.8}, 'shift': [0, 0, -0.25, 0, 0.25, 0, -0.25, 0, 0, 0, 0, 0], 'loads': 'pg0 xt pg1 pre0 lim pre1 pg2 pre2 pg3 pre3'})
 TURN = [[i for i, x in enumerate(CFG["seq"]) if x == "ABCD"[u]] for u in range(NU)]
 END = CFG["t0"] + CFG["slot"] * (len(CFG["seq"]) - 1) + CFG["tail"]
 
 B16, F32, I32, U16 = "bfloat16", "float32", "int32", "uint16"
 SCRATCH = {}
 for _n, _p, _w, _d in (
-        ("X", 128, 4096, B16), ("pgi", 128, 2048, I32), ("pgw", 128, 2048, F32), ("prew", 128, 2048, F32),
-        ("preb", 128, 2048, B16), ("loff", 32, 512, B16),
-        ("vvi", 128, 256, I32), ("vvb", 128, 256, B16), ("R", 64, 2048, B16), ("limS", 128, NS * 256, B16),
-        ("ones", 128, 128, B16), ("wide", 128, 224, B16), ("ident", 128, 128, B16), ("mI", 128, 128 * 10, B16), ("i5", 128, 128, F32),
-        ("gA", 128, 128, B16), ("gm", 128, 128, B16), ("okw", 128, 128, B16), ("W", 128, 3 * 144, B16),
-        ("g8A", 64, 8, B16), ("g8m", 64, 8, B16), ("W8", 64, 144, B16), ("cst", 64, 128, B16), ("crow", 64, 224, B16), ("cz", 64, 8 * NK, B16),
+        ("XP", 128, NS * XW, B16), ("win", 128, (NS + 1) * NU * WW, F32),
+        ("cout", 128, NS * NL, I32), ("cin", 128, NS * NL, I32), ("lin", 128, NU * NK, U16),
+        ("pgi", 128, 8 * NL, I32), ("pf", 128, NL, F32), ("loff", 128, LU, F32), ("limb", 128, NL, B16),
+        ("vvi", 128, NL, I32), ("vvb", 128, NL, B16), ("R", 64, 8 * NL, B16),
+        ("ones", 128, 128, B16), ("ident", 128, 128, B16), ("mI", 128, 3 * 128, B16), ("i5", 128, 128, F32),
+        ("gA", 128, 128, B16), ("gm", 128, 128, B16), ("okw", 128, 128, B16), ("W", 128, 2 * 144, B16),
+        ("g8A", 64, 8, B16), ("g8m", 64, 8, B16), ("W8", 64, 144, B16), ("cst", 64, 128, B16), ("crow", 64, 128, B16), ("cz", 64, HD, B16),
         ("pm", 128, 128, I32), ("pm2", 128, 128, I32), ("same", 128, 256, B16),
         ("om", 64, 8, I32), ("om2", 64, 8, I32), ("omask", 64, 8, F32),
         ("vp", 128, 16, I32), ("vp2", 128, 16, I32), ("vperm", 128, 16, U16),
-        ("p1", 128, 2, I32), ("p8", 128, 2, I32), ("bi", 128, 8, I32), ("bf", 128, 8, F32), ("cc", 128, 8, I32),
-        ("rep7", 128, 8, U16), ("repk", 128, 8, U16), ("turn8", 128, 8, U16), ("repg", 128, 8, U16), ("pa", 128, 8, F32),
-        ("lane8", 128, NK, B16), ("rst", 128, KW, B16), ("oko", 128, KW, B16), ("ook", 128, KW, B16),
-        ("keys", 128, (NS + 1) * NT * PW, B16), ("pay", 128, NS * NT * PW, B16),
-        ("ks", 128, NT * KW, B16), ("eq", 128, NT * KW, B16), ("tt", 128, NT * KW, B16), ("lst", 128, NT * NK, U16),
-        ("fx", 128, NT * ST * NK, B16), ("hn", 128, NT * 2 * NK, B16), ("sg", 128, ST * NL, B16),
-        ("fa", 128, NT * KW, B16), ("fv", 128, NT * KW, B16), ("yvs", 8, 8 * NL, F32), ("yms", 8, NL, F32),
+        ("p1", 128, 2, I32), ("p8", 128, 2, I32), ("bi", 128, 4, I32), ("bf", 128, 4, F32), ("cc", 128, 4, I32),
+        ("rep7", 128, 2, U16), ("repk", 128, 2, U16), ("repg", 128, 2, U16), ("lane8", 128, NK, B16),
+        ("rst", 128, KW, B16), ("cpl", 128, KW, F32), ("co", 128, KW, B16), ("oko", 128, KW, B16), ("orow", 32, 8 * LU, B16),
+        ("keys", 128, (NS + 1) * NU * PW, B16), ("ks", 128, NU * KW, B16), ("eq", 128, NU * KW, B16), ("ne", 128, NU * KW, B16), ("od", 128, NU * KW, B16),
+        ("tt", 128, NU * KW, B16), ("fv", 128, NU * KW, B16), ("lst", 128, NU * NK, U16),
+        ("fx", 128, NU * ST * NK, B16), ("hn", 128, NU * 2 * NK, B16), ("sg", 128, ST * NL, B16), ("yvs", 8, 8 * NL, F32), ("yms", 8, NL, F32),
         ("c16", 128, NL, U16), ("p16", 128, NL, U16), ("cf", 128, NL, F32), ("ci", 128, NL, I32), ("cpp", 128, NL, I32), ("qq", 128, NL, F32),
         ("F", 128, 16 * NL, B16), ("F2", 128, 16 * NL, B16), ("D", 128, 16 * NL, B16)):
     SCRATCH[_n] = ("sbuf", [_p, _w], _d)
-DUP = CFG["dup"]
-LB = 512 // DUP
 for _n in ("AD", "ni"):
     SCRATCH[_n] = ("sbuf", [128, NL, 16], B16)
-for _i in range(NL // LB):
-    SCRATCH["LP%d" % _i] = ("psum", [128, LB, DUP], F32)
-POOLS = {}
-for _k, _n, _w in zip("APN", (8 - NL // LB, 0, 0), (CH, 512, 512)):
-    POOLS[_k] = ["P%s%d" % (_k, _i) for _i in range(_n)]
-    for _b in POOLS[_k]:
-        SCRATCH[_b] = ("psum", [128, _w], F32)
+for _u in range(NU):
+    SCRATCH["LP%d" % _u] = ("psum", [128, LU, DUP], F32)
+BANKS = ["PB%d" % _i for _i in range(8 - NU)]
+for _b in BANKS:
+    SCRATCH[_b] = ("psum", [128, 512], F32)
 
-SEMAPHORES = ["cV", "cS", "cP", "cG", "lvv", "llim", "lxt", "outs", "sent"]
-SEMAPHORES += ["lpg%d" % t for t in range(NT)] + ["lpre%d" % t for t in range(NT)] + ["cp%d" % x for x in range(NU * 4) if "Q" in CFG["copy"]]
-SEMAPHORES += ["alim%d" % s for s in range(1, NS)] + ["akey%d%d" % (s, t) for s in range(1, NS + 1) for t in range(NT)]
+SEMAPHORES = ["cV", "cS", "cP", "cG", "lvv", "llim", "lxt", "outs", "sent"] + ["lpg%d" % u for u in range(NU)] + ["lpre%d" % u for u in range(NU)]
+SEMAPHORES += ["aX%d" % s for s in range(1, NS)] + ["a%s%d%d" % (x, s, u) for x, k in (("win", CFG["grp"]), ("cin", 1)) for s in range(1, NS + 1) for u in range(0, NU, k)]
 
 CYC, PEC = 0.83, 0.42
-VFIX, SFIX = CFG.get("vfix", 5), CFG.get("sfix", 10)
 
 
 def graph(ctx):
-    T, A, NE = ctx["T"], AluOpType, ctx["NE"]
-    GAT = CFG["gat"]
-    ops, at = [], [0.0, END]
+    T, A = ctx["T"], AluOpType
+    GAT, SCAT = CFG["gat"], 3.8
+    ops, at = [], [0.0, END, 0]
 
-    def add(eng, cost, rd, wr, fn, pool=None, free=None, sem=None, inc=None, lat=0.0, bk=(0,), due=1e9, fix=None):
-        if pool:
-            pool = ("A", pool[0] + pool[1])
-        ops.append(dict(fix=fix, eng=eng, cost=cost, rd=rd, wr=wr, fn=fn, due=due, end=at[1], pool=pool, free=free, sem=sem, inc=inc, lat=lat, bk=bk))
+    def add(eng, cost, rd, wr, fn, pool=None, free=None, sem=None, inc=None, lat=0.0, due=1e9, fix=None, rel=0.0):
+        ops.append(dict(eng=eng, cost=cost, rd=rd, wr=wr, fn=fn, pool=pool, free=free, sem=sem, inc=inc, lat=lat, due=due, fix=fix, rel=rel, end=at[1], st=at[2]))
 
     def V(n, cyc, rd, wr, fn, **k):
-        add("V", 50 + n * cyc * CYC if cyc in (GAT, 3.5) and VFIX < 50 else VFIX + max(64, n * cyc) * CYC, rd, wr, fn, **k)
+        add("V", 50 + n * cyc * CYC if cyc in (GAT, SCAT) else CFG["vfix"] + max(64, n * cyc) * CYC, rd, wr, fn, **k)
 
     def S(n, cyc, rd, wr, fn, **k):
-        add("S", 65 + n * cyc * CYC if cyc == GAT and VFIX < 50 else SFIX + max(64, n * cyc) * CYC, rd, wr, fn, **k)
+        add("S", 65 + n * cyc * CYC if cyc == GAT else CFG["sfix"] + max(64, n * cyc) * CYC, rd, wr, fn, **k)
 
     def P(k, n, rd, wr, fn, **kw):
         add("P", k * max(64, n) * PEC, rd, wr, fn, **kw)
@@ -93,8 +79,16 @@ def graph(ctx):
     def G(n, rd, wr, fn, **k):
         add("G", 150 + 2 * n * CYC, rd, wr, fn, **k)
 
-    def load(eng, out, inp, tile, sem, lat, rd=()):
-        add(eng, 60, list(rd), [tile], lambda e, p: e.dma_start(out, inp), sem=sem, inc=16, lat=lat, due=len(ops) - 1e9)
+    def load(out, inp, tile, sem, lat):
+        add("Q", 60, [], [tile], lambda e, p: e.dma_start(out, inp), sem=sem, inc=16, lat=lat, due=len(ops) - 1e9)
+
+    def send(d, out, inp, rd, tile, part, lat, tiles=(), **k):
+        n = ctx["engines"](part)
+        add("G", 500 + 2000 * (tile == CFG["one"]), rd, ["snd" + tile], lambda e, p: ctx["send"](d, out, inp, "a" + tile, part), sem="sent", inc=n, lat=lat - 500, **k)
+        add("W", 0, ["snd" + tile], list(tiles) or [tile], None, sem="a" + tile, inc=n)
+
+    def fill(buf, tile, a, b, c, d, step, val):
+        V(len(range(c, d, step)), 0.5, [], [tile] if isinstance(tile, str) else tile, lambda e, p: e.memset(T[buf][a:b, c:d:step], val))
 
     def mms(lst, start=True, stop=True):
         def fn(e, p):
@@ -103,44 +97,40 @@ def graph(ctx):
             return x
         return fn
 
-    def cols(a, b, c=None):
-        return (slice(None), slice(a, b, c))
+    def cols(a, b):
+        return (slice(None), slice(a, b))
 
-    def kv(s, t, a, b, c=None):
-        return T.keys[:, (NT * s + t) * PW + a:(NT * s + t) * PW + b:c]
+    def kv(s, u, a, b):
+        return T.keys[:, (NU * s + u) * PW + a:(NU * s + u) * PW + b]
 
-    MUL = (2, 3, 4, 5, 6, 7, -1, -8, -16)
-    WMUL = (1, BIG, -1) if set(CFG["way"]) & set("AC") else (1, BIG)
+    def wv(s, u, a, b, c=None):
+        return T.win[:, (NU * s + u) * WW + a:(NU * s + u) * WW + b:c]
+
+    def part(buf, u, w, a=0, c=None):
+        return T[buf][:, w * u + a:w * u + w:c]
+
+    MUL = (-1, -8, -16)
 
     def mI(x):
-        return T.ident[:] if x == 1 else T.mI[:, 128 * MUL.index(x):128 * MUL.index(x) + 128]
-
-    def mt(x):
-        return "ident" if x == 1 else "mI%d" % x
+        return T.ident[:] if x == 1 else part("mI", MUL.index(x), 128)
 
     def sel(x, b):
-        return T.W[:, 144 * WMUL.index(x) + 15 - b:144 * WMUL.index(x) + 143 - b]
+        return T.W[:, 144 * (x != 1) + 15 - b:144 * (x != 1) + 143 - b]
 
-    load("Q", T.vvi[0:64, :], T.vv[:], "vvi", "lvv", 2000)
+    def pieces(split):
+        ends = [sum(int(x) for x in split[:i]) for i in range(len(split) + 1)]
+        return list(zip(ends, ends[1:]))
+
+    load(T.vvi[0:64, :], T.vv[:], "vvi", "lvv", 2000)
     lat = 1800
     for x in CFG["loads"].split():
-        w = slice(8 * LT * int(x[-1]), 8 * LT * int(x[-1]) + 8 * LT) if x[-1].isdigit() else None
-        out, inp, dt = {"pg": (T.pgi, T.pg, 1200), "pr": (T.preb, T.pre, 800), "li": (T.limS, T.lim, 600), "xt": (T.X, T.xt, 3700)}[x[:2]]
+        out, inp, tile, dt = {"pg": (T.pgi, T.pg, "pgi", 1200), "pr": (T.XP, T.pre, "prew0_", 800), "li": (T.limb, T.lim, "limb", 600), "xt": (T.XP, T.xt, "X0", 3700)}[x[:2]]
+        w = slice(8 * LU * int(x[-1]), 8 * LU * int(x[-1]) + 8 * LU) if x[-1].isdigit() else slice(0, inp.shape[1])
+        a = 4096 * (x[:2] == "pr")
         lat += dt * CFG["ld"]
-        load("Q", out[:, w] if w else out[:, 0:inp.shape[1]], inp[:, w] if w else inp[:], {"pg": "pgi", "pr": "preb", "li": "lim0", "xt": "X"}[x[:2]] + (x[-1] if w else ""), "l" + x, lat)
-
-    bits = (("p1", A.bitwise_and, 8, None, None), ("p1", A.logical_shift_right, 3, A.bitwise_and, 1), ("p8", A.bitwise_and, 127, None, None),
-            ("p8", A.bitwise_and, 8 * NK - 8, None, None), ("p1", A.bitwise_and, 15, A.logical_shift_right, LG), ("p1", A.bitwise_and, NK - 1, None, None))
-    def fill(buf, tile, a, b, c, d, step, val):
-        m, tiles = len(range(c, d, step)), [tile] if isinstance(tile, str) else tile
-        if buf in CFG["fillS"]:
-            S(m, 1, ["wide"], tiles, lambda e, p: e.activation(T[buf][a:b, c:d:step], T.wide[a:b, 0:m], ACT.Copy, scale=val))
-        else:
-            V(m, 0.5, [], tiles, lambda e, p: e.memset(T[buf][a:b, c:d:step], val))
+        load(out[:, a + w.start:a + w.stop], inp[:, w], tile + x[-1] * x[-1].isdigit(), "l" + x, lat)
 
     V(128, 0.5, [], ["ones"], lambda e, p: e.memset(T.ones[:], 1.0))
-    if CFG["fillS"]:
-        V(224, 0.5, [], ["wide"], lambda e, p: e.memset(T.wide[:], 1.0))
     V(256, 1, [], ["vvu"], lambda e, p: e.memset(T.vvi[64:128, :], 0))
     G(16, [], ["vp"], lambda e, p: e.iota(T.vp[:], [[1, 16]], 0, 16))
     V(16, 1, ["vp"], ["vp2"], lambda e, p: e.tensor_scalar(T.vp2[:], T.vp[:], 255, None, A.bitwise_and))
@@ -150,48 +140,42 @@ def graph(ctx):
     V(8, 1, ["om2"], ["omask"], lambda e, p: e.tensor_scalar(T.omask[:], T.om2[:], 0.0, None, A.is_equal))
     G(2, [], ["p1"], lambda e, p: e.iota(T.p1[:], [[0, 2]], 0, 1))
     G(2, [], ["p8"], lambda e, p: e.iota(T.p8[:], [[0, 2]], 0, 8))
-    G(8, [], ["cc"], lambda e, p: e.iota(T.cc[:], [[1, 8]], 0, 0))
-    for i, (src, o0, a0, o1, a1) in enumerate(bits):
-        V(1, 1, [src], ["bi%d" % i], lambda e, p, i=i, src=src, o0=o0, a0=a0, o1=o1, a1=a1:
-          e.tensor_scalar(T.bi[:, i:i + 1], T[src][:, 0:1], a0, a1, o0, o1) if o1 else e.tensor_scalar(T.bi[:, i:i + 1], T[src][:, 0:1], a0, None, o0))
-    V(3, 1, ["bi0", "bi1", "bi2"], ["bfa"], lambda e, p: e.tensor_copy(T.bf[:, 0:3], T.bi[:, 0:3]))
-    V(3, 1, ["bi3", "bi4", "bi5"], ["bfb"], lambda e, p: e.tensor_copy(T.bf[:, 3:6], T.bi[:, 3:6]))
-    S(1, 1, ["bfa"], ["bf7"], lambda e, p: e.activation(T.bf[:, 6:7], T.bf[:, 0:1], ACT.Identity, bias=7.0))
-    S(1, 1, ["bfb"], ["bfg"], lambda e, p: e.activation(T.bf[:, 7:8], T.bf[:, 5:6], ACT.Identity, bias=float(NK)))
-    V(8, 1, ["cc", "bf7"], ["rep7"], lambda e, p: e.tensor_scalar(T.rep7[:], T.cc[:], 16.0, T.bf[:, 6:7], A.mult, A.add))
-    V(8, 1, ["cc", "bfa"], ["repk"], lambda e, p: e.tensor_scalar(T.repk[:], T.cc[:], 2.0, T.bf[:, 1:2], A.mult, A.add))
-    V(8, 1, ["cc", "bfa"], ["lane8"], lambda e, p: e.tensor_scalar(T.lane8[:], T.cc[:, 0:NK], 128.0, T.bf[:, 2:3], A.mult, A.add))
-    V(8, 1, ["cc", "bfb"], ["pa"], lambda e, p: e.tensor_scalar(T.pa[:], T.cc[:], float(16 // NK), T.bf[:, 3:4], A.mult, A.add))
-    V(8, 1, ["pa", "bfb"], ["perm"], lambda e, p: e.tensor_scalar(T.turn8[:], T.pa[:], T.bf[:, 4:5], None, A.add))
-    V(8, 1, ["cc", "bfg"], ["repg"], lambda e, p: e.tensor_scalar(T.repg[:], T.cc[:], 0.0, T.bf[:, 7:8], A.mult, A.add))
-    fill("rst", "rst", 0, 128, 0, KW, 1, 0.0)
-    fill("rst", "rst", 0, 128, 0, KW, 8, 1024.0)
+    G(4, [], ["cc"], lambda e, p: e.iota(T.cc[:], [[1, 4]], 0, 0))
+    V(1, 1, ["p1"], ["bi0"], lambda e, p: e.tensor_scalar(T.bi[:, 0:1], T.p1[:, 0:1], 8, None, A.bitwise_and))
+    V(1, 1, ["p1"], ["bi1"], lambda e, p: e.tensor_scalar(T.bi[:, 1:2], T.p1[:, 0:1], 3, 1, A.logical_shift_right, A.bitwise_and))
+    V(1, 1, ["p8"], ["bi2"], lambda e, p: e.tensor_scalar(T.bi[:, 2:3], T.p8[:, 0:1], 127, None, A.bitwise_and))
+    V(3, 1, ["bi0", "bi1", "bi2"], ["bf"], lambda e, p: e.tensor_copy(T.bf[:, 0:3], T.bi[:, 0:3]))
+    S(1, 1, ["bf"], ["bf7"], lambda e, p: e.activation(T.bf[:, 3:4], T.bf[:, 0:1], ACT.Identity, bias=7.0))
+    V(2, 1, ["cc", "bf7"], ["rep7"], lambda e, p: e.tensor_scalar(T.rep7[:], T.cc[:, 0:2], 16.0, T.bf[:, 3:4], A.mult, A.add))
+    V(2, 1, ["cc", "bf"], ["repk"], lambda e, p: e.tensor_scalar(T.repk[:], T.cc[:, 0:2], 2.0, T.bf[:, 1:2], A.mult, A.add))
+    V(2, 1, ["repk"], ["repg"], lambda e, p: e.tensor_scalar(T.repg[:], T.repk[:], float(NK), None, A.add))
+    V(NK, 1, ["cc", "bf"], ["lane8"], lambda e, p: e.tensor_scalar(T.lane8[:], T.cc[:], 128.0, T.bf[:, 2:3], A.mult, A.add))
+    fill("cpl", "cpl", 0, 128, 0, KW, 1, -1.0)
+    V(NK, 1, ["lane8"], ["cpl"], lambda e, p: e.tensor_scalar(T.cpl[:, 7:KW:8], T.lane8[:], 7.0, None, A.add))
+    for buf, rest, a, val in (("co", -1.0, 7, 7.0), ("rst", 0.0, 0, 1024.0)):
+        fill(buf, buf, 0, 128, 0, KW, 1, rest)
+        fill(buf, buf, 0, 128, a, KW, 8, val)
     G(KW, [], ["oko"], lambda e, p: e.iota(T.oko[:], [[0, NK], [1, 8]], 0, 0, allow_small_or_imprecise_dtypes=True))
-    G(KW, [], ["ook"], lambda e, p: e.iota(T.ook[:], [[1, 8], [0, NK]], 0, 0, allow_small_or_imprecise_dtypes=True))
-    fill("keys", ["key0%d" % t for t in range(NT)], 0, 128, 0, NT * PW, 1, 0.0)
+    G(8 * LU, [], ["orow"], lambda e, p: e.iota(T.orow[:], [[1, 8], [0, LU]], 64, 0, allow_small_or_imprecise_dtypes=True), rel=20000.0)
+    G(LU, [], ["loff"], lambda e, p: e.iota(T.loff[:], [[16, LU]], 0, 0, allow_small_or_imprecise_dtypes=True))
+    fill("keys", [x + "0%d" % u for u in range(NU) for x in ("kh", "kk")], 0, 128, 0, NU * PW, 1, -64.0)
     G(8, ["ones"], ["g8A"], lambda e, p: e.affine_select(T.g8A[:], T.ones[0:64, 0:8], [[-8, 8]], A.is_ge, 0.0, 0, 1))
     G(8, ["g8A"], ["g8m"], lambda e, p: e.affine_select(T.g8m[:], T.g8A[:], [[8, 8]], A.is_ge, 0.0, 7, -1))
     fill("W8", "W8", 0, 64, 0, 144, 1, 0.0)
     V(8, 1, ["g8m"], ["W8"], lambda e, p: e.tensor_scalar(T.W8[:, 15:143:16], T.g8m[:], -8.0, None, A.mult))
     G(128, ["ones"], ["ident"], lambda e, p: e.affine_select(T.ident[:], T.ones[:], [[-1, 128]], A.is_equal, 0.0, 0, 1))
     for x in MUL:
-        if x not in CFG["mV"]:
-            S(128, 1, ["ident"], [mt(x)], lambda e, p, x=x: e.activation(mI(x), T.ident[:], ACT.Copy, scale=float(x)))
-        else:
-            V(128, 0.5, ["ident"], [mt(x)], lambda e, p, x=x: e.tensor_scalar(mI(x), T.ident[:], float(x), None, A.mult))
+        S(128, 1, ["ident"], ["mI%d" % -x], lambda e, p, x=x: e.activation(mI(x), T.ident[:], ACT.Copy, scale=float(x)))
     S(128, 1, ["ident"], ["i5"], lambda e, p: e.activation(T.i5[:], T.ident[:], ACT.Copy, scale=5.0))
     G(128, ["ones"], ["gA"], lambda e, p: e.affine_select(T.gA[:], T.ones[:], [[-16, 8], [0, 16]], A.is_ge, 0.0, 0, 1))
     G(128, ["gA"], ["gm"], lambda e, p: e.affine_select(T.gm[:], T.gA[:], [[16, 8], [0, 16]], A.is_ge, 0.0, 15, -1))
     S(128, 1, ["gm"], ["okw"], lambda e, p: e.activation(T.okw[:], T.gm[:], ACT.Copy, scale=float(OFF // 16)))
-    for i, x in enumerate(WMUL):
-        fill("W", "W%d" % x, 0, 128, 144 * i, 144 * i + 144, 1, 0.0)
-    for i, x in enumerate(WMUL):
-        S(8, 1, ["gm"], ["W%d" % x], lambda e, p, i=i, x=x: e.activation(T.W[:, 144 * i + 15:144 * i + 143:16], T.gm[:, 0:128:16], ACT.Copy, scale=float(x)))
-    for buf, (a, b, c, d), val in (("cst", (0, 32, 0, 128), 1 / 32), ("cst", (32, 64, 0, 128), BIG / 64), ("crow", (0, 32, 0, 224), 1.0), ("crow", (32, 64, 0, 160), -15.0),
-                                   ("crow", (32, 64, 64, 128), 2.0), ("crow", (32, 64, 160, 224), -30.0)):
+    fill("W", ["W0", "W1"], 0, 128, 0, 288, 1, 0.0)
+    for i, x in enumerate((1, BIG)):
+        S(8, 1, ["gm"], ["W%d" % i], lambda e, p, i=i, x=x: e.activation(T.W[:, 144 * i + 15:144 * i + 143:16], T.gm[:, 0:128:16], ACT.Copy, scale=float(x)))
+    for buf, a, b, c, d, val in (("cst", 0, 32, 0, 128, 1 / 32), ("cst", 32, 64, 0, 128, BIG / 64), ("crow", 0, 32, 0, 128, 1.0), ("crow", 32, 64, 0, 64, -15.0), ("crow", 32, 64, 64, 128, -30.0)):
         fill(buf, "cst", a, b, c, d, 1, val)
-    for (a, b, c, d), val in (((0, 64, 0, 8 * NK), 0.0), ((0, 32, 0, NK), (24 * MAG + 8) / 32), ((0, 32, NK, 2 * NK), 16 * MAG / 32), ((32, 64, NK, 2 * NK), 8 / 32),
-                              ((0, 32, 4 * NK, 7 * NK), 16 / 32))[:4 + (CFG["sg"] == "S")]:
+    for a, b, c, d, val in ((0, 64, 0, HD, 0.0), (0, 32, 0, NK, (24 * MAG + 8 + 64) / 32), (0, 32, NK, 2 * NK, 16 * MAG / 32), (32, 64, NK, 2 * NK, 8 / 32)):
         fill("cz", "cz", a, b, c, d, 1, val)
     G(128, [], ["pm"], lambda e, p: e.iota(T.pm[:], [[-1, 128]], 2048, 1))
     V(128, 1, ["pm"], ["pm2"], lambda e, p: e.tensor_scalar(T.pm2[:], T.pm[:], 15, None, A.bitwise_and))
@@ -206,200 +190,152 @@ def graph(ctx):
             V(256, 0.5, ["vvb", "omask"], ["R%d" % o], lambda e, p, o=o: e.tensor_scalar(T.R[:, o:2048:8], T.vvb[0:64, :], T.omask[:, o:o + 1], None, A.mult))
     for h in range(2):
         P(16, 64, ["W8"] + ["R%d" % o for o in range(8)], ["vP%d" % h],
-          mms([(cols(0, 64), T.W8[:, 15 - b:143 - b], T.R[:, 128 * b + 64 * h:128 * b + 64 * h + 64]) for b in range(16)]), pool=("N", "vP%d" % h))
-    G(512, [], ["loff"], lambda e, p: e.iota(T.loff[:], [[16, LU], [0, 8]], 0, 0, allow_small_or_imprecise_dtypes=True))
-    for t in range(NT):
-        V(KW, 1, ["vP%d" % (t // 2), "oko"], ["key0%d" % t], lambda e, p, t=t: e.tensor_tensor(kv(0, t, HD, PW), p[:, KW * (t % 2):KW * (t % 2) + KW], T.oko[:], A.add),
-          pool=("N", "vP%d" % (t // 2)), free=2)
-        w = slice(8 * LT * t, 8 * LT * t + 8 * LT)
-        if CFG["pgw"][t] == "G":
-            G(8 * LT, ["pgi%d" % t], ["pgw%d" % t], lambda e, p, w=w: e.affine_select(T.pgw[:, w], T.pgi[:, w], [[0, 8 * LT]], A.is_ge, 0.0, 0, 0))
-        else:
-            V(8 * LT, 1, ["pgi%d" % t], ["pgw%d" % t], lambda e, p, w=w: e.tensor_copy(T.pgw[:, w], T.pgi[:, w]))
-        P(2, 512, ["preb%d" % t, "loff", "cst", "ident"], ["pP%d" % t], mms([(cols(0, 512), T.cst[0:32, :], T.loff[:]), (cols(0, 512), mI(1), T.preb[:, w])]), pool=("A", "pP%d" % t))
-        S(512, 1, ["pP%d" % t], ["prew%d" % t], lambda e, p, w=w: e.activation(T.prew[:, w], p[:, 0:512], ACT.Copy), pool=("A", "pP%d" % t), free=1)
+          mms([(cols(0, 64), T.W8[:, 15 - b:143 - b], T.R[:, 128 * b + 64 * h:128 * b + 64 * h + 64]) for b in range(16)]), pool="vP%d" % h)
+    for u in range(NU):
+        V(KW, 1, ["vP%d" % (u // 2), "oko"], ["kk0%d" % u], lambda e, p, u=u: e.tensor_tensor(kv(0, u, HD, PW), p[:, KW * (u % 2):KW * (u % 2) + KW], T.oko[:], A.add),
+          pool="vP%d" % (u // 2), free=2)
+        V(8 * LU, 1, ["pgi%d" % u], ["win0%d" % u], lambda e, p, u=u: e.tensor_copy(wv(0, u, 0, 8 * LU), part("pgi", u, 8 * LU)))
+        P(DUP, LU, ["limb", "ident"], ["lp%d" % u], lambda e, p, u=u: [e.matmul(p[:, :, j], T.ident[:], part("limb", u, LU), True, True) for j in range(DUP)][-1], fix="LP%d" % u)
 
     for s in range(1, NS):
-        add("G", 500 + 2000 * (s == 1), ["lim0"] + ["loff", "gm", "oko", "g8m", "ident", "cc"] * CFG["limw"], ["sl%d" % s],
-            lambda e, p, s=s: ctx["send"](s, T.limS[:, 256 * s:256 * s + 256], T.limS[:, 0:256], "alim%d" % s), sem="sent", inc=NE, lat=2500, due=CFG["limt"] + 1000 * s)
-        add("W", 0, ["sl%d" % s], ["lim%d" % s], None, sem="alim%d" % s, inc=NE, lat=8000)
+        send(-s, part("XP", s, XW), part("XP", 0, XW), ["X0"] + ["prew0_%d" % u for u in range(NU)], "X%d" % s, CFG["parts"][0], 9000, rel=CFG["big"][s - 1], due=CFG["big"][s - 1] + 2000)
 
-    def begin(s, t):
-        kt, n = "key%d%d" % (s, t), lambda x: "%s%d" % (x, t)
-        ks, eq, lst = T.ks[:, KW * t:KW * t + KW], T.eq[:, KW * t:KW * t + KW], T.lst[:, NK * t:NK * t + NK]
-        w, ln = slice(8 * LT * t, 8 * LT * t + 8 * LT), slice(LT * t, LT * t + LT)
-        us = range(LT * t // LU, (LT * t + LT) // LU)
-        V(KW, 0.5, [kt, "rst"], [n("ks")], lambda e, p: e.tensor_tensor_scan(ks, T.rst[:], kv(s, t, HD, PW), 0.0, A.add, A.min))
-        V(KW, GAT, [kt, n("ks"), "rep7"], [n("eq")], lambda e, p: e.tensor_tensor(eq, ks.indirect(T.rep7[:, 0:KW // 16]), kv(s, t, HD, PW), A.is_equal))
-        P(8, NK, [n("eq"), "lane8"] + [mt(o) for o in range(1, 8)], [n("O")],
-          mms([(cols(0, NK), mI(1), T.lane8[:])] + [(cols(0, NK), mI(o), T.eq[:, KW * t + o:KW * t + KW:8]) for o in range(1, 8)]), pool=("N", n("O")))
-        V(NK, 1, [n("O")], [n("lst")], lambda e, p: e.tensor_copy(lst, p[:, 0:NK]), pool=("N", n("O")), free=1)
-        V(LT, GAT, [n("pgw"), n("lst")], ["c16%d" % u for u in us], lambda e, p: e.tensor_copy(T.c16[:, ln], T.pgw[:, w].indirect(lst)))
-        V(LT, GAT, [n("prew"), n("lst")], [n("p16")], lambda e, p: e.tensor_copy(T.p16[:, ln], T.prew[:, w].indirect(lst)))
-        S(LT, GAT, [n("pgw"), n("lst")], ["cf%d" % u for u in us], lambda e, p: e.activation(T.cf[:, ln], T.pgw[:, w].indirect(lst), ACT.Copy))
-        l0 = LT * t % LB
-        P(DUP, LT, ["lim%d" % s, "ident", n("lst")], [n("lp")], lambda e, p: [e.matmul(p[:, l0:l0 + LT, j], T.ident[:], T.limS[:, 256 * s + LT * t:256 * s + LT * t + LT], True, True)
-                                                                          for j in range(DUP)][-1], fix="LP%d" % (LT * t // LB))
+    def mend(s, u):
+        q = "%d%d" % (s, u)
+        V(NK, 1, ["pl" + q], ["lin%d" % u], lambda e, p: e.tensor_copy(part("lin", u, NK), wv(s, u, 8 * LU + 7, WW, 8)))
+        V(LU, SCAT, ["lin%d" % u, "cin" + q], ["win" + q], lambda e, p: e.tensor_copy(wv(s, u, 0, 8 * LU).indirect(part("lin", u, NK)), part("cin", NU * (s - 1) + u, LU)))
 
-    def step(s, st, u):
-        t = u * LU // LT
-        way = [CFG["way"][(NC * TURN[u][ST * s + st] + c) % len(CFG["way"])] for c in range(NC)]
-        ln = slice(LU * u, LU * u + LU)
-        sgc = ST * LT * t + LT * st + LU * u - LT * t
-        sg, sgt = T.sg[:, sgc:sgc + LU], "sg%d%d" % (u, st)
-        kP, kN = "P%d" % u, "N%d" % u
-        n = lambda x: "%s%d" % (x, u)
-        wide(s, st, u, way)
-        al = lambda x: ["%s%d%d" % (x, u, q) for q in range(4)]
-        red = lambda x, buf: [(cols(0, LU), sel(x, b), buf[:, ln, b]) for b in range(16)]
-        base = lambda k: [(cols(0, LU), T.i5[:], T.cf[:, ln]), (cols(0, LU), T.cst[:], T.crow[:, k:k + LU])]
-        m = 16 // CFG["cutS"]
-        P(5 + m, LU, al("AD") + [n("cf"), "i5", "cst", "W1"], [kP], mms(base(0) + red(1, T.AD)[:m], True, False), pool=("P", kP))
-        for i in range(m, 16, m):
-            P(m, LU, al("AD") + ["W1"], [kP], mms(red(1, T.AD)[i:i + m], False, False), pool=("P", kP))
-        for j in range(0, 16, DUP):
-            P(DUP, LU, ["ni%d%d_%d" % (u, q, j) for q in range(4)] + ["W%d" % BIG], [kP], mms(red(BIG, T.ni)[j:j + DUP], False, j + DUP == 16), pool=("P", kP))
-        if CFG["sg"] == "V":
-            V(LU, 1, [kP], [sgt], lambda e, p: e.tensor_scalar(sg, p[:, 0:LU], 0.0, 2.0, A.is_lt, A.mult), pool=("P", kP), free=2)
+    def begin(s, u):
+        n, q = lambda x: "%s%d" % (x, u), "%d%d" % (s, u)
+        ks, eq, ne, od, lst, keys = part("ks", u, KW), part("eq", u, KW), part("ne", u, KW), part("od", u, KW), part("lst", u, NK), kv(s, u, HD, PW)
+        c16, src = part("c16", u, LU), wv(s, u, 0, 8 * LU) if s else part("pgi", u, 8 * LU)
+        V(KW, 0.5, ["kk" + q, "rst"], [n("ks")], lambda e, p: e.tensor_tensor_scan(ks, T.rst[:], keys, 0.0, A.add, A.min))
+        V(KW, GAT, ["kk" + q, n("ks"), "rep7"], [n("ne")], lambda e, p: e.tensor_tensor(ne, ks.indirect(T.rep7[:]), keys, A.not_equal))
+        V(KW, 1, [n("ne"), "cpl"], ["pl" + q], lambda e, p: e.tensor_tensor_scan(wv(s, u, 8 * LU, WW), ne, T.cpl[:], 0.0, A.mult, A.add))
+        V(NK, 1, ["pl" + q], [n("lst")], lambda e, p: e.tensor_copy(lst, wv(s, u, 8 * LU + 7, WW, 8)))
+        V(LU, GAT, ["win" + q if s else n("pgi"), n("lst")], [n("c16")], lambda e, p: e.tensor_copy(c16, src.indirect(lst)))
+        V(LU, GAT, ["X%d" % s if s else n("prew0_"), n("lst"), "loff"], [n("pf")],
+          lambda e, p: e.tensor_tensor(part("pf", u, LU), T.XP[:, XW * s + 4096 + 8 * LU * u:XW * s + 4096 + 8 * LU * (u + 1)].indirect(lst), T.loff[:], A.add))
+        V(LU, 1, [n("pf")], [n("p16")], lambda e, p: e.tensor_copy(part("p16", u, LU), part("pf", u, LU)))
+        if s and CFG["cfS"]:
+            S(LU, GAT, ["win" + q, n("lst")], [n("cf")], lambda e, p: e.activation(part("cf", u, LU), src.indirect(lst), ACT.Copy))
         else:
-            S(LU, 1, [kP], [sgt], lambda e, p: e.activation(sg, p[:, 0:LU], ACT.Sign, scale=-1.0), pool=("P", kP), free=2)
-        V(LU, 1, [kP, n("cf")] + [sgt] * (CFG["sg"] == "S"), [n("qq")], lambda e, p: e.tensor_tensor(T.qq[:, ln], p[:, 0:LU], T.cf[:, ln], A.max), pool=("P", kP), free=2)
-        P(5, LU, [n("cf"), "i5", "cst", kP], [kN], mms(base(160 * (CFG["sg"] == "V")), True, False), pool=("N", kN))
-        P(1, LU, [sgt, "okw"], [kN], mms([(cols(0, LU), T.okw[:], sg)], False, True), pool=("N", kN))
-        V(LU, 1, [kN, n("qq")], [n("cpp")], lambda e, p: e.tensor_tensor(T.cpp[:, ln], p[:, 0:LU], T.qq[:, ln], A.max), pool=("N", kN), free=1)
-        V(LU, 1, [n("cpp")], [n("ci")], lambda e, p: e.tensor_scalar(T.ci[:, ln], T.cpp[:, ln], 4095, None, A.bitwise_and))
-        if st < ST - 1:
-            V(LU, 1, [n("ci")], [n("c16")], lambda e, p: e.tensor_copy(T.c16[:, ln], T.ci[:, ln]))
-            if CFG["cf"] == "G":
-                G(LU, [n("ci")], [n("cf")], lambda e, p: e.affine_select(T.cf[:, ln], T.ci[:, ln], [[0, LU]], A.is_ge, 0.0, 0, 0))
-            else:
-                V(LU, 1, [n("ci")], [n("cf")], lambda e, p: e.tensor_copy(T.cf[:, ln], T.ci[:, ln]))
+            V(LU, 1, [n("c16")], [n("cf")], lambda e, p: e.tensor_copy(part("cf", u, LU), c16))
+        V(KW, GAT, ["kk" + q, n("ks"), "rep7"], [n("eq")], lambda e, p: e.tensor_tensor(eq, ks.indirect(T.rep7[:]), keys, A.is_equal))
+        V(KW, 0.5, [n("ne"), "co"], [n("od")], lambda e, p: e.tensor_tensor_scan(od, ne, T.co[:], 0.0, A.mult, A.add))
+        k = CFG["grp"]
+        if u % k == k - 1:
+            tiles = lambda z: ["%s%d%d" % (x, z, y) for x in ("win", "pl") for y in range(u + 1 - k, u + 1)]
+            send(-1, wv(s + 1, u + 1 - k, 0, k * WW), wv(s, u + 1 - k, 0, k * WW), tiles(s), "win%d%d" % (s + 1, u + 1 - k), CFG["parts"][1], 3500 + 1000 * k, tiles(s + 1),
+                 due=1e9 if s or u >= k else CFG["first"])
 
-    def pieces(split):
-        out, a = [], 0
-        for x in split:
-            out.append((a, a + int(x)))
-            a += int(x)
-        return out
-
-    def wide(s, st, u, way):
-        t, byP = u * LU // LT, {}
+    def wide(s, st, u):
         n = lambda y, a, b: ["%s%d%d" % (y, u, q) for q in range(a, b)]
-        v = lambda y, a, b: T[y][:, 1024 * u + 256 * a:1024 * u + 256 * b]
-        ln = lambda y, a, b: T[y][:, LU * u + 16 * a:LU * u + 16 * b]
-        for i, (a, b) in enumerate(pieces(CFG["cutF"])):
-            if CFG["fE"][(len(CFG["cutF"]) * TURN[u][ST * s + st] + i) % len(CFG["fE"])] == "V":
-                V(256 * (b - a), GAT, ["X", "c16%d" % u], n("F", a, b), lambda e, p, a=a, b=b: e.tensor_copy(v("F", a, b), T.X[:].indirect(ln("c16", a, b))),
-                  due=at[0] + 256 * a * GAT * CYC)
-                continue
-            S(256 * (b - a), GAT, ["X", "c16%d" % u], n("F", a, b), lambda e, p, a=a, b=b: e.activation(v("F", a, b), T.X[:].indirect(ln("c16", a, b)), ACT.Copy),
+        v = lambda y, a, b: T[y][:, 16 * LU * u + 256 * a:16 * LU * u + 256 * b]
+        ln = lambda a, b: slice(LU * u + 16 * a, LU * u + 16 * b)
+        how = [CFG["copy"][(2 * TURN[u][ST * s + st] + h) % len(CFG["copy"])] for h in range(2)]
+        for a, b in pieces(CFG["cutF"]):
+            S(256 * (b - a), GAT, ["X%d" % s, "c16%d" % u], n("F", a, b), lambda e, p, a=a, b=b: e.activation(v("F", a, b), T.XP[:, XW * s:XW * s + 4096].indirect(T.c16[:, ln(a, b)]), ACT.Copy),
               due=at[0] + 256 * a * GAT * CYC)
-        for i, (a, b) in enumerate(pieces(CFG["cutC"])):
-            how, m = CFG["copy"][(len(CFG["cutC"]) * TURN[u][ST * s + st] + i) % len(CFG["copy"])], 256 * (b - a)
-            if TURN[u][ST * s + st] >= len(CFG["seq"]) - CFG["rush"] or TURN[u][ST * s + st] < CFG["rush0"]:
-                how = CFG["rushc"][i]
-            if how in "PR":
-                byP.update(dict.fromkeys(range(a, b), how))
-            elif how == "Q":
-                add("Q", 60, n("F", a, b), n("F2", a, b), lambda e, p, a=a, b=b: e.dma_start(v("F2", a, b), v("F", a, b)), sem="cp%d" % (4 * u + i), inc=16,
-                    lat=CFG["dma"] * (0.7 + 0.3 * m / 512))
-            elif how == "G":
-                G(m, n("F", a, b), n("F2", a, b), lambda e, p, a=a, b=b, m=m: e.affine_select(v("F2", a, b), v("F", a, b), [[0, m]], A.is_ge, 0.0, 0, 0))
-            else:
-                V(m, 0.5, n("F", a, b), n("F2", a, b), lambda e, p, a=a, b=b: e.tensor_copy(v("F2", a, b), v("F", a, b)))
+        for a, b in pieces(CFG["cutC"]):
+            if how[a // 2] == "G":
+                G(256 * (b - a), n("F", a, b), n("Fc", a, b), lambda e, p, a=a, b=b: e.affine_select(v("F2", a, b), v("F", a, b), [[0, 256 * (b - a)]], A.is_ge, 0.0, 0, 0))
+        for a in (0, 2):
+            if how[a // 2] == "R":
+                k = "B%d%d" % (u, a)
+                S(512, GAT, n("F", 0, a + 2) + ["p16%d" % u], n("D", a, a + 2), lambda e, p, a=a: e.activation(v("D", a, a + 2), v("F", 0, a + 2).indirect(T.p16[:, ln(a, a + 2)]), ACT.Copy))
+                P(1, 512, n("F", a, a + 2) + ["ident"], [k], mms([(cols(0, 512), mI(1), v("F", a, a + 2))], True, False), pool=k)
+                P(1, 512, n("D", a, a + 2) + ["mI1"], [k], mms([(cols(0, 512), mI(-1), v("D", a, a + 2))], False, True), pool=k)
+                S(512, 1, [k], n("AD", a, a + 2), lambda e, p, a=a: e.activation(T.AD[:, ln(a, a + 2), :], p[:, 0:512], ACT.Abs), pool=k, free=1)
         for a, b in pieces(CFG["cutD"]):
-            if a in byP:
-                kD = "B%d%d" % (u, a)
-                if byP[a] == "P":
-                    V(512, GAT, n("F", 0, b) + ["p16%d" % t], n("D", a, b), lambda e, p, a=a, b=b: e.tensor_copy(v("D", a, b), v("F", 0, b).indirect(ln("p16", a, b))))
-                else:
-                    S(512, GAT, n("F", 0, b) + ["p16%d" % t], n("D", a, b), lambda e, p, a=a, b=b: e.activation(v("D", a, b), v("F", 0, b).indirect(ln("p16", a, b)), ACT.Copy))
-                P(1, 512, n("F", a, b) + ["ident"], [kD], mms([(cols(0, 512), mI(1), v("F", a, b))], True, False), pool=("A", kD))
-                P(1, 512, n("D", a, b) + [mt(-1)], [kD], mms([(cols(0, 512), mI(-1), v("D", a, b))], False, True), pool=("A", kD))
-                S(512, 1, [kD], n("AD", a, b), lambda e, p, a=a, b=b: e.activation(T.AD[:, LU * u + 16 * a:LU * u + 16 * b, :], p[:, 0:512], ACT.Abs), pool=("A", kD), free=1)
-                continue
-            V(256 * (b - a), GAT, n("F", 0, b) + n("F2", a, b) + ["p16%d" % t], n("D", a, b),
-              lambda e, p, a=a, b=b: e.tensor_tensor(v("D", a, b), v("F", 0, b).indirect(ln("p16", a, b)), v("F2", a, b), A.subtract))
+            if how[a // 2] == "G":
+                V(256 * (b - a), GAT, n("F", 0, b) + n("Fc", a, b) + ["p16%d" % u], n("D", a, b),
+                  lambda e, p, a=a, b=b: e.tensor_tensor(v("D", a, b), v("F", 0, b).indirect(T.p16[:, ln(a, b)]), v("F2", a, b), A.subtract))
         for a, b in pieces(CFG["cutA"]):
-            if a not in byP:
-                S(256 * (b - a), 1, n("D", a, b), n("AD", a, b), lambda e, p, a=a, b=b: e.activation(T.AD[:, LU * u + 16 * a:LU * u + 16 * b, :], v("D", a, b), ACT.Abs))
+            if how[a // 2] == "G":
+                S(256 * (b - a), 1, n("D", a, b), n("AD", a, b), lambda e, p, a=a, b=b: e.activation(T.AD[:, ln(a, b), :], v("D", a, b), ACT.Abs))
         for a, b in pieces(CFG["cutN"]):
             for j in range(0, 16, DUP):
-                l, l0 = slice(LU * u + 16 * a, LU * u + 16 * b), LU * u % LB
                 V(16 * (b - a) * DUP, 1, n("AD", a, b) + ["lp%d" % u], ["ni%d%d_%d" % (u, q, j) for q in range(a, b)],
-                  lambda e, p, l=l, j=j, m=slice(l0 + 16 * a, l0 + 16 * b): e.tensor_tensor(T.ni[:, l, j:j + DUP], T.AD[:, l, j:j + DUP], p[:, m, :], A.is_gt), fix="LP%d" % (LU * u // LB))
+                  lambda e, p, a=a, b=b, j=j: e.tensor_tensor(T.ni[:, ln(a, b), j:j + DUP], T.AD[:, ln(a, b), j:j + DUP], p[:, 16 * a:16 * b, :], A.is_gt), fix="LP%d" % u)
 
-    def end(s, t):
-        n, q = lambda x: "%s%d" % (x, t), "%d%d" % (s, t)
-        kt = "key" + q
-        us = range(LT * t // LU, (LT * t + LT) // LU)
-        pay = lambda a, b: T.pay[:, PW * (NT * s + t) + a:PW * (NT * s + t) + b]
-        fx = lambda k: T.fx[:, NK * (ST * t + k):NK * (ST * t + k + 1)]
-        hn = lambda k: T.hn[:, NK * (2 * t + k):NK * (2 * t + k + 1)]
-        eq, tt, lst = T.eq[:, KW * t:KW * t + KW], T.tt[:, KW * t:KW * t + KW], T.lst[:, NK * t:NK * t + NK]
+    def step(s, st, u):
+        n, ln = lambda x: "%s%d" % (x, u), slice(LU * u, LU * u + LU)
+        sg, sgt, kP, kN = part("sg", ST * u + st, LU), "sg%d%d" % (u, st), n("P"), n("N")
+        wide(s, st, u)
+        al = ["AD%d%d" % (u, q) for q in range(4)]
+        red = lambda x, buf: [(cols(0, LU), sel(x, b), buf[:, ln, b]) for b in range(16)]
+        base = lambda k: [(cols(0, LU), T.i5[:], T.cf[:, ln]), (cols(0, LU), T.cst[:], part("crow", k, LU))]
+        m = 16 // CFG["cutS"]
+        P(5, LU, al[:2] + [n("cf"), "i5", "cst"], [kP], mms(base(0), True, False), pool=kP)
+        for i in range(0, 16, m):
+            P(m, LU, al + ["W0"], [kP], mms(red(1, T.AD)[i:i + m], False, False), pool=kP)
+        for j in range(0, 16, DUP):
+            P(DUP, LU, ["ni%d%d_%d" % (u, q, j) for q in range(4)] + ["W1"], [kP], mms(red(BIG, T.ni)[j:j + DUP], False, j + DUP == 16), pool=kP)
+        V(LU, 1, [kP], [sgt], lambda e, p: e.tensor_scalar(sg, p[:, 0:LU], 0.0, 2.0, A.is_lt, A.mult), pool=kP, free=2)
+        V(LU, 1, [kP, n("cf")], [n("qq")], lambda e, p: e.tensor_tensor(T.qq[:, ln], p[:, 0:LU], T.cf[:, ln], A.max), pool=kP, free=2)
+        P(5, LU, [n("cf"), "i5", "cst", kP], [kN], mms(base(1), True, False), pool=kN)
+        P(1, LU, [sgt, "okw"], [kN], mms([(cols(0, LU), T.okw[:], sg)], False, True), pool=kN)
+        V(LU, 1, [kN, n("qq")], [n("cpp")], lambda e, p: e.tensor_tensor(T.cpp[:, ln], p[:, 0:LU], T.qq[:, ln], A.max), pool=kN, free=1)
+        if st < ST - 1:
+            V(LU, 1, [n("cpp")], [n("ci")], lambda e, p: e.tensor_scalar(T.ci[:, ln], T.cpp[:, ln], 4095, None, A.bitwise_and))
+            V(LU, 1, [n("ci")], [n("c16")], lambda e, p: e.tensor_copy(T.c16[:, ln], T.ci[:, ln]))
+            V(LU, 1, [n("ci")], [n("cf")], lambda e, p: e.tensor_copy(T.cf[:, ln], T.ci[:, ln]))
+        else:
+            co = part("cout", NU * s + u, LU)
+            V(LU, 1, [n("cpp")], ["cout%d%d" % (s, u)], lambda e, p: e.tensor_scalar(co, T.cpp[:, ln], 4095, None, A.bitwise_and))
+            send(-1, part("cin", NU * s + u, LU), co, ["cout%d%d" % (s, u)], "cin%d%d" % (s + 1, u), CFG["parts"][2], CFG["send"])
+
+    def end(s, u):
+        n, q, r = lambda x: "%s%d" % (x, u), "%d%d" % (s, u), "%d%d" % (s + 1, u)
+        fx, hn = lambda k: part("fx", ST * u + k, NK), lambda k: part("hn", 2 * u + k, NK)
         kL, kZ = n("L"), n("Z")
         d, g8, mc = cols(0, NK), cols(NK, 2 * NK), cols(2 * NK, 3 * NK)
-        P(17, ST * NK, ["sg%d%d" % (u, k) for u in us for k in range(ST)] + ["W1", "cz", "ones"], [kL],
-          mms([(cols(0, ST * NK), T.ones[0:64, :], T.cz[:, 4 * NK:7 * NK])] * (CFG["sg"] == "S") +
-              [(cols(0, ST * NK), sel(1, b), T.sg[:, ST * LT * t + b:ST * LT * (t + 1):16]) for b in range(16)]), pool=("N", kL))
-        P(11, NK, [kL, kt, n("ks"), n("eq"), "cz", "ones"] + [mt(o) for o in (1, 2, 3, 4, 5, 6, 7, -1)], [kZ],
-          mms([(cols(0, HD), T.ones[0:64, :], T.cz[:, 0:HD]), (d, mI(1), kv(s, t, NK, 2 * NK)), (cols(NK, 3 * NK), mI(1), kv(s, t, NK, 3 * NK)),
-               (d, mI(-1), T.ks[:, KW * t + 7:KW * t + KW:8])] + [(d, mI(o), T.eq[:, KW * t + o:KW * t + KW:8]) for o in range(1, 8)], True, False), pool=("N", kZ))
-        S(ST * NK, 1, [kL], [n("fx")], lambda e, p: e.activation(T.fx[:, ST * NK * t:ST * NK * (t + 1)], p[:, 0:ST * NK], ACT.Relu, bias=-31.0), pool=("N", kL))
-        P(3, NK, [n("fx"), "same1"], [kL], mms([(cols(ST * NK, (ST + 1) * NK), T.same[:, 0:128], fx(k)) for k in range(ST)]), pool=("N", kL))
-        P(9, NK, [n("fx"), "same8", "ident", kL], [kZ], mms([(o, l, fx(k)) for k in range(ST) for o, l in ((d, T.same[:, 128:256]), (g8, T.same[:, 128:256]), (mc, mI(1)))], False, False),
-          pool=("N", kZ))
-        S(2 * NK, 1, [kL], [n("hn")], lambda e, p: e.activation(T.hn[:, 2 * NK * t:2 * NK * (t + 1)], p[:, (ST - 1) * NK:(ST + 1) * NK], ACT.Identity, scale=0.5, bias=MAG - 0.25),
-          pool=("N", kL), free=1)
-        P(3, NK, [n("hn"), mt(-8), mt(-16)], [kZ], mms([(d, mI(-8), hn(0)), (d, mI(-16), hn(1)), (g8, mI(-16), hn(1))], False, True), pool=("N", kZ))
-        if CFG["head"] == "V":
-            V(3 * NK, 1, [kZ], ["payh" + q], lambda e, p: e.tensor_copy(pay(0, HD), p[:, 0:HD]), pool=("N", kZ), free=1)
-        else:
-            S(3 * NK, 1, [kZ], ["payh" + q], lambda e, p: e.activation(pay(0, HD), p[:, 0:HD], ACT.Copy), pool=("N", kZ), free=1)
-        V(KW, GAT, ["payh" + q, n("eq"), "repk"], [n("tt")], lambda e, p: e.tensor_tensor(tt, pay(0, HD).indirect(T.repk[:, 0:KW // 16]), eq, A.mult))
-        V(KW, 2, [kt, n("tt")], ["pay" + q], lambda e, p: e.tensor_tensor(pay(HD, PW), kv(s, t, HD, PW), tt, A.add))
-        add("G", 500, ["pay" + q, "payh" + q], ["snd" + q], lambda e, p: ctx["send"](1, kv(s + 1, t, 0, PW), pay(0, PW), "akey%d%d" % (s + 1, t)), sem="sent", inc=NE, lat=CFG["send"] - 500)
-        add("W", 0, ["snd" + q], ["key%d%d" % (s + 1, t)], None, sem="akey%d%d" % (s + 1, t), inc=NE)
-        V(LT, 3.5, [n("lst")] + ["ci%d" % u for u in us], [n("pgw")],
-          lambda e, p: e.tensor_copy(T.pgw[:, 8 * LT * t:8 * LT * (t + 1)].indirect(lst), T.ci[:, LT * t:LT * t + LT]))
+        P(16, ST * NK, ["sg%d%d" % (u, k) for k in range(ST)] + ["W0"], [kL], mms([(cols(0, ST * NK), sel(1, b), part("sg", u, ST * LU, b, 16)) for b in range(16)]), pool=kL)
+        P(5, NK, [kL, "kh" + q, n("ks"), n("od"), "cz", "ones", "ident", "mI1"], [kZ],
+          mms([(cols(0, HD), T.ones[0:64, :], T.cz[:]), (d, mI(1), kv(s, u, NK, 2 * NK)), (cols(NK, 3 * NK), mI(1), kv(s, u, NK, 3 * NK)),
+               (d, mI(-1), part("ks", u, KW, 7, 8)), (d, mI(1), part("od", u, KW, 7, 8))], True, False), pool=kZ)
+        S(ST * NK, 1, [kL], [n("fx")], lambda e, p: e.activation(part("fx", u, ST * NK), p[:, 0:ST * NK], ACT.Relu, bias=-31.0), pool=kL)
+        P(3, NK, [n("fx"), "same1"], [kL], mms([(cols(ST * NK, (ST + 1) * NK), T.same[:, 0:128], fx(k)) for k in range(ST)]), pool=kL)
+        P(9, NK, [n("fx"), "same8", kL], [kZ], mms([(o, l, fx(k)) for k in range(ST) for o, l in ((d, T.same[:, 128:256]), (g8, T.same[:, 128:256]), (mc, mI(1)))], False, False), pool=kZ)
+        S(2 * NK, 1, [kL], [n("hn")], lambda e, p: e.activation(part("hn", u, 2 * NK), p[:, (ST - 1) * NK:(ST + 1) * NK], ACT.Identity, scale=0.5, bias=MAG - 0.25), pool=kL, free=1)
+        P(3, NK, [n("hn"), "mI8", "mI16"], [kZ], mms([(d, mI(-8), hn(0)), (d, mI(-16), hn(1)), (g8, mI(-16), hn(1))], False, True), pool=kZ)
+        S(HD, 1, [kZ], ["kh" + r], lambda e, p: e.activation(kv(s + 1, u, 0, HD), p[:, 0:HD], ACT.Copy), pool=kZ, free=1)
+        V(KW, GAT, ["kh" + r, n("eq"), "repk"], [n("tt")], lambda e, p: e.tensor_tensor(part("tt", u, KW), kv(s + 1, u, 0, HD).indirect(T.repk[:]), part("eq", u, KW), A.mult))
+        V(KW, 2, ["kk" + q, n("tt")], ["kk" + r], lambda e, p: e.tensor_tensor(kv(s + 1, u, HD, PW), kv(s, u, HD, PW), part("tt", u, KW), A.add))
 
-    def final(t):
-        n, kt = lambda x: "%s%d" % (x, t), "key%d%d" % (NS, t)
-        fa, fv = T.fa[:, KW * t:KW * t + KW], T.fv[:, KW * t:KW * t + KW]
-        w = slice(8 * LT * t, 8 * LT * (t + 1))
-        add("Q", 60, [n("pgw")] + ["snd%d%d" % (NS - 1, t)] * CFG["ygw"], [], lambda e, p: e.dma_start(T.yg[:, w], T.pgw[:, w]), sem="outs", inc=16, lat=3000)
-        V(KW, GAT, [kt, "ook", "perm"], [n("fa")], lambda e, p: e.tensor_tensor(fa, kv(NS, t, HD, PW).indirect(T.turn8[:, 0:KW // 16]), T.ook[:], A.subtract))
-        V(KW, GAT, [kt, n("fa"), "repg"], [n("fv")], lambda e, p: e.tensor_tensor(fv, kv(NS, t, 0, HD).indirect(T.repg[:, 0:KW // 16]), fa, A.subtract))
+    def final(u):
+        n, q = lambda x: "%s%d" % (x, u), "%d%d" % (NS, u)
+        mend(NS, u)
+        add("Q", 60, ["win" + q], [], lambda e, p: e.dma_start(T.yg[:, 8 * LU * u:8 * LU * (u + 1)], wv(NS, u, 0, 8 * LU)), sem="outs", inc=16, lat=2500)
+        V(KW, GAT, ["kh" + q, "kk" + q, "repg"], [n("fv")], lambda e, p: e.tensor_tensor(part("fv", u, KW), kv(NS, u, 0, HD).indirect(T.repg[:]), kv(NS, u, HD, PW), A.subtract))
         for c in range(2):
-            k = "Y%d%d" % (t, c)
-            P(4, 64, [n("fv"), "ident"], [k], lambda e, p, c=c: [e.matmul(p[0:8, b:256:16], T.ident[:, b:128:16], T.fv[:, KW * t + 16 * c:KW * t + 16 * c + 16], True, True)
-                                                               for b in range(16)][-1], pool=("A", k))
-            y = T.yvs[:, 8 * LT * t + 256 * c:8 * LT * t + 256 * c + 256]
+            k, y = "Y%d%d" % (u, c), part("yvs", 2 * u + c, 256)
+            P(1, 256, ["kh" + q, "cst", "orow"], [k], lambda e, p, c=c: e.matmul(p[0:8, 0:256], T.cst[0:32, 0:8], part("orow", c, 256), True, False), pool=k)
+            P(8, 64, [n("fv"), "ident"], [k], lambda e, p, c=c: [e.matmul(p[0:8, 16 * j + b:256:LU], T.ident[:, b:128:16], part("fv", 8 * u + 2 * j + c, 4), False, b == 15 and j == NK - 1)
+                                                               for b in range(16) for j in range(NK)][-1], pool=k)
             if c:
-                V(256, 1, [k], ["yv%d%d" % (t, c)], lambda e, p, y=y: e.tensor_scalar(y, p[0:8, 0:256], 0.125, None, A.mult), pool=("A", k), free=1)
+                V(256, 1, [k], ["yv%d%d" % (u, c)], lambda e, p, y=y: e.tensor_scalar(y, p[0:8, 0:256], 0.125, None, A.mult), pool=k, free=1)
             else:
-                S(256, 1, [k], ["yv%d%d" % (t, c)], lambda e, p, y=y: e.activation(y, p[0:8, 0:256], ACT.Copy, scale=0.125), pool=("A", k), free=1)
-        add("Q", 60, ["yv%d%d" % (t, c) for c in range(2)], [], lambda e, p: e.dma_start(T.yv[:, LT * t:LT * t + LT], T.yvs[:, w]), sem="outs", inc=16, lat=2200)
-        P(4, 64, [kt, "ident"], [n("M")], lambda e, p: [e.matmul(p[0:8, b:LT:16], T.ident[:, b:128:16], kv(NS, t, 2 * NK, 3 * NK), True, True) for b in range(16)][-1], pool=("N", n("M")))
-        S(LT, 1, [n("M")], [n("ym")], lambda e, p: e.activation(T.yms[:, LT * t:LT * t + LT], p[0:8, 0:LT], ACT.Copy), pool=("N", n("M")), free=1)
-
-    def due(s, st, u):
-        return CFG["t0"] + CFG["slot"] * (TURN[u][ST * s + st] + CFG["shift"][ST * u + st])
+                S(256, 1, [k], ["yv%d%d" % (u, c)], lambda e, p, y=y: e.activation(y, p[0:8, 0:256], ACT.Copy, scale=0.125), pool=k, free=1)
+        add("Q", 60, ["yv%d%d" % (u, c) for c in range(2)], [], lambda e, p: e.dma_start(T.yv[:, LU * u:LU * u + LU], part("yvs", u, 8 * LU)), sem="outs", inc=16, lat=2000)
+        P(4, 64, ["kh" + q, "ident"], [n("M")], lambda e, p: [e.matmul(p[0:8, b:LU:16], T.ident[:, b:128:16], kv(NS, u, 2 * NK, 3 * NK), True, True) for b in range(16)][-1], pool=n("M"))
+        S(LU, 1, [n("M")], [n("ym")], lambda e, p: e.activation(part("yms", u, LU), p[0:8, 0:LU], ACT.Identity, bias=64.0), pool=n("M"), free=1)
 
     for s in range(NS):
-        for t in range(NT):
-            u0 = LT * t // LU
-            begin(s, t)
+        for u in range(NU):
+            if s:
+                mend(s, u)
+            begin(s, u)
             for st in range(ST):
-                for u in range(u0, u0 + LT // LU):
-                    at[0] = due(s, st, u)
-                    step(s, st, u)
-            end(s, t)
-    for t in range(NT):
-        at[1] = END - CFG["early"] * (len(CFG["seq"]) - 1 - TURN[t][-1])
-        final(t)
+                at[0], at[2] = CFG["t0"] + CFG["slot"] * (TURN[u][ST * s + st] + CFG["shift"][ST * u + st]), st
+                step(s, st, u)
+            end(s, u)
+    for u in range(NU):
+        at[1] = END - CFG["early"] * (len(CFG["seq"]) - 1 - TURN[u][-1])
+        final(u)
     at[1] = END
-    add("Q", 60, ["ym%d" % t for t in range(NT)], [], lambda e, p: e.dma_start(T.ym[:], T.yms[:]), sem="outs", inc=16, lat=2200)
+    add("Q", 60, ["ym%d" % u for u in range(NU)], [], lambda e, p: e.dma_start(T.ym[:], T.yms[:]), sem="outs", inc=16, lat=2000)
     return ops
 
 
@@ -432,27 +368,27 @@ def plan(ops):
     for i in range(n):
         for d in dep[i]:
             succ[d].append(i)
-    pr = [0.0] * n
+    span = [o["cost"] + o["lat"] + wake for o in ops]
+    late, soon = [0.0] * n, [0.0] * n
     for i in reversed(range(n)):
-        pr[i] = min(ops[i]["due"], min([pr[x] for x in succ[i]] + [ops[i]["end"]]) - ops[i]["cost"] - ops[i]["lat"] - wake)
-    es = [0.0] * n
+        late[i] = min(ops[i]["due"], min([late[x] for x in succ[i]] + [ops[i]["end"]]) - span[i])
     for i in range(n):
-        es[i] = ops[i]["due"] if ops[i]["due"] < 1e8 else max([es[d] + ops[d]["cost"] + ops[d]["lat"] + wake for d in dep[i]] + [0.0])
-    pr = [pr[i] if pr[i] < CFG["t0"] else pr[i] + CFG["mix"] * min(0.0, max(es[i] - pr[i], -CFG["cap"])) for i in range(n)]
-    pr = [pr[i] + CFG["bias"].get((ops[i]["wr"] + [""])[0].rstrip("0123456789"), 0.0) for i in range(n)]
+        soon[i] = ops[i]["due"] if ops[i]["due"] < 1e8 else max([soon[d] + span[d] for d in dep[i]] + [0.0])
+    pr = [late[i] if late[i] < CFG["t0"] else late[i] + CFG["mix"] * min(0.0, max(soon[i] - late[i], -CFG["cap"])) for i in range(n)]
+    kind = [(o["wr"] + [""])[0].rstrip("0123456789_") for o in ops]
+    pr = [pr[i] + CFG["bias"].get(kind[i], 0.0) + CFG["bias"].get("%s@%d" % (kind[i], ops[i]["st"]), 0.0) for i in range(n)]
     done, start, buf = [0.0] * n, [0.0] * n, {}
     free = {e: 0.0 for e in "VSPGQW"}
-    slot = {k: [0.0] * len(v) for k, v in POOLS.items()}
-    held, fin = {}, {}
+    slot, held, fin = [0.0] * len(BANKS), {}, {}
     ready = [i for i in range(n) if not need[i]]
-    can, order = [o["due"] - CFG["hold"] if o["due"] < 1e8 else 0.0 for o in ops], []
+    can, order = [o["rel"] for o in ops], []
     while ready:
         best = {}
         for i in ready:
             o = ops[i]
             t = max(can[i], free[o["eng"]] if o["eng"] != "W" else 0.0)
             if o["pool"] and o["pool"] not in held:
-                fr = [x for x in slot[o["pool"][0]] if x is not None]
+                fr = [x for x in slot if x is not None]
                 if not fr:
                     continue
                 t = max(t, min(fr))
@@ -460,36 +396,35 @@ def plan(ops):
         cand = None
         for e, lst in best.items():
             t0 = min(lst)[0]
-            pick = min((pr[i], t, i) for t, i in lst if t <= t0 + CFG["look"].get(e, 0.0))
+            pick = min((pr[i], t, i) for t, i in lst if t <= t0)
             d = ops[pick[2]]["cost"]
-            soon = min((pr[i], t, i) for t, i in lst if t <= pick[1] + d)
-            if soon[0] < pick[0] - CFG["gap"] and CFG["idle"].get(e):
-                fit = [(pr[i], t, i) for t, i in lst if t + ops[i]["cost"] <= soon[1] + CFG["tol"] and i != soon[2]]
+            near = min((pr[i], t, i) for t, i in lst if t <= t0 + d)
+            if near[0] < pick[0] - CFG["gap"] and CFG["idle"].get(e):
+                fit = [(pr[i], t, i) for t, i in lst if t + ops[i]["cost"] <= near[1] + CFG["tol"] and i != near[2]]
                 if fit:
                     pick = min(fit)
-                elif soon[1] - pick[1] <= CFG["idle"][e] * (pick[1] + d - soon[1]):
-                    pick = soon
+                elif near[1] - t0 <= CFG["idle"][e] * (t0 + d - near[1]):
+                    pick = near
             if cand is None or pick[1] < cand[0]:
                 cand = (pick[1], pick[2])
         t, i = cand
         o = ops[i]
         ready.remove(i)
-        if o["pool"]:
-            k = o["pool"]
+        k = o["pool"]
+        if k:
             if k not in held:
-                held[k] = min((x, y) for y, x in enumerate(slot[k[0]]) if x is not None)[1]
-                slot[k[0]][held[k]] = None
-            buf[i] = POOLS[k[0]][held[k]]
+                held[k] = min((x, y) for y, x in enumerate(slot) if x is not None)[1]
+                slot[held[k]] = None
+            buf[i] = BANKS[held[k]]
         if o["fix"]:
             buf[i] = o["fix"]
         start[i] = t
         done[i] = t + o["cost"] + o["lat"]
         free[o["eng"]] = t + o["cost"]
-        if o["pool"] and o["free"]:
-            ends = fin.setdefault(o["pool"], []) + [done[i] + wake]
-            fin[o["pool"]] = ends
-            if len(ends) == o["free"]:
-                slot[o["pool"][0]][held.pop(o["pool"])] = max(fin.pop(o["pool"]))
+        if k and o["free"]:
+            fin[k] = fin.get(k, []) + [done[i] + wake]
+            if len(fin[k]) == o["free"]:
+                slot[held.pop(k)] = max(fin.pop(k))
         order.append(i)
         for x in succ[i]:
             need[x] -= 1
@@ -512,10 +447,9 @@ def emit(g, T, ops, order, buf):
         d = set(dep[i])
         b = buf.get(i)
         if b:
-            for k in o["bk"]:
-                use = bank.setdefault((b, k), {})
-                d.update(v for x, v in use.items() if x != o["eng"])
-                use[o["eng"]] = i
+            use = bank.setdefault(b, {})
+            d.update(v for x, v in use.items() if x != o["eng"])
+            use[o["eng"]] = i
         if o["eng"] == "W":
             at[i] = (o["sem"], o["inc"])
             after[i] = {o["sem"]: o["inc"]}
@@ -548,12 +482,14 @@ def rank_program(g, core, T, topo):
         return
     cores = T.cores
 
-    def send(d, out, inp, sem):
-        dst = cores[(rank + d) % len(cores)]
-        rid, pid = topo.addr(dst)[:2]
-        return g.remote_dma(out, inp, T.sem[sem], T.sem["sent"], pid, rid, topo.mask(core, dst))
+    def engines(d, part):
+        e = topo.engines(core, cores[(rank + d) % len(cores)])
+        return (e, e[:len(e) // 2], e[len(e) // 2:])[part]
 
-    ne = len(topo.engines(core, cores[(rank + 1) % len(cores)]))
-    ops = graph({"T": T, "send": send, "NE": ne})
+    def send(d, out, inp, sem, part):
+        rid, pid = topo.addr(cores[(rank + d) % len(cores)])[:2]
+        return g.remote_dma(out, inp, T.sem[sem], T.sem["sent"], pid, rid, sum(1 << e for e in engines(d, part)))
+
+    ops = graph({"T": T, "send": send, "engines": lambda part: len(engines(-1, part))})
     order, buf, start, done = plan(ops)
     emit(g, T, ops, order, buf)

from concourse.mybir import AluOpType, ActivationFunctionType

ACT = ActivationFunctionType
NS, ST, NL = 4, 3, 256
LU, NU = 64, 4
NK = LU // 16
KW, HD = 8 * NK, 16
PW = HD + KW
WW = 8 * LU + KW
XW = 4096 + 8 * NL
BIG = 65536
OFF = 491520
MAG = 129
DUP = 8

CFG = dict(seq="ABCABDACBDCADBACBDACBDCADBACBDACBDCADBACBDACDBCD", t0=7500.0, slot=3000.0, shift=(0,) * 12, tail=9000.0, early=0.0,
           copy="RGGGGG", cutF="22", cutC="22", cutD="22", cutA="22", cutN="22", cutS=2, cfS=1,
           loads="pg0 xt pre0 lim pg1 pre1 pg2 pre2 pg3 pre3", ld=0.72, rS=2, big=(13000.0, 46000.0, 80000.0), parts=(0, 0, 0), first=6000.0, grp=2, one="win10",
           gat=1.5, wake=190.0, send=2600.0, vfix=5, sfix=10, mix=0.85, cap=5000.0, idle={"P": 0.8, "V": 0.15, "S": 0.15}, gap=0.0, tol=60.0, bias={})
CFG.update({'seq': 'ABCD' * 12, 'slot': 2900, 'grp': 4, 'big': (11000.0, 16000.0, 21000.0), 'mix': 0.75, 'tol': 30.0, 'early': 400.0, 'tail': 11000.0, 'gat': 1.55, 'first': 6000,
            'bias': {'sg': -300, 'N': -300, 'cpp': -300, 'ci': -300, 'c': -300, 'cout': -300, 'p': -300, 'Fc': 900, 'od': -4200, 'B': -300, 'eq': 2400, 'cf': 300, 'sndwin': -1200},
            'idle': {'P': 0.15, 'V': 0.15, 'S': 0.15, 'G': 0.8}, 'shift': [0, 0, -0.25, 0, 0.25, 0, -0.25, 0, 0, 0, 0, 0], 'loads': 'pg0 xt pg1 pre0 lim pre1 pg2 pre2 pg3 pre3'})
TURN = [[i for i, x in enumerate(CFG["seq"]) if x == "ABCD"[u]] for u in range(NU)]
END = CFG["t0"] + CFG["slot"] * (len(CFG["seq"]) - 1) + CFG["tail"]

B16, F32, I32, U16 = "bfloat16", "float32", "int32", "uint16"
SCRATCH = {}
for _n, _p, _w, _d in (
        ("XP", 128, NS * XW, B16), ("win", 128, (NS + 1) * NU * WW, F32),
        ("cout", 128, NS * NL, I32), ("cin", 128, NS * NL, I32), ("lin", 128, NU * NK, U16),
        ("pgi", 128, 8 * NL, I32), ("pf", 128, NL, F32), ("loff", 128, LU, F32), ("limb", 128, NL, B16),
        ("vvi", 128, NL, I32), ("vvb", 128, NL, B16), ("R", 64, 8 * NL, B16),
        ("ones", 128, 128, B16), ("ident", 128, 128, B16), ("mI", 128, 3 * 128, B16), ("i5", 128, 128, F32),
        ("gA", 128, 128, B16), ("gm", 128, 128, B16), ("okw", 128, 128, B16), ("W", 128, 2 * 144, B16),
        ("g8A", 64, 8, B16), ("g8m", 64, 8, B16), ("W8", 64, 144, B16), ("cst", 64, 128, B16), ("crow", 64, 128, B16), ("cz", 64, HD, B16),
        ("pm", 128, 128, I32), ("pm2", 128, 128, I32), ("same", 128, 256, B16),
        ("om", 64, 8, I32), ("om2", 64, 8, I32), ("omask", 64, 8, F32),
        ("vp", 128, 16, I32), ("vp2", 128, 16, I32), ("vperm", 128, 16, U16),
        ("p1", 128, 2, I32), ("p8", 128, 2, I32), ("bi", 128, 4, I32), ("bf", 128, 4, F32), ("cc", 128, 4, I32),
        ("rep7", 128, 2, U16), ("repk", 128, 2, U16), ("repg", 128, 2, U16), ("lane8", 128, NK, B16),
        ("rst", 128, KW, B16), ("cpl", 128, KW, F32), ("co", 128, KW, B16), ("oko", 128, KW, B16), ("orow", 32, 8 * LU, B16),
        ("keys", 128, (NS + 1) * NU * PW, B16), ("ks", 128, NU * KW, B16), ("eq", 128, NU * KW, B16), ("ne", 128, NU * KW, B16), ("od", 128, NU * KW, B16),
        ("tt", 128, NU * KW, B16), ("fv", 128, NU * KW, B16), ("lst", 128, NU * NK, U16),
        ("fx", 128, NU * ST * NK, B16), ("hn", 128, NU * 2 * NK, B16), ("sg", 128, ST * NL, B16), ("yvs", 8, 8 * NL, F32), ("yms", 8, NL, F32),
        ("c16", 128, NL, U16), ("p16", 128, NL, U16), ("cf", 128, NL, F32), ("ci", 128, NL, I32), ("cpp", 128, NL, I32), ("qq", 128, NL, F32),
        ("F", 128, 16 * NL, B16), ("F2", 128, 16 * NL, B16), ("D", 128, 16 * NL, B16)):
    SCRATCH[_n] = ("sbuf", [_p, _w], _d)
for _n in ("AD", "ni"):
    SCRATCH[_n] = ("sbuf", [128, NL, 16], B16)
for _u in range(NU):
    SCRATCH["LP%d" % _u] = ("psum", [128, LU, DUP], F32)
BANKS = ["PB%d" % _i for _i in range(8 - NU)]
for _b in BANKS:
    SCRATCH[_b] = ("psum", [128, 512], F32)

SEMAPHORES = ["cV", "cS", "cP", "cG", "lvv", "llim", "lxt", "outs", "sent"] + ["lpg%d" % u for u in range(NU)] + ["lpre%d" % u for u in range(NU)]
SEMAPHORES += ["aX%d" % s for s in range(1, NS)] + ["a%s%d%d" % (x, s, u) for x, k in (("win", CFG["grp"]), ("cin", 1)) for s in range(1, NS + 1) for u in range(0, NU, k)]

CYC, PEC = 0.83, 0.42


def graph(ctx):
    T, A = ctx["T"], AluOpType
    GAT, SCAT = CFG["gat"], 3.8
    ops, at = [], [0.0, END, 0]

    def add(eng, cost, rd, wr, fn, pool=None, free=None, sem=None, inc=None, lat=0.0, due=1e9, fix=None, rel=0.0):
        ops.append(dict(eng=eng, cost=cost, rd=rd, wr=wr, fn=fn, pool=pool, free=free, sem=sem, inc=inc, lat=lat, due=due, fix=fix, rel=rel, end=at[1], st=at[2]))

    def V(n, cyc, rd, wr, fn, **k):
        add("V", 50 + n * cyc * CYC if cyc in (GAT, SCAT) else CFG["vfix"] + max(64, n * cyc) * CYC, rd, wr, fn, **k)

    def S(n, cyc, rd, wr, fn, **k):
        add("S", 65 + n * cyc * CYC if cyc == GAT else CFG["sfix"] + max(64, n * cyc) * CYC, rd, wr, fn, **k)

    def P(k, n, rd, wr, fn, **kw):
        add("P", k * max(64, n) * PEC, rd, wr, fn, **kw)

    def G(n, rd, wr, fn, **k):
        add("G", 150 + 2 * n * CYC, rd, wr, fn, **k)

    def load(out, inp, tile, sem, lat):
        add("Q", 60, [], [tile], lambda e, p: e.dma_start(out, inp), sem=sem, inc=16, lat=lat, due=len(ops) - 1e9)

    def send(d, out, inp, rd, tile, part, lat, tiles=(), **k):
        n = ctx["engines"](part)
        add("G", 500 + 2000 * (tile == CFG["one"]), rd, ["snd" + tile], lambda e, p: ctx["send"](d, out, inp, "a" + tile, part), sem="sent", inc=n, lat=lat - 500, **k)
        add("W", 0, ["snd" + tile], list(tiles) or [tile], None, sem="a" + tile, inc=n)

    def fill(buf, tile, a, b, c, d, step, val):
        V(len(range(c, d, step)), 0.5, [], [tile] if isinstance(tile, str) else tile, lambda e, p: e.memset(T[buf][a:b, c:d:step], val))

    def mms(lst, start=True, stop=True):
        def fn(e, p):
            for i, (o, l, r) in enumerate(lst):
                x = e.matmul(p[o], l, r, start and i == 0, stop and i == len(lst) - 1)
            return x
        return fn

    def cols(a, b):
        return (slice(None), slice(a, b))

    def kv(s, u, a, b):
        return T.keys[:, (NU * s + u) * PW + a:(NU * s + u) * PW + b]

    def wv(s, u, a, b, c=None):
        return T.win[:, (NU * s + u) * WW + a:(NU * s + u) * WW + b:c]

    def part(buf, u, w, a=0, c=None):
        return T[buf][:, w * u + a:w * u + w:c]

    MUL = (-1, -8, -16)

    def mI(x):
        return T.ident[:] if x == 1 else part("mI", MUL.index(x), 128)

    def sel(x, b):
        return T.W[:, 144 * (x != 1) + 15 - b:144 * (x != 1) + 143 - b]

    def pieces(split):
        ends = [sum(int(x) for x in split[:i]) for i in range(len(split) + 1)]
        return list(zip(ends, ends[1:]))

    load(T.vvi[0:64, :], T.vv[:], "vvi", "lvv", 2000)
    lat = 1800
    for x in CFG["loads"].split():
        out, inp, tile, dt = {"pg": (T.pgi, T.pg, "pgi", 1200), "pr": (T.XP, T.pre, "prew0_", 800), "li": (T.limb, T.lim, "limb", 600), "xt": (T.XP, T.xt, "X0", 3700)}[x[:2]]
        w = slice(8 * LU * int(x[-1]), 8 * LU * int(x[-1]) + 8 * LU) if x[-1].isdigit() else slice(0, inp.shape[1])
        a = 4096 * (x[:2] == "pr")
        lat += dt * CFG["ld"]
        load(out[:, a + w.start:a + w.stop], inp[:, w], tile + x[-1] * x[-1].isdigit(), "l" + x, lat)

    V(128, 0.5, [], ["ones"], lambda e, p: e.memset(T.ones[:], 1.0))
    V(256, 1, [], ["vvu"], lambda e, p: e.memset(T.vvi[64:128, :], 0))
    G(16, [], ["vp"], lambda e, p: e.iota(T.vp[:], [[1, 16]], 0, 16))
    V(16, 1, ["vp"], ["vp2"], lambda e, p: e.tensor_scalar(T.vp2[:], T.vp[:], 255, None, A.bitwise_and))
    V(16, 1, ["vp2"], ["vperm"], lambda e, p: e.tensor_copy(T.vperm[:], T.vp2[:]))
    G(8, [], ["om"], lambda e, p: e.iota(T.om[:], [[-1, 8]], 8, 1))
    V(8, 1, ["om"], ["om2"], lambda e, p: e.tensor_scalar(T.om2[:], T.om[:], 7, None, A.bitwise_and))
    V(8, 1, ["om2"], ["omask"], lambda e, p: e.tensor_scalar(T.omask[:], T.om2[:], 0.0, None, A.is_equal))
    G(2, [], ["p1"], lambda e, p: e.iota(T.p1[:], [[0, 2]], 0, 1))
    G(2, [], ["p8"], lambda e, p: e.iota(T.p8[:], [[0, 2]], 0, 8))
    G(4, [], ["cc"], lambda e, p: e.iota(T.cc[:], [[1, 4]], 0, 0))
    V(1, 1, ["p1"], ["bi0"], lambda e, p: e.tensor_scalar(T.bi[:, 0:1], T.p1[:, 0:1], 8, None, A.bitwise_and))
    V(1, 1, ["p1"], ["bi1"], lambda e, p: e.tensor_scalar(T.bi[:, 1:2], T.p1[:, 0:1], 3, 1, A.logical_shift_right, A.bitwise_and))
    V(1, 1, ["p8"], ["bi2"], lambda e, p: e.tensor_scalar(T.bi[:, 2:3], T.p8[:, 0:1], 127, None, A.bitwise_and))
    V(3, 1, ["bi0", "bi1", "bi2"], ["bf"], lambda e, p: e.tensor_copy(T.bf[:, 0:3], T.bi[:, 0:3]))
    S(1, 1, ["bf"], ["bf7"], lambda e, p: e.activation(T.bf[:, 3:4], T.bf[:, 0:1], ACT.Identity, bias=7.0))
    V(2, 1, ["cc", "bf7"], ["rep7"], lambda e, p: e.tensor_scalar(T.rep7[:], T.cc[:, 0:2], 16.0, T.bf[:, 3:4], A.mult, A.add))
    V(2, 1, ["cc", "bf"], ["repk"], lambda e, p: e.tensor_scalar(T.repk[:], T.cc[:, 0:2], 2.0, T.bf[:, 1:2], A.mult, A.add))
    V(2, 1, ["repk"], ["repg"], lambda e, p: e.tensor_scalar(T.repg[:], T.repk[:], float(NK), None, A.add))
    V(NK, 1, ["cc", "bf"], ["lane8"], lambda e, p: e.tensor_scalar(T.lane8[:], T.cc[:], 128.0, T.bf[:, 2:3], A.mult, A.add))
    fill("cpl", "cpl", 0, 128, 0, KW, 1, -1.0)
    V(NK, 1, ["lane8"], ["cpl"], lambda e, p: e.tensor_scalar(T.cpl[:, 7:KW:8], T.lane8[:], 7.0, None, A.add))
    for buf, rest, a, val in (("co", -1.0, 7, 7.0), ("rst", 0.0, 0, 1024.0)):
        fill(buf, buf, 0, 128, 0, KW, 1, rest)
        fill(buf, buf, 0, 128, a, KW, 8, val)
    G(KW, [], ["oko"], lambda e, p: e.iota(T.oko[:], [[0, NK], [1, 8]], 0, 0, allow_small_or_imprecise_dtypes=True))
    G(8 * LU, [], ["orow"], lambda e, p: e.iota(T.orow[:], [[1, 8], [0, LU]], 64, 0, allow_small_or_imprecise_dtypes=True), rel=20000.0)
    G(LU, [], ["loff"], lambda e, p: e.iota(T.loff[:], [[16, LU]], 0, 0, allow_small_or_imprecise_dtypes=True))
    fill("keys", [x + "0%d" % u for u in range(NU) for x in ("kh", "kk")], 0, 128, 0, NU * PW, 1, -64.0)
    G(8, ["ones"], ["g8A"], lambda e, p: e.affine_select(T.g8A[:], T.ones[0:64, 0:8], [[-8, 8]], A.is_ge, 0.0, 0, 1))
    G(8, ["g8A"], ["g8m"], lambda e, p: e.affine_select(T.g8m[:], T.g8A[:], [[8, 8]], A.is_ge, 0.0, 7, -1))
    fill("W8", "W8", 0, 64, 0, 144, 1, 0.0)
    V(8, 1, ["g8m"], ["W8"], lambda e, p: e.tensor_scalar(T.W8[:, 15:143:16], T.g8m[:], -8.0, None, A.mult))
    G(128, ["ones"], ["ident"], lambda e, p: e.affine_select(T.ident[:], T.ones[:], [[-1, 128]], A.is_equal, 0.0, 0, 1))
    for x in MUL:
        S(128, 1, ["ident"], ["mI%d" % -x], lambda e, p, x=x: e.activation(mI(x), T.ident[:], ACT.Copy, scale=float(x)))
    S(128, 1, ["ident"], ["i5"], lambda e, p: e.activation(T.i5[:], T.ident[:], ACT.Copy, scale=5.0))
    G(128, ["ones"], ["gA"], lambda e, p: e.affine_select(T.gA[:], T.ones[:], [[-16, 8], [0, 16]], A.is_ge, 0.0, 0, 1))
    G(128, ["gA"], ["gm"], lambda e, p: e.affine_select(T.gm[:], T.gA[:], [[16, 8], [0, 16]], A.is_ge, 0.0, 15, -1))
    S(128, 1, ["gm"], ["okw"], lambda e, p: e.activation(T.okw[:], T.gm[:], ACT.Copy, scale=float(OFF // 16)))
    fill("W", ["W0", "W1"], 0, 128, 0, 288, 1, 0.0)
    for i, x in enumerate((1, BIG)):
        S(8, 1, ["gm"], ["W%d" % i], lambda e, p, i=i, x=x: e.activation(T.W[:, 144 * i + 15:144 * i + 143:16], T.gm[:, 0:128:16], ACT.Copy, scale=float(x)))
    for buf, a, b, c, d, val in (("cst", 0, 32, 0, 128, 1 / 32), ("cst", 32, 64, 0, 128, BIG / 64), ("crow", 0, 32, 0, 128, 1.0), ("crow", 32, 64, 0, 64, -15.0), ("crow", 32, 64, 64, 128, -30.0)):
        fill(buf, "cst", a, b, c, d, 1, val)
    for a, b, c, d, val in ((0, 64, 0, HD, 0.0), (0, 32, 0, NK, (24 * MAG + 8 + 64) / 32), (0, 32, NK, 2 * NK, 16 * MAG / 32), (32, 64, NK, 2 * NK, 8 / 32)):
        fill("cz", "cz", a, b, c, d, 1, val)
    G(128, [], ["pm"], lambda e, p: e.iota(T.pm[:], [[-1, 128]], 2048, 1))
    V(128, 1, ["pm"], ["pm2"], lambda e, p: e.tensor_scalar(T.pm2[:], T.pm[:], 15, None, A.bitwise_and))
    V(128, 1, ["pm2"], ["same1"], lambda e, p: e.tensor_scalar(T.same[:, 0:128], T.pm2[:], 0.0, None, A.is_equal))
    V(128, 0.5, ["same1"], ["same8"], lambda e, p: e.tensor_scalar(T.same[:, 128:256], T.same[:, 0:128], 8.0, None, A.mult))

    V(256, GAT, ["vvi", "vvu", "vperm"], ["vvb"], lambda e, p: e.tensor_copy(T.vvb[:], T.vvi[:].indirect(T.vperm[:])))
    for o in range(8):
        if o < CFG["rS"]:
            S(256, 1, ["vvb", "omask"], ["R%d" % o], lambda e, p, o=o: e.activation(T.R[:, o:2048:8], T.vvb[0:64, :], ACT.Copy, scale=T.omask[:, o:o + 1]))
        else:
            V(256, 0.5, ["vvb", "omask"], ["R%d" % o], lambda e, p, o=o: e.tensor_scalar(T.R[:, o:2048:8], T.vvb[0:64, :], T.omask[:, o:o + 1], None, A.mult))
    for h in range(2):
        P(16, 64, ["W8"] + ["R%d" % o for o in range(8)], ["vP%d" % h],
          mms([(cols(0, 64), T.W8[:, 15 - b:143 - b], T.R[:, 128 * b + 64 * h:128 * b + 64 * h + 64]) for b in range(16)]), pool="vP%d" % h)
    for u in range(NU):
        V(KW, 1, ["vP%d" % (u // 2), "oko"], ["kk0%d" % u], lambda e, p, u=u: e.tensor_tensor(kv(0, u, HD, PW), p[:, KW * (u % 2):KW * (u % 2) + KW], T.oko[:], A.add),
          pool="vP%d" % (u // 2), free=2)
        V(8 * LU, 1, ["pgi%d" % u], ["win0%d" % u], lambda e, p, u=u: e.tensor_copy(wv(0, u, 0, 8 * LU), part("pgi", u, 8 * LU)))
        P(DUP, LU, ["limb", "ident"], ["lp%d" % u], lambda e, p, u=u: [e.matmul(p[:, :, j], T.ident[:], part("limb", u, LU), True, True) for j in range(DUP)][-1], fix="LP%d" % u)

    for s in range(1, NS):
        send(-s, part("XP", s, XW), part("XP", 0, XW), ["X0"] + ["prew0_%d" % u for u in range(NU)], "X%d" % s, CFG["parts"][0], 9000, rel=CFG["big"][s - 1], due=CFG["big"][s - 1] + 2000)

    def mend(s, u):
        q = "%d%d" % (s, u)
        V(NK, 1, ["pl" + q], ["lin%d" % u], lambda e, p: e.tensor_copy(part("lin", u, NK), wv(s, u, 8 * LU + 7, WW, 8)))
        V(LU, SCAT, ["lin%d" % u, "cin" + q], ["win" + q], lambda e, p: e.tensor_copy(wv(s, u, 0, 8 * LU).indirect(part("lin", u, NK)), part("cin", NU * (s - 1) + u, LU)))

    def begin(s, u):
        n, q = lambda x: "%s%d" % (x, u), "%d%d" % (s, u)
        ks, eq, ne, od, lst, keys = part("ks", u, KW), part("eq", u, KW), part("ne", u, KW), part("od", u, KW), part("lst", u, NK), kv(s, u, HD, PW)
        c16, src = part("c16", u, LU), wv(s, u, 0, 8 * LU) if s else part("pgi", u, 8 * LU)
        V(KW, 0.5, ["kk" + q, "rst"], [n("ks")], lambda e, p: e.tensor_tensor_scan(ks, T.rst[:], keys, 0.0, A.add, A.min))
        V(KW, GAT, ["kk" + q, n("ks"), "rep7"], [n("ne")], lambda e, p: e.tensor_tensor(ne, ks.indirect(T.rep7[:]), keys, A.not_equal))
        V(KW, 1, [n("ne"), "cpl"], ["pl" + q], lambda e, p: e.tensor_tensor_scan(wv(s, u, 8 * LU, WW), ne, T.cpl[:], 0.0, A.mult, A.add))
        V(NK, 1, ["pl" + q], [n("lst")], lambda e, p: e.tensor_copy(lst, wv(s, u, 8 * LU + 7, WW, 8)))
        V(LU, GAT, ["win" + q if s else n("pgi"), n("lst")], [n("c16")], lambda e, p: e.tensor_copy(c16, src.indirect(lst)))
        V(LU, GAT, ["X%d" % s if s else n("prew0_"), n("lst"), "loff"], [n("pf")],
          lambda e, p: e.tensor_tensor(part("pf", u, LU), T.XP[:, XW * s + 4096 + 8 * LU * u:XW * s + 4096 + 8 * LU * (u + 1)].indirect(lst), T.loff[:], A.add))
        V(LU, 1, [n("pf")], [n("p16")], lambda e, p: e.tensor_copy(part("p16", u, LU), part("pf", u, LU)))
        if s and CFG["cfS"]:
            S(LU, GAT, ["win" + q, n("lst")], [n("cf")], lambda e, p: e.activation(part("cf", u, LU), src.indirect(lst), ACT.Copy))
        else:
            V(LU, 1, [n("c16")], [n("cf")], lambda e, p: e.tensor_copy(part("cf", u, LU), c16))
        V(KW, GAT, ["kk" + q, n("ks"), "rep7"], [n("eq")], lambda e, p: e.tensor_tensor(eq, ks.indirect(T.rep7[:]), keys, A.is_equal))
        V(KW, 0.5, [n("ne"), "co"], [n("od")], lambda e, p: e.tensor_tensor_scan(od, ne, T.co[:], 0.0, A.mult, A.add))
        k = CFG["grp"]
        if u % k == k - 1:
            tiles = lambda z: ["%s%d%d" % (x, z, y) for x in ("win", "pl") for y in range(u + 1 - k, u + 1)]
            send(-1, wv(s + 1, u + 1 - k, 0, k * WW), wv(s, u + 1 - k, 0, k * WW), tiles(s), "win%d%d" % (s + 1, u + 1 - k), CFG["parts"][1], 3500 + 1000 * k, tiles(s + 1),
                 due=1e9 if s or u >= k else CFG["first"])

    def wide(s, st, u):
        n = lambda y, a, b: ["%s%d%d" % (y, u, q) for q in range(a, b)]
        v = lambda y, a, b: T[y][:, 16 * LU * u + 256 * a:16 * LU * u + 256 * b]
        ln = lambda a, b: slice(LU * u + 16 * a, LU * u + 16 * b)
        how = [CFG["copy"][(2 * TURN[u][ST * s + st] + h) % len(CFG["copy"])] for h in range(2)]
        for a, b in pieces(CFG["cutF"]):
            S(256 * (b - a), GAT, ["X%d" % s, "c16%d" % u], n("F", a, b), lambda e, p, a=a, b=b: e.activation(v("F", a, b), T.XP[:, XW * s:XW * s + 4096].indirect(T.c16[:, ln(a, b)]), ACT.Copy),
              due=at[0] + 256 * a * GAT * CYC)
        for a, b in pieces(CFG["cutC"]):
            if how[a // 2] == "G":
                G(256 * (b - a), n("F", a, b), n("Fc", a, b), lambda e, p, a=a, b=b: e.affine_select(v("F2", a, b), v("F", a, b), [[0, 256 * (b - a)]], A.is_ge, 0.0, 0, 0))
        for a in (0, 2):
            if how[a // 2] == "R":
                k = "B%d%d" % (u, a)
                S(512, GAT, n("F", 0, a + 2) + ["p16%d" % u], n("D", a, a + 2), lambda e, p, a=a: e.activation(v("D", a, a + 2), v("F", 0, a + 2).indirect(T.p16[:, ln(a, a + 2)]), ACT.Copy))
                P(1, 512, n("F", a, a + 2) + ["ident"], [k], mms([(cols(0, 512), mI(1), v("F", a, a + 2))], True, False), pool=k)
                P(1, 512, n("D", a, a + 2) + ["mI1"], [k], mms([(cols(0, 512), mI(-1), v("D", a, a + 2))], False, True), pool=k)
                S(512, 1, [k], n("AD", a, a + 2), lambda e, p, a=a: e.activation(T.AD[:, ln(a, a + 2), :], p[:, 0:512], ACT.Abs), pool=k, free=1)
        for a, b in pieces(CFG["cutD"]):
            if how[a // 2] == "G":
                V(256 * (b - a), GAT, n("F", 0, b) + n("Fc", a, b) + ["p16%d" % u], n("D", a, b),
                  lambda e, p, a=a, b=b: e.tensor_tensor(v("D", a, b), v("F", 0, b).indirect(T.p16[:, ln(a, b)]), v("F2", a, b), A.subtract))
        for a, b in pieces(CFG["cutA"]):
            if how[a // 2] == "G":
                S(256 * (b - a), 1, n("D", a, b), n("AD", a, b), lambda e, p, a=a, b=b: e.activation(T.AD[:, ln(a, b), :], v("D", a, b), ACT.Abs))
        for a, b in pieces(CFG["cutN"]):
            for j in range(0, 16, DUP):
                V(16 * (b - a) * DUP, 1, n("AD", a, b) + ["lp%d" % u], ["ni%d%d_%d" % (u, q, j) for q in range(a, b)],
                  lambda e, p, a=a, b=b, j=j: e.tensor_tensor(T.ni[:, ln(a, b), j:j + DUP], T.AD[:, ln(a, b), j:j + DUP], p[:, 16 * a:16 * b, :], A.is_gt), fix="LP%d" % u)

    def step(s, st, u):
        n, ln = lambda x: "%s%d" % (x, u), slice(LU * u, LU * u + LU)
        sg, sgt, kP, kN = part("sg", ST * u + st, LU), "sg%d%d" % (u, st), n("P"), n("N")
        wide(s, st, u)
        al = ["AD%d%d" % (u, q) for q in range(4)]
        red = lambda x, buf: [(cols(0, LU), sel(x, b), buf[:, ln, b]) for b in range(16)]
        base = lambda k: [(cols(0, LU), T.i5[:], T.cf[:, ln]), (cols(0, LU), T.cst[:], part("crow", k, LU))]
        m = 16 // CFG["cutS"]
        P(5, LU, al[:2] + [n("cf"), "i5", "cst"], [kP], mms(base(0), True, False), pool=kP)
        for i in range(0, 16, m):
            P(m, LU, al + ["W0"], [kP], mms(red(1, T.AD)[i:i + m], False, False), pool=kP)
        for j in range(0, 16, DUP):
            P(DUP, LU, ["ni%d%d_%d" % (u, q, j) for q in range(4)] + ["W1"], [kP], mms(red(BIG, T.ni)[j:j + DUP], False, j + DUP == 16), pool=kP)
        V(LU, 1, [kP], [sgt], lambda e, p: e.tensor_scalar(sg, p[:, 0:LU], 0.0, 2.0, A.is_lt, A.mult), pool=kP, free=2)
        V(LU, 1, [kP, n("cf")], [n("qq")], lambda e, p: e.tensor_tensor(T.qq[:, ln], p[:, 0:LU], T.cf[:, ln], A.max), pool=kP, free=2)
        P(5, LU, [n("cf"), "i5", "cst", kP], [kN], mms(base(1), True, False), pool=kN)
        P(1, LU, [sgt, "okw"], [kN], mms([(cols(0, LU), T.okw[:], sg)], False, True), pool=kN)
        V(LU, 1, [kN, n("qq")], [n("cpp")], lambda e, p: e.tensor_tensor(T.cpp[:, ln], p[:, 0:LU], T.qq[:, ln], A.max), pool=kN, free=1)
        if st < ST - 1:
            V(LU, 1, [n("cpp")], [n("ci")], lambda e, p: e.tensor_scalar(T.ci[:, ln], T.cpp[:, ln], 4095, None, A.bitwise_and))
            V(LU, 1, [n("ci")], [n("c16")], lambda e, p: e.tensor_copy(T.c16[:, ln], T.ci[:, ln]))
            V(LU, 1, [n("ci")], [n("cf")], lambda e, p: e.tensor_copy(T.cf[:, ln], T.ci[:, ln]))
        else:
            co = part("cout", NU * s + u, LU)
            V(LU, 1, [n("cpp")], ["cout%d%d" % (s, u)], lambda e, p: e.tensor_scalar(co, T.cpp[:, ln], 4095, None, A.bitwise_and))
            send(-1, part("cin", NU * s + u, LU), co, ["cout%d%d" % (s, u)], "cin%d%d" % (s + 1, u), CFG["parts"][2], CFG["send"])

    def end(s, u):
        n, q, r = lambda x: "%s%d" % (x, u), "%d%d" % (s, u), "%d%d" % (s + 1, u)
        fx, hn = lambda k: part("fx", ST * u + k, NK), lambda k: part("hn", 2 * u + k, NK)
        kL, kZ = n("L"), n("Z")
        d, g8, mc = cols(0, NK), cols(NK, 2 * NK), cols(2 * NK, 3 * NK)
        P(16, ST * NK, ["sg%d%d" % (u, k) for k in range(ST)] + ["W0"], [kL], mms([(cols(0, ST * NK), sel(1, b), part("sg", u, ST * LU, b, 16)) for b in range(16)]), pool=kL)
        P(5, NK, [kL, "kh" + q, n("ks"), n("od"), "cz", "ones", "ident", "mI1"], [kZ],
          mms([(cols(0, HD), T.ones[0:64, :], T.cz[:]), (d, mI(1), kv(s, u, NK, 2 * NK)), (cols(NK, 3 * NK), mI(1), kv(s, u, NK, 3 * NK)),
               (d, mI(-1), part("ks", u, KW, 7, 8)), (d, mI(1), part("od", u, KW, 7, 8))], True, False), pool=kZ)
        S(ST * NK, 1, [kL], [n("fx")], lambda e, p: e.activation(part("fx", u, ST * NK), p[:, 0:ST * NK], ACT.Relu, bias=-31.0), pool=kL)
        P(3, NK, [n("fx"), "same1"], [kL], mms([(cols(ST * NK, (ST + 1) * NK), T.same[:, 0:128], fx(k)) for k in range(ST)]), pool=kL)
        P(9, NK, [n("fx"), "same8", kL], [kZ], mms([(o, l, fx(k)) for k in range(ST) for o, l in ((d, T.same[:, 128:256]), (g8, T.same[:, 128:256]), (mc, mI(1)))], False, False), pool=kZ)
        S(2 * NK, 1, [kL], [n("hn")], lambda e, p: e.activation(part("hn", u, 2 * NK), p[:, (ST - 1) * NK:(ST + 1) * NK], ACT.Identity, scale=0.5, bias=MAG - 0.25), pool=kL, free=1)
        P(3, NK, [n("hn"), "mI8", "mI16"], [kZ], mms([(d, mI(-8), hn(0)), (d, mI(-16), hn(1)), (g8, mI(-16), hn(1))], False, True), pool=kZ)
        S(HD, 1, [kZ], ["kh" + r], lambda e, p: e.activation(kv(s + 1, u, 0, HD), p[:, 0:HD], ACT.Copy), pool=kZ, free=1)
        V(KW, GAT, ["kh" + r, n("eq"), "repk"], [n("tt")], lambda e, p: e.tensor_tensor(part("tt", u, KW), kv(s + 1, u, 0, HD).indirect(T.repk[:]), part("eq", u, KW), A.mult))
        V(KW, 2, ["kk" + q, n("tt")], ["kk" + r], lambda e, p: e.tensor_tensor(kv(s + 1, u, HD, PW), kv(s, u, HD, PW), part("tt", u, KW), A.add))

    def final(u):
        n, q = lambda x: "%s%d" % (x, u), "%d%d" % (NS, u)
        mend(NS, u)
        add("Q", 60, ["win" + q], [], lambda e, p: e.dma_start(T.yg[:, 8 * LU * u:8 * LU * (u + 1)], wv(NS, u, 0, 8 * LU)), sem="outs", inc=16, lat=2500)
        V(KW, GAT, ["kh" + q, "kk" + q, "repg"], [n("fv")], lambda e, p: e.tensor_tensor(part("fv", u, KW), kv(NS, u, 0, HD).indirect(T.repg[:]), kv(NS, u, HD, PW), A.subtract))
        for c in range(2):
            k, y = "Y%d%d" % (u, c), part("yvs", 2 * u + c, 256)
            P(1, 256, ["kh" + q, "cst", "orow"], [k], lambda e, p, c=c: e.matmul(p[0:8, 0:256], T.cst[0:32, 0:8], part("orow", c, 256), True, False), pool=k)
            P(8, 64, [n("fv"), "ident"], [k], lambda e, p, c=c: [e.matmul(p[0:8, 16 * j + b:256:LU], T.ident[:, b:128:16], part("fv", 8 * u + 2 * j + c, 4), False, b == 15 and j == NK - 1)
                                                               for b in range(16) for j in range(NK)][-1], pool=k)
            if c:
                V(256, 1, [k], ["yv%d%d" % (u, c)], lambda e, p, y=y: e.tensor_scalar(y, p[0:8, 0:256], 0.125, None, A.mult), pool=k, free=1)
            else:
                S(256, 1, [k], ["yv%d%d" % (u, c)], lambda e, p, y=y: e.activation(y, p[0:8, 0:256], ACT.Copy, scale=0.125), pool=k, free=1)
        add("Q", 60, ["yv%d%d" % (u, c) for c in range(2)], [], lambda e, p: e.dma_start(T.yv[:, LU * u:LU * u + LU], part("yvs", u, 8 * LU)), sem="outs", inc=16, lat=2000)
        P(4, 64, ["kh" + q, "ident"], [n("M")], lambda e, p: [e.matmul(p[0:8, b:LU:16], T.ident[:, b:128:16], kv(NS, u, 2 * NK, 3 * NK), True, True) for b in range(16)][-1], pool=n("M"))
        S(LU, 1, [n("M")], [n("ym")], lambda e, p: e.activation(part("yms", u, LU), p[0:8, 0:LU], ACT.Identity, bias=64.0), pool=n("M"), free=1)

    for s in range(NS):
        for u in range(NU):
            if s:
                mend(s, u)
            begin(s, u)
            for st in range(ST):
                at[0], at[2] = CFG["t0"] + CFG["slot"] * (TURN[u][ST * s + st] + CFG["shift"][ST * u + st]), st
                step(s, st, u)
            end(s, u)
    for u in range(NU):
        at[1] = END - CFG["early"] * (len(CFG["seq"]) - 1 - TURN[u][-1])
        final(u)
    at[1] = END
    add("Q", 60, ["ym%d" % u for u in range(NU)], [], lambda e, p: e.dma_start(T.ym[:], T.yms[:]), sem="outs", inc=16, lat=2000)
    return ops


def deps_of(ops, order):
    last, readers, out = {}, {}, {}
    for i in order:
        o, d = ops[i], set()
        for r in o["rd"]:
            if r in last:
                d.add(last[r])
        for w in o["wr"]:
            if w in last:
                d.add(last[w])
            d.update(readers.get(w, ()))
        d.discard(i)
        out[i] = d
        for r in o["rd"]:
            readers.setdefault(r, []).append(i)
        for w in o["wr"]:
            last[w] = i
            readers[w] = []
    return out


def plan(ops):
    n, wake = len(ops), CFG["wake"]
    dep = deps_of(ops, range(n))
    succ = [[] for _ in range(n)]
    need = [len(dep[i]) for i in range(n)]
    for i in range(n):
        for d in dep[i]:
            succ[d].append(i)
    span = [o["cost"] + o["lat"] + wake for o in ops]
    late, soon = [0.0] * n, [0.0] * n
    for i in reversed(range(n)):
        late[i] = min(ops[i]["due"], min([late[x] for x in succ[i]] + [ops[i]["end"]]) - span[i])
    for i in range(n):
        soon[i] = ops[i]["due"] if ops[i]["due"] < 1e8 else max([soon[d] + span[d] for d in dep[i]] + [0.0])
    pr = [late[i] if late[i] < CFG["t0"] else late[i] + CFG["mix"] * min(0.0, max(soon[i] - late[i], -CFG["cap"])) for i in range(n)]
    kind = [(o["wr"] + [""])[0].rstrip("0123456789_") for o in ops]
    pr = [pr[i] + CFG["bias"].get(kind[i], 0.0) + CFG["bias"].get("%s@%d" % (kind[i], ops[i]["st"]), 0.0) for i in range(n)]
    done, start, buf = [0.0] * n, [0.0] * n, {}
    free = {e: 0.0 for e in "VSPGQW"}
    slot, held, fin = [0.0] * len(BANKS), {}, {}
    ready = [i for i in range(n) if not need[i]]
    can, order = [o["rel"] for o in ops], []
    while ready:
        best = {}
        for i in ready:
            o = ops[i]
            t = max(can[i], free[o["eng"]] if o["eng"] != "W" else 0.0)
            if o["pool"] and o["pool"] not in held:
                fr = [x for x in slot if x is not None]
                if not fr:
                    continue
                t = max(t, min(fr))
            best.setdefault(o["eng"], []).append((t, i))
        cand = None
        for e, lst in best.items():
            t0 = min(lst)[0]
            pick = min((pr[i], t, i) for t, i in lst if t <= t0)
            d = ops[pick[2]]["cost"]
            near = min((pr[i], t, i) for t, i in lst if t <= t0 + d)
            if near[0] < pick[0] - CFG["gap"] and CFG["idle"].get(e):
                fit = [(pr[i], t, i) for t, i in lst if t + ops[i]["cost"] <= near[1] + CFG["tol"] and i != near[2]]
                if fit:
                    pick = min(fit)
                elif near[1] - t0 <= CFG["idle"][e] * (t0 + d - near[1]):
                    pick = near
            if cand is None or pick[1] < cand[0]:
                cand = (pick[1], pick[2])
        t, i = cand
        o = ops[i]
        ready.remove(i)
        k = o["pool"]
        if k:
            if k not in held:
                held[k] = min((x, y) for y, x in enumerate(slot) if x is not None)[1]
                slot[held[k]] = None
            buf[i] = BANKS[held[k]]
        if o["fix"]:
            buf[i] = o["fix"]
        start[i] = t
        done[i] = t + o["cost"] + o["lat"]
        free[o["eng"]] = t + o["cost"]
        if k and o["free"]:
            fin[k] = fin.get(k, []) + [done[i] + wake]
            if len(fin[k]) == o["free"]:
                slot[held.pop(k)] = max(fin.pop(k))
        order.append(i)
        for x in succ[i]:
            need[x] -= 1
            can[x] = max(can[x], done[i] + (0.0 if ops[x]["eng"] == "W" or o["eng"] == ops[x]["eng"] == "P" else wake))
            if not need[x]:
                ready.append(x)
    assert len(order) == n
    order.sort(key=lambda i: start[i])
    return order, buf, start, done


def emit(g, T, ops, order, buf):
    eng = {"V": g.vector, "S": g.scalar, "P": g.tensor, "Q": g.sync, "G": g}
    cnt = {"V": "cV", "S": "cS", "P": "cP", "G": "cG"}
    dep = deps_of(ops, order)
    total, at, after, bank = {}, {}, {}, {}
    clock = {e: {} for e in eng}
    for i in order:
        o = ops[i]
        d = set(dep[i])
        b = buf.get(i)
        if b:
            use = bank.setdefault(b, {})
            d.update(v for x, v in use.items() if x != o["eng"])
            use[o["eng"]] = i
        if o["eng"] == "W":
            at[i] = (o["sem"], o["inc"])
            after[i] = {o["sem"]: o["inc"]}
            continue
        e, c = eng[o["eng"]], clock[o["eng"]]
        for k in sorted(d, reverse=True, key=lambda k: (at[k][1], k)):
            if o["eng"] == "P" and ops[k]["eng"] == "P":
                continue
            s, v = at[k]
            if c.get(s, 0) >= v:
                continue
            e.wait_ge(T.sem[s], v)
            for s2, v2 in after[k].items():
                c[s2] = max(c.get(s2, 0), v2)
        r = o["fn"](e, T[b] if b else None)
        s = o["sem"] or cnt[o["eng"]]
        if s != "sent":
            r.then_inc(T.sem[s], o["inc"] or 1)
        total[s] = total.get(s, 0) + (o["inc"] or 1)
        at[i] = (s, total[s])
        after[i] = dict(c)
        after[i][s] = total[s]
    for s in ("cV", "cS", "cP", "cG", "outs", "sent"):
        g.wait_ge(T.sem[s], total[s])


def rank_program(g, core, T, topo):
    rank = T.rank_of(core)
    if rank is None:
        return
    cores = T.cores

    def engines(d, part):
        e = topo.engines(core, cores[(rank + d) % len(cores)])
        return (e, e[:len(e) // 2], e[len(e) // 2:])[part]

    def send(d, out, inp, sem, part):
        rid, pid = topo.addr(cores[(rank + d) % len(cores)])[:2]
        return g.remote_dma(out, inp, T.sem[sem], T.sem["sent"], pid, rid, sum(1 << e for e in engines(d, part)))

    ops = graph({"T": T, "send": send, "engines": lambda part: len(engines(-1, part))})
    order, buf, start, done = plan(ops)
    emit(g, T, ops, order, buf)
